import numpy as np
import ml_dtypes


def mxq(x, axis, fmt="e4m3"):
    dtype, down = {"e4m3": (ml_dtypes.float8_e4m3fn, 7), "e5m2": (ml_dtypes.float8_e5m2, 14)}[fmt]
    v = np.moveaxis(np.asarray(x, np.float32).astype(ml_dtypes.bfloat16).astype(np.float64), axis, -1)
    blocks = v.reshape(v.shape[:-1] + (-1, 32))
    amax = np.abs(blocks).max(-1, keepdims=True)
    byte = np.maximum(np.where(amax > 0, np.frexp(amax)[1] - 1 + 127, 0) - down, 1)
    scale = np.exp2(byte - 127.0)
    codes = (blocks / scale).astype(np.float32).astype(dtype).astype(np.float64)
    return np.moveaxis((codes * scale).reshape(v.shape), -1, axis)


WIDE = False


def mx_kscale(k):
    if not WIDE:
        return np.ones(k)
    levels = np.array([10, -10, 5, -5, 0])
    if k % 512:
        return np.exp2(np.random.permutation(np.resize(levels, k // 32))).repeat(32)
    a = np.empty((k // 512, 16))
    for p in range(k // 512):
        a[p, :8] = np.random.permutation(np.resize(levels, 8))
        for g in range(8):
            far = levels[np.abs(levels - a[p, g]) >= 10]
            a[p, g + 8] = far[np.random.randint(len(far))]
    return np.exp2(a.ravel()).repeat(32)


def f64(x):
    return np.asarray(x).astype(np.float64)


def striped(idx):
    return np.tile(idx.reshape(-1, 16).T, (8, 1)).astype(np.uint16)


def unstriped(offs):
    return offs[:16].T.reshape(-1).astype(np.int64)


E2M1 = np.array([0.0, 0.5, 1.0, 1.5, 2.0, 3.0, 4.0, 6.0, -0.0, -0.5, -1.0, -1.5, -2.0, -3.0, -4.0, -6.0])


def pack_weight(w, fmt):
    k, n = w.shape
    w = f64(np.asarray(w, np.float32).astype(ml_dtypes.bfloat16)).reshape(k // 32, 32, n)
    amax = np.abs(w).max(1)
    if fmt == "e4m3":
        byte = np.frexp(amax)[1] - 1 + 127 - 7
    else:
        mant, ex = np.frexp(amax / 6.0)
        byte = np.where(mant > 0.5, ex, ex - 1) + 127
    byte = np.clip(np.where(amax > 0, byte, 1), 1, 254)
    scaled = (w * np.exp2(127.0 - byte)[:, None, :]).reshape(k, n).astype(np.float32)
    by_word = np.ascontiguousarray(scaled.reshape(k // 512, 128, 4, n).transpose(0, 1, 3, 2))
    if fmt == "e4m3":
        words = by_word.astype(ml_dtypes.float8_e4m3fn).view(np.uint8)
    else:
        c = by_word.astype(ml_dtypes.float4_e2m1fn).view(np.uint8) & 0xF
        words = (c[..., 0::2] | (c[..., 1::2] << 4)).reshape(k // 512, 128, 2 * n)
    return np.ascontiguousarray(words), np.ascontiguousarray(byte.astype(np.uint8).reshape(k // 512, 16, n))


def unpack_weight(words, scales, fmt):
    g, _, n = scales.shape
    words = np.ascontiguousarray(words).reshape(g, 128, n, -1)
    if fmt == "e4m3":
        vals = words.view(ml_dtypes.float8_e4m3fn).astype(np.float64)
    else:
        nib = np.empty((g, 128, n, 4), np.uint8)
        nib[..., 0::2] = words & 0xF
        nib[..., 1::2] = words >> 4
        vals = E2M1[nib]
    vals = vals * np.repeat(np.exp2(scales.astype(np.float64) - 127.0), 8, axis=1)[..., None]
    return vals.transpose(0, 1, 3, 2).reshape(g * 512, n)


def gelu(v):
    return 0.5 * v * (1.0 + np.tanh(np.sqrt(2.0 / np.pi) * (v + 0.044715 * v**3)))


K, H, N, T, S, T2, P = 1024, 1024, 512, 4096, 1024, 2048, 1024

def setup_inputs():
    n = np.random.standard_normal
    s = mx_kscale(K)[:, None]
    u = mx_kscale(H)[:, None]
    tab_words, tab_scales = pack_weight(n((K, T)) * s, "e4m3")
    w1_words, w1_scales = pack_weight(n((K, H)) / np.sqrt(K) / s, "e2m1")
    return {
        "tab_words": tab_words, "tab_scales": tab_scales,
        "offs": striped(np.random.permutation(T)[:S]),
        "w1_words": w1_words, "w1_scales": w1_scales,
        "b1": (0.5 * n(H)).astype(np.float32),
        "gain": (np.random.uniform(0.7, 1.8, H) * u[:, 0]).astype(np.float32),
        "offs2": striped(np.random.permutation(T2)[:S]),
        "wgs": np.exp(0.3 * n((128, S))).astype(np.float32),
        "board": (0.7 * n((H, T2)) * u).astype(np.float32),
        "w2": (n((H, N)) / np.sqrt(H) / u).astype(np.float32),
        "offs3": striped(np.random.permutation(T2)[:P]),
        "style": (0.7 * n((N, P))).astype(np.float32),
        "offs4": striped(np.random.permutation(T2)[:P]),
        "wgo": np.exp(0.3 * n((128, P))).astype(np.float32),
    }

def reference(tab_words, tab_scales, offs, w1_words, w1_scales, b1, gain, offs2, wgs,
              board, w2, offs3, style, offs4, wgo):
    v = unpack_weight(tab_words, tab_scales, "e4m3")[:, unstriped(offs)]
    w1 = unpack_weight(w1_words, w1_scales, "e2m1")
    h = np.tanh((w1.T @ v) + f64(b1)[:, None]) * f64(gain)[:, None]
    page = np.zeros((H, T2))
    page[:, unstriped(offs2)] = np.tile(f64(wgs), (H // 128, 1)) * h
    z = page + f64(board)
    y = mxq(f64(w2), 0, "e4m3").T @ mxq(z, 0, "e4m3")
    x = y[:, unstriped(offs3)] - f64(style)
    out = np.zeros((N, T2))
    out[:, unstriped(offs4)] = np.tile(f64(wgo), (N // 128, 1)) * x
    return out

@@ -1,0 +1,264 @@
+from contextlib import ExitStack
+
+import concourse.mybir as mybir
+from concourse.masks import make_identity
+
+K, H, N, T, S, T2, M = 1024, 1024, 512, 4096, 1024, 2048, 1024
+FLOPS = 2 * K * H * S + 2 * H * N * T2
+
+F32 = mybir.dt.float32
+BF16 = mybir.dt.bfloat16
+I32 = mybir.dt.int32
+U32 = mybir.dt.uint32
+U16 = mybir.dt.uint16
+U8 = mybir.dt.uint8
+FP8X4 = mybir.dt.float8_e4m3fn_x4
+FP4X4 = mybir.dt.float4_e2m1fn_x4
+MULT = mybir.AluOpType.mult
+SUBTRACT = mybir.AluOpType.subtract
+TANH = mybir.ActivationFunctionType.Tanh
+COPY = mybir.ActivationFunctionType.Copy
+
+P = 128
+BANK = 512
+PASSES = 2
+ROW_TILES = H // P
+TILES_PER_PASS = ROW_TILES // PASSES
+CHUNKS = T2 // BANK
+BLOCKS = BANK // P
+OUT_TILES = N // P
+RING = 3
+AHEAD = 3
+KB = 1024
+
+
+def tile_list_proof_board_kernel(tc, tab_words, tab_scales, offs, w1_words, w1_scales, b1, gain, offs2, wgs,
+                                           board, w2, offs3, style, offs4, wgo, out):
+    nc = tc.nc
+    with ExitStack() as ctx:
+        lists = ctx.enter_context(tc.tile_pool(name="lists", bufs=1))
+        keep = ctx.enter_context(tc.tile_pool(name="keep", bufs=1))
+        shared = ctx.enter_context(tc.tile_pool(name="shared", bufs=1))
+        psum = ctx.enter_context(tc.psum_pool(name="psum", bufs=1))
+
+        def kept(name, shape, dtype):
+            return keep.tile(shape, dtype, name=name, align_bytes=64)
+
+        def placed(name, shape, dtype, kb):
+            return shared.tile(shape, dtype, name=name, align_bytes=64, offset=kb * KB)
+
+        idx = lists.tile([P, S // 16], U16, name="idx")
+        idx2 = lists.tile([P, S // 16], U16, name="idx2")
+        idx3 = lists.tile([P, M // 16], U16, name="idx3")
+        idx4 = lists.tile([P, M // 16], U16, name="idx4")
+
+        sum_banks = [psum.tile([P, BLOCKS, P], F32, name="sum_bank%d" % g) for g in range(CHUNKS)]
+        back_banks = [psum.tile([P, BLOCKS, P], F32, name="back_bank%d" % b) for b in range(2)]
+        mx_banks = [psum.tile([P, BANK], F32, name="mx_bank%d" % b) for b in range(2)]
+
+        table = [placed("table0", [P, T], U32, 0), placed("table1", [P, T], U32, 40)]
+        table_scales = placed("table_scales", [P, PASSES, T], U8, 16)
+        warm_in = placed("warm_in", [P, 32], F32, 52)
+        warm_out = shared.tile([P, 32], F32, name="warm_out", align_bytes=64, offset=28 * KB - 64)
+        picked = [placed("picked%d" % a, [P, S], U32, 107 + 4 * a) for a in range(PASSES)]
+        h_at = (71, 83, 95, 99, 103, 95, 99, 103)
+        h_sb = [placed("h%d" % i, [P, S], F32, h_at[i]) for i in range(ROW_TILES)]
+
+        identity = kept("identity", [P, P], F32)
+        vector_rows = kept("vector_rows", [P, P], F32)
+        vector_cols = kept("vector_cols", [P, 2 * ROW_TILES], F32)
+        picked_scales = kept("picked_scales", [P, PASSES, S], U8)
+        w1_planes = kept("w1_planes", [P, PASSES, H], U8)
+        turned = [kept("turned%d" % g, [P, 2, BLOCKS, 2 * P], BF16) for g in range(CHUNKS)]
+        z_grouped = [[placed("z_grouped0_%d" % g, [P, BANK, 4], BF16, 4 * g) for g in range(CHUNKS)],
+                     [kept("z_grouped1_%d" % g, [P, BANK, 4], BF16) for g in range(CHUNKS)]]
+        z_codes = [[kept("z_codes%d_%d" % (a, g), [P, BANK], U32) for g in range(CHUNKS)] for a in range(PASSES)]
+        w2_grouped = [kept("w2_grouped%d" % a, [P, N, 4], BF16) for a in range(PASSES)]
+        w2_codes = kept("w2_codes", [P, PASSES, N], U32)
+        pages = [kept("page%d" % s, [P, T2], F32) for s in range(RING - 1)]
+        pulled = [kept("pulled%d" % s, [P, M], F32) for s in range(2)]
+
+        nc.vector.memset(table_scales[:].rearrange("p a t -> p (a t)").bitcast(I32), 0)
+        nc.vector.memset(vector_rows[:], 0.0)
+        nc.vector.memset(warm_in[:], 0.0)
+        nc.vector.memset(w1_planes[:].rearrange("p a c -> p (a c)").bitcast(I32), 0)
+        make_identity(nc, identity[:])
+        for page in pages:
+            nc.vector.memset(page[:], 0.0)
+
+        def load_table(a):
+            nc.sync.dma_start(table[a][:].bitcast(I32), tab_words[a].rearrange("p t i -> p (t i)").bitcast(I32))
+
+        nc.sync.dma_start(idx[:], offs)
+        nc.sync.dma_start(idx2[:], offs2)
+        nc.sync.dma_start(idx3[:], offs3)
+        nc.sync.dma_start(idx4[:], offs4)
+        load_table(0)
+        for q in range(4):
+            nc.scalar.dma_start(table_scales[32 * q:32 * q + 4, :, :].bitcast(I32),
+                                tab_scales[:, 4 * q:4 * q + 4, :].rearrange("a r t -> r a t").bitcast(I32))
+        nc.scalar.dma_start(vector_rows[0:ROW_TILES, :], b1.rearrange("(i p) -> i p", p=P))
+        nc.scalar.activation(warm_out[:], warm_in[:], TANH)
+        load_table(1)
+        w1_codes = placed("w1_codes", [P, PASSES, 2 * H], U8, 24)
+        nc.sync.dma_start(w1_codes[:].bitcast(I32), w1_words.rearrange("a p c -> p a c").bitcast(I32))
+        wgs_sb = placed("wgs_sb", [P, S], F32, 28)
+        nc.sync.dma_start(wgs_sb[:], wgs)
+        nc.scalar.dma_start(vector_rows[ROW_TILES:2 * ROW_TILES, :], gain.rearrange("(i p) -> i p", p=P))
+        for q in range(4):
+            nc.scalar.dma_start(w1_planes[32 * q:32 * q + 4, :, :].bitcast(I32),
+                                w1_scales[:, 4 * q:4 * q + 4, :].rearrange("a r c -> r a c").bitcast(I32))
+
+        nc.tensor.transpose(back_banks[0][:, 0, 0:P], vector_rows[:], identity[:])
+        nc.scalar.copy(vector_cols[:], back_banks[0][:, 0, 0:2 * ROW_TILES])
+
+        nc.vector.tensor_copy(picked[0][:], table[0][:].indirect(idx[:]))
+        for half in range(2):
+            cols = slice(BANK * half, BANK * (half + 1))
+            entries = idx[:, 32 * half:32 * (half + 1)]
+            for a in range(PASSES):
+                nc.vector.tensor_copy(picked_scales[:, a, cols], table_scales[:, a, :].indirect(entries))
+            nc.vector.tensor_copy(picked[1][:, cols], table[1][:].indirect(entries))
+
+        board_at = (33, 55, 64)
+        board_sb = [placed("board%d" % s, [P, T2], F32, board_at[s]) for s in range(RING)]
+        w2_at = (74, 86)
+        w2_raw = [placed("w2_raw%d" % a, [P, 4, N], F32, w2_at[a]) for a in range(PASSES)]
+        pages = pages + [placed("page_last", [P, T2], F32, 42)]
+        nc.gpsimd.memset(pages[RING - 1][:], 0.0)
+
+        def load_board(i):
+            nc.sync.dma_start(board_sb[i % RING][:], board[P * i:P * (i + 1), :])
+
+        def load_w2(a):
+            nc.sync.dma_start(w2_raw[a][:], w2[512 * a:512 * (a + 1), :].rearrange("(p j) n -> p j n", j=4))
+
+        for i in range(RING - 1):
+            load_board(i)
+
+        def first_product(i, half):
+            cols = slice(BANK * half, BANK * (half + 1))
+            for a in range(PASSES):
+                nc.tensor.matmul_mx(
+                    out=mx_banks[half][:],
+                    lhsT=w1_codes[:, a, 2 * P * i:2 * P * (i + 1)].bitcast(FP4X4),
+                    lhsT_scale=w1_planes[:, a, P * i:P * (i + 1)],
+                    rhs=picked[a][:, cols].bitcast(FP8X4),
+                    rhs_scale=picked_scales[:, a, cols],
+                    start=(a == 0), stop=(a == PASSES - 1))
+            nc.scalar.activation(h_sb[i][:, cols], mx_banks[half][:], TANH, bias=vector_cols[:, i:i + 1])
+
+        def scores(i):
+            for half in range(2):
+                first_product(i, half)
+            h = h_sb[i]
+            nc.scalar.activation(h[:], h[:], COPY, scale=vector_cols[:, ROW_TILES + i:ROW_TILES + i + 1])
+
+        def turn_board(i):
+            for g in range(CHUNKS):
+                for c in range(BLOCKS):
+                    t0 = BANK * g + P * c
+                    nc.tensor.matmul(sum_banks[g][:, c, :], board_sb[i % RING][:, t0:t0 + P], identity[:],
+                                     start=(c == 0), stop=False, is_transpose=True)
+
+        def turn_page(i):
+            place = i % TILES_PER_PASS
+            for g in range(CHUNKS):
+                for c in range(BLOCKS):
+                    t0 = BANK * g + P * c
+                    nc.tensor.matmul(sum_banks[g][:, c, :], pages[i % RING][:, t0:t0 + P], identity[:],
+                                     start=False, stop=(c == BLOCKS - 1), is_transpose=True)
+                nc.scalar.copy(
+                    turned[g][:, :, :, 64 * place:64 * (place + 1)].rearrange("t u c (w e) -> t u c w e", e=2),
+                    sum_banks[g][:].rearrange("t c (w u e) -> t u c w e", u=2, e=2))
+
+        def turn_back(g, grouped, banks, second_copy):
+            words = turned[g][:].bitcast(F32)
+            grouped_words = grouped[:].bitcast(F32)
+            for b in range(2):
+                for u in range(2):
+                    for c in range(2):
+                        nc.tensor.transpose(banks[b][:, 2 * u + c, :], words[:, u, 2 * b + c, :], identity[:])
+                copy = second_copy if b == 1 else nc.scalar.copy
+                copy(grouped_words[:, 2 * P * b:2 * P * (b + 1), :], banks[b][:].rearrange("p (u c) t -> p (c t) u", u=2))
+
+        for half in range(2):
+            cols = slice(BANK * half, BANK * (half + 1))
+            first_product(0, half)
+            nc.vector.tensor_scalar(h_sb[0][:, cols], h_sb[0][:, cols], vector_cols[:, ROW_TILES:ROW_TILES + 1], None, MULT)
+            nc.vector.tensor_tensor(pages[0][:].indirect(idx2[:, 32 * half:32 * (half + 1)]), h_sb[0][:, cols],
+                                    wgs_sb[:, cols], MULT)
+        load_board(RING - 1)
+        for i in range(1, AHEAD):
+            scores(i)
+
+        for i in range(ROW_TILES):
+            turn_board(i)
+            if i + RING < ROW_TILES:
+                load_board(i + RING)
+            if i > 0:
+                nc.vector.tensor_tensor(pages[i % RING][:].indirect(idx2[:]), h_sb[i][:], wgs_sb[:], MULT)
+            if i < PASSES:
+                load_w2(i)
+            if i + AHEAD < ROW_TILES:
+                scores(i + AHEAD)
+            turn_page(i)
+            if i in (1, 2):
+                a = i - 1
+                nc.scalar.copy(w2_grouped[a][:].rearrange("p (c k) j -> p c j k", k=4),
+                               w2_raw[a][:].rearrange("p j (c k) -> p c j k", k=4))
+            if i == TILES_PER_PASS - 1:
+                for g in range(CHUNKS):
+                    turn_back(g, z_grouped[0][g], back_banks, nc.scalar.copy)
+
+        z_planes = [placed("z_planes0", [P, T2], U8, 103), kept("z_planes1", [P, T2], U8)]
+        w2_planes = placed("w2_planes", [P, PASSES, N], U8, 105)
+        y_sb = [placed("y%d" % j, [P, T2], F32, board_at[j]) for j in range(RING)] + [placed("y_last", [P, T2], F32, 16)]
+        style_sb = [placed("style%d" % j, [P, M], F32, w2_at[j // 2] + 4 * (j % 2)) for j in range(OUT_TILES)]
+        wgo_sb = placed("wgo_sb", [P, M], F32, 24)
+        released = [placed("released0", [P, T2], F32, 107), placed("released1", [P, T2], F32, 95)]
+        for j in range(OUT_TILES):
+            nc.sync.dma_start(style_sb[j][:], style[P * j:P * (j + 1), :])
+        nc.sync.dma_start(wgo_sb[:], wgo)
+        for window in released:
+            nc.gpsimd.memset(window[:], 0.0)
+
+        def quantize_z(a, g):
+            nc.vector.quantize_mx(out=z_codes[a][g][:].bitcast(FP8X4), scales=z_planes[a][:, BANK * g:BANK * (g + 1)],
+                                  in_=z_grouped[a][g][:].rearrange("p t j -> p (t j)"))
+
+        def second_product(j, g, copy):
+            cols = slice(BANK * g, BANK * (g + 1))
+            bank = mx_banks[g % 2]
+            for a in range(PASSES):
+                nc.tensor.matmul_mx(
+                    out=bank[:],
+                    lhsT=w2_codes[:, a, P * j:P * (j + 1)].bitcast(FP8X4),
+                    lhsT_scale=w2_planes[:, a, P * j:P * (j + 1)],
+                    rhs=z_codes[a][g][:].bitcast(FP8X4),
+                    rhs_scale=z_planes[a][:, cols],
+                    start=(a == 0), stop=(a == PASSES - 1))
+            copy(y_sb[j][:, cols], bank[:])
+
+        for a in range(PASSES):
+            nc.vector.quantize_mx(out=w2_codes[:, a, :].bitcast(FP8X4), scales=w2_planes[:, a, :],
+                                  in_=w2_grouped[a][:].rearrange("p n j -> p (n j)"))
+        free_banks = back_banks + sum_banks + back_banks
+        for g in range(CHUNKS):
+            late = g >= CHUNKS - 2
+            quantize_z(0, g)
+            turn_back(g, z_grouped[1][g], free_banks[2 * g:2 * g + 2], nc.vector.tensor_copy if late else nc.scalar.copy)
+            quantize_z(1, g)
+            second_product(0, g, nc.vector.tensor_copy if g == CHUNKS - 1 else nc.scalar.copy)
+
+        def pull(j):
+            nc.vector.tensor_tensor(pulled[j % 2][:], y_sb[j][:].indirect(idx3[:]), style_sb[j][:], SUBTRACT)
+
+        pull(0)
+        for j in range(OUT_TILES):
+            if j + 1 < OUT_TILES:
+                for g in range(CHUNKS):
+                    second_product(j + 1, g, nc.scalar.copy)
+                pull(j + 1)
+            nc.vector.tensor_tensor(released[j % 2][:].indirect(idx4[:]), pulled[j % 2][:], wgo_sb[:], MULT)
+            nc.sync.dma_start(out[P * j:P * (j + 1), :], released[j % 2][:])

@@ -54,18 +54,20 @@ def tile_list_proof_board_kernel(tc, tab_words, tab_scales, offs, w1_words, w1_s
 
         sum_banks = [psum.tile([P, BLOCKS, P], F32, name="sum_bank%d" % g) for g in range(CHUNKS)]
         back_banks = [psum.tile([P, BLOCKS, P], F32, name="back_bank%d" % b) for b in range(2)]
-        mx_banks = [psum.tile([P, BANK], F32, name="mx_bank%d" % b) for b in range(2)]
+        mx_banks = [psum.tile([P, BLOCKS, P], F32, name="mx_bank%d" % b) for b in range(2)]
+
+        def whole(bank):
+            return bank[:].rearrange("p c t -> p (c t)")
 
         table = [placed("table0", [P, T], U32, 0), placed("table1", [P, T], U32, 40)]
         table_scales = placed("table_scales", [P, PASSES, T], U8, 16)
-        warm_in = placed("warm_in", [P, 32], F32, 52)
-        warm_out = shared.tile([P, 32], F32, name="warm_out", align_bytes=64, offset=28 * KB - 64)
+        zeros = placed("zeros", [P, P], F32, 52)
+        vector_rows = shared.tile([P, P], F32, name="vector_rows", align_bytes=64, offset=28 * KB - 256)
         picked = [placed("picked%d" % a, [P, S], U32, 107 + 4 * a) for a in range(PASSES)]
         h_at = (71, 83, 95, 99, 103, 95, 99, 103)
         h_sb = [placed("h%d" % i, [P, S], F32, h_at[i]) for i in range(ROW_TILES)]
 
         identity = kept("identity", [P, P], F32)
-        vector_rows = kept("vector_rows", [P, P], F32)
         vector_cols = kept("vector_cols", [P, 2 * ROW_TILES], F32)
         picked_scales = kept("picked_scales", [P, PASSES, S], U8)
         w1_planes = kept("w1_planes", [P, PASSES, H], U8)
@@ -75,16 +77,16 @@ def tile_list_proof_board_kernel(tc, tab_words, tab_scales, offs, w1_words, w1_s
         z_codes = [[kept("z_codes%d_%d" % (a, g), [P, BANK], U32) for g in range(CHUNKS)] for a in range(PASSES)]
         w2_grouped = [kept("w2_grouped%d" % a, [P, N, 4], BF16) for a in range(PASSES)]
         w2_codes = kept("w2_codes", [P, PASSES, N], U32)
-        pages = [kept("page%d" % s, [P, T2], F32) for s in range(RING - 1)]
+        pages = [kept("page%d" % s, [P, T2], F32) for s in range(RING)]
+        released = [kept("released0", [P, T2], F32)]
         pulled = [kept("pulled%d" % s, [P, M], F32) for s in range(2)]
 
         nc.vector.memset(table_scales[:].rearrange("p a t -> p (a t)").bitcast(I32), 0)
-        nc.vector.memset(vector_rows[:], 0.0)
-        nc.vector.memset(warm_in[:], 0.0)
+        nc.vector.memset(zeros[:], 0.0)
         nc.vector.memset(w1_planes[:].rearrange("p a c -> p (a c)").bitcast(I32), 0)
         make_identity(nc, identity[:])
-        for page in pages:
-            nc.vector.memset(page[:], 0.0)
+        for window in pages + released:
+            nc.vector.memset(window[:].bitcast(I32), 0)
 
         def load_table(a):
             nc.sync.dma_start(table[a][:].bitcast(I32), tab_words[a].rearrange("p t i -> p (t i)").bitcast(I32))
@@ -97,20 +99,19 @@ def tile_list_proof_board_kernel(tc, tab_words, tab_scales, offs, w1_words, w1_s
         for q in range(4):
             nc.scalar.dma_start(table_scales[32 * q:32 * q + 4, :, :].bitcast(I32),
                                 tab_scales[:, 4 * q:4 * q + 4, :].rearrange("a r t -> r a t").bitcast(I32))
-        nc.scalar.dma_start(vector_rows[0:ROW_TILES, :], b1.rearrange("(i p) -> i p", p=P))
-        nc.scalar.activation(warm_out[:], warm_in[:], TANH)
+        nc.scalar.activation(vector_rows[:], zeros[:], TANH)
         load_table(1)
-        w1_codes = placed("w1_codes", [P, PASSES, 2 * H], U8, 24)
-        nc.sync.dma_start(w1_codes[:].bitcast(I32), w1_words.rearrange("a p c -> p a c").bitcast(I32))
-        wgs_sb = placed("wgs_sb", [P, S], F32, 28)
-        nc.sync.dma_start(wgs_sb[:], wgs)
+        nc.scalar.dma_start(vector_rows[0:ROW_TILES, :], b1.rearrange("(i p) -> i p", p=P))
         nc.scalar.dma_start(vector_rows[ROW_TILES:2 * ROW_TILES, :], gain.rearrange("(i p) -> i p", p=P))
         for q in range(4):
             nc.scalar.dma_start(w1_planes[32 * q:32 * q + 4, :, :].bitcast(I32),
                                 w1_scales[:, 4 * q:4 * q + 4, :].rearrange("a r c -> r a c").bitcast(I32))
-
-        nc.tensor.transpose(back_banks[0][:, 0, 0:P], vector_rows[:], identity[:])
+        nc.tensor.transpose(back_banks[0][:, 0, :], vector_rows[:], identity[:])
         nc.scalar.copy(vector_cols[:], back_banks[0][:, 0, 0:2 * ROW_TILES])
+        w1_codes = placed("w1_codes", [P, PASSES, 2 * H], U8, 24)
+        nc.sync.dma_start(w1_codes[:].bitcast(I32), w1_words.rearrange("a p c -> p a c").bitcast(I32))
+        wgs_sb = placed("wgs_sb", [P, S], F32, 28)
+        nc.sync.dma_start(wgs_sb[:], wgs)
 
         nc.vector.tensor_copy(picked[0][:], table[0][:].indirect(idx[:]))
         for half in range(2):
@@ -124,8 +125,8 @@ def tile_list_proof_board_kernel(tc, tab_words, tab_scales, offs, w1_words, w1_s
         board_sb = [placed("board%d" % s, [P, T2], F32, board_at[s]) for s in range(RING)]
         w2_at = (74, 86)
         w2_raw = [placed("w2_raw%d" % a, [P, 4, N], F32, w2_at[a]) for a in range(PASSES)]
-        pages = pages + [placed("page_last", [P, T2], F32, 42)]
-        nc.gpsimd.memset(pages[RING - 1][:], 0.0)
+        released = released + [placed("released1", [P, T2], F32, 42)]
+        nc.vector.memset(released[1][:].bitcast(I32), 0)
 
         def load_board(i):
             nc.sync.dma_start(board_sb[i % RING][:], board[P * i:P * (i + 1), :])
@@ -140,13 +141,13 @@ def tile_list_proof_board_kernel(tc, tab_words, tab_scales, offs, w1_words, w1_s
             cols = slice(BANK * half, BANK * (half + 1))
             for a in range(PASSES):
                 nc.tensor.matmul_mx(
-                    out=mx_banks[half][:],
+                    out=whole(mx_banks[half]),
                     lhsT=w1_codes[:, a, 2 * P * i:2 * P * (i + 1)].bitcast(FP4X4),
                     lhsT_scale=w1_planes[:, a, P * i:P * (i + 1)],
                     rhs=picked[a][:, cols].bitcast(FP8X4),
                     rhs_scale=picked_scales[:, a, cols],
                     start=(a == 0), stop=(a == PASSES - 1))
-            nc.scalar.activation(h_sb[i][:, cols], mx_banks[half][:], TANH, bias=vector_cols[:, i:i + 1])
+            nc.scalar.activation(h_sb[i][:, cols], whole(mx_banks[half]), TANH, bias=vector_cols[:, i:i + 1])
 
         def scores(i):
             for half in range(2):
@@ -156,6 +157,12 @@ def tile_list_proof_board_kernel(tc, tab_words, tab_scales, offs, w1_words, w1_s
 
         def turn_board(i):
             for g in range(CHUNKS):
+                if i == ROW_TILES - 1:
+                    nc.tensor.matmul_mx(
+                        out=whole(sum_banks[g]),
+                        lhsT=w1_codes[:, 0, 0:2 * P].bitcast(FP4X4), lhsT_scale=w1_planes[:, 0, 0:P],
+                        rhs=picked[0][:, 0:BANK].bitcast(FP8X4), rhs_scale=picked_scales[:, 0, 0:BANK],
+                        start=True, stop=True)
                 for c in range(BLOCKS):
                     t0 = BANK * g + P * c
                     nc.tensor.matmul(sum_banks[g][:, c, :], board_sb[i % RING][:, t0:t0 + P], identity[:],
@@ -163,10 +170,14 @@ def tile_list_proof_board_kernel(tc, tab_words, tab_scales, offs, w1_words, w1_s
 
         def turn_page(i):
             place = i % TILES_PER_PASS
+            page_identity = identity
+            if i == ROW_TILES - 1:
+                page_identity = placed("last_identity", [P, P], F32, board_at[i % RING] + 4)
+                nc.scalar.copy(page_identity[:], identity[:])
             for g in range(CHUNKS):
                 for c in range(BLOCKS):
                     t0 = BANK * g + P * c
-                    nc.tensor.matmul(sum_banks[g][:, c, :], pages[i % RING][:, t0:t0 + P], identity[:],
+                    nc.tensor.matmul(sum_banks[g][:, c, :], pages[i % RING][:, t0:t0 + P], page_identity[:],
                                      start=False, stop=(c == BLOCKS - 1), is_transpose=True)
                 nc.scalar.copy(
                     turned[g][:, :, :, 64 * place:64 * (place + 1)].rearrange("t u c (w e) -> t u c w e", e=2),
@@ -216,49 +227,63 @@ def tile_list_proof_board_kernel(tc, tab_words, tab_scales, offs, w1_words, w1_s
         y_sb = [placed("y%d" % j, [P, T2], F32, board_at[j]) for j in range(RING)] + [placed("y_last", [P, T2], F32, 16)]
         style_sb = [placed("style%d" % j, [P, M], F32, w2_at[j // 2] + 4 * (j % 2)) for j in range(OUT_TILES)]
         wgo_sb = placed("wgo_sb", [P, M], F32, 24)
-        released = [placed("released0", [P, T2], F32, 107), placed("released1", [P, T2], F32, 95)]
         for j in range(OUT_TILES):
             nc.sync.dma_start(style_sb[j][:], style[P * j:P * (j + 1), :])
         nc.sync.dma_start(wgo_sb[:], wgo)
-        for window in released:
-            nc.gpsimd.memset(window[:], 0.0)
 
         def quantize_z(a, g):
             nc.vector.quantize_mx(out=z_codes[a][g][:].bitcast(FP8X4), scales=z_planes[a][:, BANK * g:BANK * (g + 1)],
                                   in_=z_grouped[a][g][:].rearrange("p t j -> p (t j)"))
 
-        def second_product(j, g, copy):
-            cols = slice(BANK * g, BANK * (g + 1))
-            bank = mx_banks[g % 2]
-            for a in range(PASSES):
-                nc.tensor.matmul_mx(
-                    out=bank[:],
-                    lhsT=w2_codes[:, a, P * j:P * (j + 1)].bitcast(FP8X4),
-                    lhsT_scale=w2_planes[:, a, P * j:P * (j + 1)],
-                    rhs=z_codes[a][g][:].bitcast(FP8X4),
-                    rhs_scale=z_planes[a][:, cols],
-                    start=(a == 0), stop=(a == PASSES - 1))
-            copy(y_sb[j][:, cols], bank[:])
+        y_banks = [whole(bank) for bank in sum_banks]
 
-        for a in range(PASSES):
-            nc.vector.quantize_mx(out=w2_codes[:, a, :].bitcast(FP8X4), scales=w2_planes[:, a, :],
-                                  in_=w2_grouped[a][:].rearrange("p n j -> p (n j)"))
-        free_banks = back_banks + sum_banks + back_banks
-        for g in range(CHUNKS):
-            late = g >= CHUNKS - 2
-            quantize_z(0, g)
-            turn_back(g, z_grouped[1][g], free_banks[2 * g:2 * g + 2], nc.vector.tensor_copy if late else nc.scalar.copy)
-            quantize_z(1, g)
-            second_product(0, g, nc.vector.tensor_copy if g == CHUNKS - 1 else nc.scalar.copy)
+        def second_pass(j, g, a):
+            nc.tensor.matmul_mx(
+                out=y_banks[g],
+                lhsT=w2_codes[:, a, P * j:P * (j + 1)].bitcast(FP8X4),
+                lhsT_scale=w2_planes[:, a, P * j:P * (j + 1)],
+                rhs=z_codes[a][g][:].bitcast(FP8X4),
+                rhs_scale=z_planes[a][:, BANK * g:BANK * (g + 1)],
+                start=(a == 0), stop=(a == PASSES - 1))
+
+        def empty_bank(j, g, copy):
+            copy(y_sb[j][:, BANK * g:BANK * (g + 1)], y_banks[g])
 
         def pull(j):
             nc.vector.tensor_tensor(pulled[j % 2][:], y_sb[j][:].indirect(idx3[:]), style_sb[j][:], SUBTRACT)
 
-        pull(0)
-        for j in range(OUT_TILES):
-            if j + 1 < OUT_TILES:
-                for g in range(CHUNKS):
-                    second_product(j + 1, g, nc.scalar.copy)
-                pull(j + 1)
+        for a in range(PASSES):
+            nc.vector.quantize_mx(out=w2_codes[:, a, :].bitcast(FP8X4), scales=w2_planes[:, a, :],
+                                  in_=w2_grouped[a][:].rearrange("p n j -> p (n j)"))
+        for g in range(CHUNKS):
+            quantize_z(0, g)
+        bank_pairs = (back_banks, mx_banks)
+        for g in range(CHUNKS):
+            outer = g in (0, CHUNKS - 1)
+            turn_back(g, z_grouped[1][g], bank_pairs[g % 2], nc.vector.tensor_copy if outer else nc.scalar.copy)
+            if g % 2 == 1:
+                second_pass(0, g - 1, 0)
+                second_pass(0, g, 0)
+            if g > 0:
+                quantize_z(1, g - 1)
+        quantize_z(1, CHUNKS - 1)
+        for g in range(CHUNKS):
+            second_pass(0, g, 1)
+        for g in range(CHUNKS):
+            empty_bank(0, g, nc.vector.tensor_copy if g == CHUNKS - 1 else nc.scalar.copy)
+
+        def release(j):
             nc.vector.tensor_tensor(released[j % 2][:].indirect(idx4[:]), pulled[j % 2][:], wgo_sb[:], MULT)
             nc.sync.dma_start(out[P * j:P * (j + 1), :], released[j % 2][:])
+
+        pull(0)
+        release(0)
+        for j in range(1, OUT_TILES):
+            for g in range(CHUNKS):
+                for a in range(PASSES):
+                    second_pass(j, g, a)
+                empty_bank(j, g, nc.scalar.copy)
+            pull(j)
+            if j > 1:
+                release(j - 1)
+        release(OUT_TILES - 1)

@@ -113,13 +113,13 @@ def tile_list_proof_board_kernel(tc, tab_words, tab_scales, offs, w1_words, w1_s
         wgs_sb = placed("wgs_sb", [P, S], F32, 28)
         nc.sync.dma_start(wgs_sb[:], wgs)
 
-        nc.vector.tensor_copy(picked[0][:], table[0][:].indirect(idx[:]))
         for half in range(2):
             cols = slice(BANK * half, BANK * (half + 1))
             entries = idx[:, 32 * half:32 * (half + 1)]
             for a in range(PASSES):
                 nc.vector.tensor_copy(picked_scales[:, a, cols], table_scales[:, a, :].indirect(entries))
-            nc.vector.tensor_copy(picked[1][:, cols], table[1][:].indirect(entries))
+            for a in range(PASSES):
+                nc.vector.tensor_copy(picked[a][:, cols], table[a][:].indirect(entries))
 
         board_at = (33, 55, 64)
         board_sb = [placed("board%d" % s, [P, T2], F32, board_at[s]) for s in range(RING)]
@@ -157,12 +157,6 @@ def tile_list_proof_board_kernel(tc, tab_words, tab_scales, offs, w1_words, w1_s
 
         def turn_board(i):
             for g in range(CHUNKS):
-                if i == ROW_TILES - 1:
-                    nc.tensor.matmul_mx(
-                        out=whole(sum_banks[g]),
-                        lhsT=w1_codes[:, 0, 0:2 * P].bitcast(FP4X4), lhsT_scale=w1_planes[:, 0, 0:P],
-                        rhs=picked[0][:, 0:BANK].bitcast(FP8X4), rhs_scale=picked_scales[:, 0, 0:BANK],
-                        start=True, stop=True)
                 for c in range(BLOCKS):
                     t0 = BANK * g + P * c
                     nc.tensor.matmul(sum_banks[g][:, c, :], board_sb[i % RING][:, t0:t0 + P], identity[:],

@@ -63,7 +63,7 @@ def tile_list_proof_board_kernel(tc, tab_words, tab_scales, offs, w1_words, w1_s
         table_scales = placed("table_scales", [P, PASSES, T], U8, 16)
         zeros = placed("zeros", [P, P], F32, 52)
         vector_rows = shared.tile([P, P], F32, name="vector_rows", align_bytes=64, offset=28 * KB - 256)
-        picked = [placed("picked%d" % a, [P, S], U32, 107 + 4 * a) for a in range(PASSES)]
+        picked = [placed("picked%d" % a, [P, S], U32, 108 + 8 * a) for a in range(PASSES)]
         h_at = (71, 83, 95, 99, 103, 95, 99, 103)
         h_sb = [placed("h%d" % i, [P, S], F32, h_at[i]) for i in range(ROW_TILES)]
 
@@ -77,15 +77,14 @@ def tile_list_proof_board_kernel(tc, tab_words, tab_scales, offs, w1_words, w1_s
         z_codes = [[kept("z_codes%d_%d" % (a, g), [P, BANK], U32) for g in range(CHUNKS)] for a in range(PASSES)]
         w2_grouped = [kept("w2_grouped%d" % a, [P, N, 4], BF16) for a in range(PASSES)]
         w2_codes = kept("w2_codes", [P, PASSES, N], U32)
-        pages = [kept("page%d" % s, [P, T2], F32) for s in range(RING)]
-        released = [kept("released0", [P, T2], F32)]
+        pages = [kept("page%d" % s, [P, T2], F32) for s in range(RING - 1)]
         pulled = [kept("pulled%d" % s, [P, M], F32) for s in range(2)]
 
         nc.vector.memset(table_scales[:].rearrange("p a t -> p (a t)").bitcast(I32), 0)
         nc.vector.memset(zeros[:], 0.0)
         nc.vector.memset(w1_planes[:].rearrange("p a c -> p (a c)").bitcast(I32), 0)
         make_identity(nc, identity[:])
-        for window in pages + released:
+        for window in pages:
             nc.vector.memset(window[:].bitcast(I32), 0)
 
         def load_table(a):
@@ -113,20 +112,19 @@ def tile_list_proof_board_kernel(tc, tab_words, tab_scales, offs, w1_words, w1_s
         wgs_sb = placed("wgs_sb", [P, S], F32, 28)
         nc.sync.dma_start(wgs_sb[:], wgs)
 
+        for a in range(PASSES):
+            nc.vector.tensor_copy(picked_scales[:, a, :], table_scales[:, a, :].indirect(idx[:]))
+        nc.vector.tensor_copy(picked[0][:], table[0][:].indirect(idx[:]))
         for half in range(2):
-            cols = slice(BANK * half, BANK * (half + 1))
-            entries = idx[:, 32 * half:32 * (half + 1)]
-            for a in range(PASSES):
-                nc.vector.tensor_copy(picked_scales[:, a, cols], table_scales[:, a, :].indirect(entries))
-            for a in range(PASSES):
-                nc.vector.tensor_copy(picked[a][:, cols], table[a][:].indirect(entries))
+            nc.vector.tensor_copy(picked[1][:, BANK * half:BANK * (half + 1)],
+                                  table[1][:].indirect(idx[:, 32 * half:32 * (half + 1)]))
 
         board_at = (33, 55, 64)
         board_sb = [placed("board%d" % s, [P, T2], F32, board_at[s]) for s in range(RING)]
         w2_at = (74, 86)
         w2_raw = [placed("w2_raw%d" % a, [P, 4, N], F32, w2_at[a]) for a in range(PASSES)]
-        released = released + [placed("released1", [P, T2], F32, 42)]
-        nc.vector.memset(released[1][:].bitcast(I32), 0)
+        pages = pages + [placed("page_last", [P, T2], F32, 42)]
+        nc.gpsimd.memset(pages[RING - 1][:].bitcast(I32), 0)
 
         def load_board(i):
             nc.sync.dma_start(board_sb[i % RING][:], board[P * i:P * (i + 1), :])
@@ -137,23 +135,27 @@ def tile_list_proof_board_kernel(tc, tab_words, tab_scales, offs, w1_words, w1_s
         for i in range(RING - 1):
             load_board(i)
 
-        def first_product(i, half):
-            cols = slice(BANK * half, BANK * (half + 1))
-            for a in range(PASSES):
-                nc.tensor.matmul_mx(
-                    out=whole(mx_banks[half]),
-                    lhsT=w1_codes[:, a, 2 * P * i:2 * P * (i + 1)].bitcast(FP4X4),
-                    lhsT_scale=w1_planes[:, a, P * i:P * (i + 1)],
-                    rhs=picked[a][:, cols].bitcast(FP8X4),
-                    rhs_scale=picked_scales[:, a, cols],
-                    start=(a == 0), stop=(a == PASSES - 1))
-            nc.scalar.activation(h_sb[i][:, cols], whole(mx_banks[half]), TANH, bias=vector_cols[:, i:i + 1])
+        def first_product(i, bank, c0, width, group):
+            for g0 in range(0, width, group):
+                cols = slice(c0 + g0, c0 + g0 + group)
+                for a in range(PASSES):
+                    nc.tensor.matmul_mx(
+                        out=whole(bank)[:, g0:g0 + group],
+                        lhsT=w1_codes[:, a, 2 * P * i:2 * P * (i + 1)].bitcast(FP4X4),
+                        lhsT_scale=w1_planes[:, a, P * i:P * (i + 1)],
+                        rhs=picked[a][:, cols].bitcast(FP8X4),
+                        rhs_scale=picked_scales[:, a, cols],
+                        start=(a == 0), stop=(a == PASSES - 1))
+            nc.scalar.activation(h_sb[i][:, c0:c0 + width], whole(bank)[:, 0:width], TANH, bias=vector_cols[:, i:i + 1])
+
+        def apply_gain(i, c0, width):
+            h = h_sb[i][:, c0:c0 + width]
+            nc.scalar.activation(h, h, COPY, scale=vector_cols[:, ROW_TILES + i:ROW_TILES + i + 1])
 
         def scores(i):
             for half in range(2):
-                first_product(i, half)
-            h = h_sb[i]
-            nc.scalar.activation(h[:], h[:], COPY, scale=vector_cols[:, ROW_TILES + i:ROW_TILES + i + 1])
+                first_product(i, mx_banks[half], BANK * half, BANK, BANK)
+            apply_gain(i, 0, S)
 
         def turn_board(i):
             for g in range(CHUNKS):
@@ -187,12 +189,11 @@ def tile_list_proof_board_kernel(tc, tab_words, tab_scales, offs, w1_words, w1_s
                 copy = second_copy if b == 1 else nc.scalar.copy
                 copy(grouped_words[:, 2 * P * b:2 * P * (b + 1), :], banks[b][:].rearrange("p (u c) t -> p (c t) u", u=2))
 
-        for half in range(2):
-            cols = slice(BANK * half, BANK * (half + 1))
-            first_product(0, half)
-            nc.vector.tensor_scalar(h_sb[0][:, cols], h_sb[0][:, cols], vector_cols[:, ROW_TILES:ROW_TILES + 1], None, MULT)
-            nc.vector.tensor_tensor(pages[0][:].indirect(idx2[:, 32 * half:32 * (half + 1)]), h_sb[0][:, cols],
-                                    wgs_sb[:, cols], MULT)
+        for bank, c0, width, group in ((mx_banks[0], 0, 256, P), (back_banks[1], 256, 256, P), (mx_banks[1], BANK, BANK, BANK)):
+            first_product(0, bank, c0, width, group)
+            apply_gain(0, c0, width)
+            nc.vector.tensor_tensor(pages[0][:].indirect(idx2[:, c0 // 16:(c0 + width) // 16]), h_sb[0][:, c0:c0 + width],
+                                    wgs_sb[:, c0:c0 + width], MULT)
         load_board(RING - 1)
         for i in range(1, AHEAD):
             scores(i)
@@ -216,6 +217,9 @@ def tile_list_proof_board_kernel(tc, tab_words, tab_scales, offs, w1_words, w1_s
                 for g in range(CHUNKS):
                     turn_back(g, z_grouped[0][g], back_banks, nc.scalar.copy)
 
+        released = [placed("released%d" % s, [P, T2], F32, 108 + 8 * s) for s in range(2)]
+        for window in released:
+            nc.gpsimd.memset(window[:].bitcast(I32), 0)
         z_planes = [placed("z_planes0", [P, T2], U8, 103), kept("z_planes1", [P, T2], U8)]
         w2_planes = placed("w2_planes", [P, PASSES, N], U8, 105)
         y_sb = [placed("y%d" % j, [P, T2], F32, board_at[j]) for j in range(RING)] + [placed("y_last", [P, T2], F32, 16)]

@@ -23,12 +23,12 @@ P = 128
 BANK = 512
 PASSES = 2
 ROW_TILES = H // P
+LAST = ROW_TILES - 1
 TILES_PER_PASS = ROW_TILES // PASSES
 CHUNKS = T2 // BANK
 BLOCKS = BANK // P
 OUT_TILES = N // P
-RING = 3
-AHEAD = 3
+PAGES = 3
 KB = 1024
 
 
@@ -45,7 +45,7 @@ def tile_list_proof_board_kernel(tc, tab_words, tab_scales, offs, w1_words, w1_s
             return keep.tile(shape, dtype, name=name, align_bytes=64)
 
         def placed(name, shape, dtype, kb):
-            return shared.tile(shape, dtype, name=name, align_bytes=64, offset=kb * KB)
+            return shared.tile(shape, dtype, name=name, align_bytes=64, offset=int(kb * KB))
 
         idx = lists.tile([P, S // 16], U16, name="idx")
         idx2 = lists.tile([P, S // 16], U16, name="idx2")
@@ -59,32 +59,41 @@ def tile_list_proof_board_kernel(tc, tab_words, tab_scales, offs, w1_words, w1_s
         def whole(bank):
             return bank[:].rearrange("p c t -> p (c t)")
 
-        table = [placed("table0", [P, T], U32, 0), placed("table1", [P, T], U32, 40)]
+        slot_at = (0, 8, 24, 32)
+        w2_at = (44, 52)
+        factor_at = 116
+        vector_rows = placed("vector_rows", [P, P], F32, 39.75)
+        table = [placed("table0", [P, T], U32, 0), placed("table1", [P, T], U32, 24)]
         table_scales = placed("table_scales", [P, PASSES, T], U8, 16)
-        zeros = placed("zeros", [P, P], F32, 52)
-        vector_rows = shared.tile([P, P], F32, name="vector_rows", align_bytes=64, offset=28 * KB - 256)
-        picked = [placed("picked%d" % a, [P, S], U32, 108 + 8 * a) for a in range(PASSES)]
-        h_at = (71, 83, 95, 99, 103, 95, 99, 103)
-        h_sb = [placed("h%d" % i, [P, S], F32, h_at[i]) for i in range(ROW_TILES)]
+        w1_codes = placed("w1_codes", [P, PASSES, 2 * H], U8, 40)
+        picked = [placed("picked%d" % a, [P, S], U32, 108 + 4 * a) for a in range(PASSES)]
+        factors = [placed("factor%d" % i, [P, S], F32, factor_at + 4 * i) for i in range(ROW_TILES)]
+        h_sb = [placed("h%d" % i, [P, S], F32, w2_at[i] if i < 2 else slot_at[(i - 2) % 4]) for i in range(ROW_TILES)]
+        board_sb = [placed("board%d" % i, [P, T2], F32, slot_at[i % 4]) for i in range(ROW_TILES)]
+        page_identity = [placed("page_identity%d" % i, [P, P], F32, slot_at[i % 4] + 4) for i in range(ROW_TILES)]
+        w2_raw = [placed("w2_raw%d" % a, [P, 4, N], F32, w2_at[a]) for a in range(PASSES)]
+        turned = [[placed("turned%d_%d" % (a, g), [P, 2, BLOCKS, 2 * P], BF16, 60 + 16 * a + 4 * g) for g in range(CHUNKS)]
+                  for a in range(PASSES)]
+        z_grouped = [[placed("z_grouped%d_%d" % (a, g), [P, BANK, 4], BF16, (92, factor_at + 8)[a] + 4 * g)
+                      for g in range(CHUNKS)] for a in range(PASSES)]
 
+        zeros = kept("zeros", [P, P], F32)
         identity = kept("identity", [P, P], F32)
         vector_cols = kept("vector_cols", [P, 2 * ROW_TILES], F32)
+        wgs_sb = kept("wgs_sb", [P, S], F32)
         picked_scales = kept("picked_scales", [P, PASSES, S], U8)
         w1_planes = kept("w1_planes", [P, PASSES, H], U8)
-        turned = [kept("turned%d" % g, [P, 2, BLOCKS, 2 * P], BF16) for g in range(CHUNKS)]
-        z_grouped = [[placed("z_grouped0_%d" % g, [P, BANK, 4], BF16, 4 * g) for g in range(CHUNKS)],
-                     [kept("z_grouped1_%d" % g, [P, BANK, 4], BF16) for g in range(CHUNKS)]]
         z_codes = [[kept("z_codes%d_%d" % (a, g), [P, BANK], U32) for g in range(CHUNKS)] for a in range(PASSES)]
         w2_grouped = [kept("w2_grouped%d" % a, [P, N, 4], BF16) for a in range(PASSES)]
         w2_codes = kept("w2_codes", [P, PASSES, N], U32)
-        pages = [kept("page%d" % s, [P, T2], F32) for s in range(RING - 1)]
-        pulled = [kept("pulled%d" % s, [P, M], F32) for s in range(2)]
+        pages = [kept("page%d" % s, [P, T2], F32) for s in range(PAGES)]
+        released_first = kept("released0", [P, T2], F32)
 
-        nc.vector.memset(table_scales[:].rearrange("p a t -> p (a t)").bitcast(I32), 0)
         nc.vector.memset(zeros[:], 0.0)
+        nc.vector.memset(table_scales[:].rearrange("p a t -> p (a t)").bitcast(I32), 0)
         nc.vector.memset(w1_planes[:].rearrange("p a c -> p (a c)").bitcast(I32), 0)
         make_identity(nc, identity[:])
-        for window in pages:
+        for window in pages + [released_first]:
             nc.vector.memset(window[:].bitcast(I32), 0)
 
         def load_table(a):
@@ -94,23 +103,21 @@ def tile_list_proof_board_kernel(tc, tab_words, tab_scales, offs, w1_words, w1_s
         nc.sync.dma_start(idx2[:], offs2)
         nc.sync.dma_start(idx3[:], offs3)
         nc.sync.dma_start(idx4[:], offs4)
+        nc.sync.dma_start(wgs_sb[:], wgs)
         load_table(0)
-        for q in range(4):
-            nc.scalar.dma_start(table_scales[32 * q:32 * q + 4, :, :].bitcast(I32),
-                                tab_scales[:, 4 * q:4 * q + 4, :].rearrange("a r t -> r a t").bitcast(I32))
         nc.scalar.activation(vector_rows[:], zeros[:], TANH)
-        load_table(1)
         nc.scalar.dma_start(vector_rows[0:ROW_TILES, :], b1.rearrange("(i p) -> i p", p=P))
         nc.scalar.dma_start(vector_rows[ROW_TILES:2 * ROW_TILES, :], gain.rearrange("(i p) -> i p", p=P))
         for q in range(4):
+            nc.scalar.dma_start(table_scales[32 * q:32 * q + 4, :, :].bitcast(I32),
+                                tab_scales[:, 4 * q:4 * q + 4, :].rearrange("a r t -> r a t").bitcast(I32))
+        nc.tensor.transpose(back_banks[0][:, 0, :], vector_rows[:], identity[:])
+        load_table(1)
+        nc.sync.dma_start(w1_codes[:].bitcast(I32), w1_words.rearrange("a p c -> p a c").bitcast(I32))
+        for q in range(4):
             nc.scalar.dma_start(w1_planes[32 * q:32 * q + 4, :, :].bitcast(I32),
                                 w1_scales[:, 4 * q:4 * q + 4, :].rearrange("a r c -> r a c").bitcast(I32))
-        nc.tensor.transpose(back_banks[0][:, 0, :], vector_rows[:], identity[:])
         nc.scalar.copy(vector_cols[:], back_banks[0][:, 0, 0:2 * ROW_TILES])
-        w1_codes = placed("w1_codes", [P, PASSES, 2 * H], U8, 24)
-        nc.sync.dma_start(w1_codes[:].bitcast(I32), w1_words.rearrange("a p c -> p a c").bitcast(I32))
-        wgs_sb = placed("wgs_sb", [P, S], F32, 28)
-        nc.sync.dma_start(wgs_sb[:], wgs)
 
         for a in range(PASSES):
             nc.vector.tensor_copy(picked_scales[:, a, :], table_scales[:, a, :].indirect(idx[:]))
@@ -119,21 +126,14 @@ def tile_list_proof_board_kernel(tc, tab_words, tab_scales, offs, w1_words, w1_s
             nc.vector.tensor_copy(picked[1][:, BANK * half:BANK * (half + 1)],
                                   table[1][:].indirect(idx[:, 32 * half:32 * (half + 1)]))
 
-        board_at = (33, 55, 64)
-        board_sb = [placed("board%d" % s, [P, T2], F32, board_at[s]) for s in range(RING)]
-        w2_at = (74, 86)
-        w2_raw = [placed("w2_raw%d" % a, [P, 4, N], F32, w2_at[a]) for a in range(PASSES)]
-        pages = pages + [placed("page_last", [P, T2], F32, 42)]
-        nc.gpsimd.memset(pages[RING - 1][:].bitcast(I32), 0)
-
         def load_board(i):
-            nc.sync.dma_start(board_sb[i % RING][:], board[P * i:P * (i + 1), :])
+            nc.sync.dma_start(board_sb[i][:], board[P * i:P * (i + 1), :])
 
         def load_w2(a):
             nc.sync.dma_start(w2_raw[a][:], w2[512 * a:512 * (a + 1), :].rearrange("(p j) n -> p j n", j=4))
 
-        for i in range(RING - 1):
-            load_board(i)
+        def make_factor(i):
+            nc.scalar.activation(factors[i][:], wgs_sb[:], COPY, scale=vector_cols[:, ROW_TILES + i:ROW_TILES + i + 1])
 
         def first_product(i, bank, c0, width, group):
             for g0 in range(0, width, group):
@@ -146,42 +146,44 @@ def tile_list_proof_board_kernel(tc, tab_words, tab_scales, offs, w1_words, w1_s
                         rhs=picked[a][:, cols].bitcast(FP8X4),
                         rhs_scale=picked_scales[:, a, cols],
                         start=(a == 0), stop=(a == PASSES - 1))
+
+        def apply_tanh(i, bank, c0, width):
             nc.scalar.activation(h_sb[i][:, c0:c0 + width], whole(bank)[:, 0:width], TANH, bias=vector_cols[:, i:i + 1])
 
-        def apply_gain(i, c0, width):
-            h = h_sb[i][:, c0:c0 + width]
-            nc.scalar.activation(h, h, COPY, scale=vector_cols[:, ROW_TILES + i:ROW_TILES + i + 1])
-
-        def scores(i):
+        def multiply(i):
             for half in range(2):
                 first_product(i, mx_banks[half], BANK * half, BANK, BANK)
-            apply_gain(i, 0, S)
+
+        def score(i):
+            for half in range(2):
+                apply_tanh(i, mx_banks[half], BANK * half, BANK)
+
+        def place_scores(i, c0, width):
+            nc.vector.tensor_tensor(pages[i % PAGES][:].indirect(idx2[:, c0 // 16:(c0 + width) // 16]),
+                                    h_sb[i][:, c0:c0 + width], factors[i][:, c0:c0 + width], MULT)
 
         def turn_board(i):
             for g in range(CHUNKS):
                 for c in range(BLOCKS):
                     t0 = BANK * g + P * c
-                    nc.tensor.matmul(sum_banks[g][:, c, :], board_sb[i % RING][:, t0:t0 + P], identity[:],
+                    nc.tensor.matmul(sum_banks[g][:, c, :], board_sb[i][:, t0:t0 + P], identity[:],
                                      start=(c == 0), stop=False, is_transpose=True)
+            nc.scalar.copy(page_identity[i][:], identity[:])
 
         def turn_page(i):
-            place = i % TILES_PER_PASS
-            page_identity = identity
-            if i == ROW_TILES - 1:
-                page_identity = placed("last_identity", [P, P], F32, board_at[i % RING] + 4)
-                nc.scalar.copy(page_identity[:], identity[:])
+            a, place = divmod(i, TILES_PER_PASS)
             for g in range(CHUNKS):
                 for c in range(BLOCKS):
                     t0 = BANK * g + P * c
-                    nc.tensor.matmul(sum_banks[g][:, c, :], pages[i % RING][:, t0:t0 + P], page_identity[:],
+                    nc.tensor.matmul(sum_banks[g][:, c, :], pages[i % PAGES][:, t0:t0 + P], page_identity[i][:],
                                      start=False, stop=(c == BLOCKS - 1), is_transpose=True)
                 nc.scalar.copy(
-                    turned[g][:, :, :, 64 * place:64 * (place + 1)].rearrange("t u c (w e) -> t u c w e", e=2),
+                    turned[a][g][:, :, :, 64 * place:64 * (place + 1)].rearrange("t u c (w e) -> t u c w e", e=2),
                     sum_banks[g][:].rearrange("t c (w u e) -> t u c w e", u=2, e=2))
 
-        def turn_back(g, grouped, banks, second_copy):
-            words = turned[g][:].bitcast(F32)
-            grouped_words = grouped[:].bitcast(F32)
+        def turn_back(a, g, banks, second_copy):
+            words = turned[a][g][:].bitcast(F32)
+            grouped_words = z_grouped[a][g][:].bitcast(F32)
             for b in range(2):
                 for u in range(2):
                     for c in range(2):
@@ -189,42 +191,50 @@ def tile_list_proof_board_kernel(tc, tab_words, tab_scales, offs, w1_words, w1_s
                 copy = second_copy if b == 1 else nc.scalar.copy
                 copy(grouped_words[:, 2 * P * b:2 * P * (b + 1), :], banks[b][:].rearrange("p (u c) t -> p (c t) u", u=2))
 
+        def group_w2(a, half):
+            cols = slice(N // 2 * half, N // 2 * (half + 1))
+            nc.scalar.copy(w2_grouped[a][:, cols, :].rearrange("p (c k) j -> p c j k", k=4),
+                           w2_raw[a][:, :, cols].rearrange("p j (c k) -> p c j k", k=4))
+
+        for i in range(4):
+            load_board(i)
+        make_factor(0)
         for bank, c0, width, group in ((mx_banks[0], 0, 256, P), (back_banks[1], 256, 256, P), (mx_banks[1], BANK, BANK, BANK)):
             first_product(0, bank, c0, width, group)
-            apply_gain(0, c0, width)
-            nc.vector.tensor_tensor(pages[0][:].indirect(idx2[:, c0 // 16:(c0 + width) // 16]), h_sb[0][:, c0:c0 + width],
-                                    wgs_sb[:, c0:c0 + width], MULT)
-        load_board(RING - 1)
-        for i in range(1, AHEAD):
-            scores(i)
+            apply_tanh(0, bank, c0, width)
+            place_scores(0, c0, width)
+        multiply(1)
+        score(1)
+        multiply(2)
 
         for i in range(ROW_TILES):
             turn_board(i)
-            if i + RING < ROW_TILES:
-                load_board(i + RING)
+            if i + 2 < ROW_TILES:
+                score(i + 2)
             if i > 0:
-                nc.vector.tensor_tensor(pages[i % RING][:].indirect(idx2[:]), h_sb[i][:], wgs_sb[:], MULT)
+                place_scores(i, 0, S)
+            if i < LAST:
+                make_factor(i + 1)
             if i < PASSES:
                 load_w2(i)
-            if i + AHEAD < ROW_TILES:
-                scores(i + AHEAD)
             turn_page(i)
-            if i in (1, 2):
-                a = i - 1
-                nc.scalar.copy(w2_grouped[a][:].rearrange("p (c k) j -> p c j k", k=4),
-                               w2_raw[a][:].rearrange("p j (c k) -> p c j k", k=4))
-            if i == TILES_PER_PASS - 1:
-                for g in range(CHUNKS):
-                    turn_back(g, z_grouped[0][g], back_banks, nc.scalar.copy)
+            if 2 <= i < ROW_TILES - 2:
+                load_board(i + 2)
+            if i + 3 < ROW_TILES:
+                multiply(i + 3)
+            if 1 <= i <= 4:
+                group_w2(*divmod(i - 1, 2))
+            if TILES_PER_PASS <= i < TILES_PER_PASS + 2:
+                for g in range(2 * (i - TILES_PER_PASS), 2 * (i - TILES_PER_PASS + 1)):
+                    turn_back(0, g, back_banks, nc.scalar.copy)
 
-        released = [placed("released%d" % s, [P, T2], F32, 108 + 8 * s) for s in range(2)]
-        for window in released:
-            nc.gpsimd.memset(window[:].bitcast(I32), 0)
-        z_planes = [placed("z_planes0", [P, T2], U8, 103), kept("z_planes1", [P, T2], U8)]
-        w2_planes = placed("w2_planes", [P, PASSES, N], U8, 105)
-        y_sb = [placed("y%d" % j, [P, T2], F32, board_at[j]) for j in range(RING)] + [placed("y_last", [P, T2], F32, 16)]
-        style_sb = [placed("style%d" % j, [P, M], F32, w2_at[j // 2] + 4 * (j % 2)) for j in range(OUT_TILES)]
-        wgo_sb = placed("wgo_sb", [P, M], F32, 24)
+        last_h_at = slot_at[(LAST - 2) % 4]
+        z_planes = [placed("z_planes0", [P, T2], U8, last_h_at), kept("z_planes1", [P, T2], U8)]
+        w2_planes = placed("w2_planes", [P, PASSES, N], U8, last_h_at + 2)
+        y_sb = [placed("y%d" % j, [P, T2], F32, at) for j, at in enumerate((slot_at[2], slot_at[3], slot_at[0], 16))]
+        style_sb = [placed("style%d" % j, [P, M], F32, w2_at[0] + 4 * j) for j in range(OUT_TILES)]
+        wgo_sb = placed("wgo_sb", [P, M], F32, 40)
+        pulled = [placed("pulled%d" % s, [P, M], F32, factor_at + 4 * s) for s in range(2)]
         for j in range(OUT_TILES):
             nc.sync.dma_start(style_sb[j][:], style[P * j:P * (j + 1), :])
         nc.sync.dma_start(wgo_sb[:], wgo)
@@ -244,8 +254,8 @@ def tile_list_proof_board_kernel(tc, tab_words, tab_scales, offs, w1_words, w1_s
                 rhs_scale=z_planes[a][:, BANK * g:BANK * (g + 1)],
                 start=(a == 0), stop=(a == PASSES - 1))
 
-        def empty_bank(j, g, copy):
-            copy(y_sb[j][:, BANK * g:BANK * (g + 1)], y_banks[g])
+        def empty_bank(j, g):
+            nc.scalar.copy(y_sb[j][:, BANK * g:BANK * (g + 1)], y_banks[g])
 
         def pull(j):
             nc.vector.tensor_tensor(pulled[j % 2][:], y_sb[j][:].indirect(idx3[:]), style_sb[j][:], SUBTRACT)
@@ -258,7 +268,7 @@ def tile_list_proof_board_kernel(tc, tab_words, tab_scales, offs, w1_words, w1_s
         bank_pairs = (back_banks, mx_banks)
         for g in range(CHUNKS):
             outer = g in (0, CHUNKS - 1)
-            turn_back(g, z_grouped[1][g], bank_pairs[g % 2], nc.vector.tensor_copy if outer else nc.scalar.copy)
+            turn_back(1, g, bank_pairs[g % 2], nc.vector.tensor_copy if outer else nc.scalar.copy)
             if g % 2 == 1:
                 second_pass(0, g - 1, 0)
                 second_pass(0, g, 0)
@@ -268,7 +278,9 @@ def tile_list_proof_board_kernel(tc, tab_words, tab_scales, offs, w1_words, w1_s
         for g in range(CHUNKS):
             second_pass(0, g, 1)
         for g in range(CHUNKS):
-            empty_bank(0, g, nc.vector.tensor_copy if g == CHUNKS - 1 else nc.scalar.copy)
+            empty_bank(0, g)
+        released = [released_first, placed("released1", [P, T2], F32, factor_at + 20)]
+        nc.vector.memset(released[1][:].bitcast(I32), 0)
 
         def release(j):
             nc.vector.tensor_tensor(released[j % 2][:].indirect(idx4[:]), pulled[j % 2][:], wgo_sb[:], MULT)
@@ -280,7 +292,7 @@ def tile_list_proof_board_kernel(tc, tab_words, tab_scales, offs, w1_words, w1_s
             for g in range(CHUNKS):
                 for a in range(PASSES):
                     second_pass(j, g, a)
-                empty_bank(j, g, nc.scalar.copy)
+                empty_bank(j, g)
             pull(j)
             if j > 1:
                 release(j - 1)

@@ -29,6 +29,8 @@ CHUNKS = T2 // BANK
 BLOCKS = BANK // P
 OUT_TILES = N // P
 PAGES = 3
+HEAD_FACTORS = 3
+W2_PIECES = 4
 KB = 1024
 
 
@@ -59,15 +61,17 @@ def tile_list_proof_board_kernel(tc, tab_words, tab_scales, offs, w1_words, w1_s
         def whole(bank):
             return bank[:].rearrange("p c t -> p (c t)")
 
-        slot_at = (0, 8, 24, 32)
+        slot_at = (0, 8.5, 23, 31.5)
         w2_at = (44, 52)
         factor_at = 116
         vector_rows = placed("vector_rows", [P, P], F32, 39.75)
         table = [placed("table0", [P, T], U32, 0), placed("table1", [P, T], U32, 24)]
-        table_scales = placed("table_scales", [P, PASSES, T], U8, 16)
+        table_scales = placed("table_scales", [P, T], U8, 16)
         w1_codes = placed("w1_codes", [P, PASSES, 2 * H], U8, 40)
         picked = [placed("picked%d" % a, [P, S], U32, 108 + 4 * a) for a in range(PASSES)]
-        factors = [placed("factor%d" % i, [P, S], F32, factor_at + 4 * i) for i in range(ROW_TILES)]
+        factors = [placed("factor%d" % i, [P, S], F32,
+                          factor_at + 4 * i if i < HEAD_FACTORS else slot_at[(i - 2) % 4] + 4.5)
+                   for i in range(ROW_TILES)]
         h_sb = [placed("h%d" % i, [P, S], F32, w2_at[i] if i < 2 else slot_at[(i - 2) % 4]) for i in range(ROW_TILES)]
         board_sb = [placed("board%d" % i, [P, T2], F32, slot_at[i % 4]) for i in range(ROW_TILES)]
         page_identity = [placed("page_identity%d" % i, [P, P], F32, slot_at[i % 4] + 4) for i in range(ROW_TILES)]
@@ -81,7 +85,7 @@ def tile_list_proof_board_kernel(tc, tab_words, tab_scales, offs, w1_words, w1_s
         identity = kept("identity", [P, P], F32)
         vector_cols = kept("vector_cols", [P, 2 * ROW_TILES], F32)
         wgs_sb = kept("wgs_sb", [P, S], F32)
-        picked_scales = kept("picked_scales", [P, PASSES, S], U8)
+        picked_scales = [kept("picked_scales%d" % a, [P, S], U8) for a in range(PASSES)]
         w1_planes = kept("w1_planes", [P, PASSES, H], U8)
         z_codes = [[kept("z_codes%d_%d" % (a, g), [P, BANK], U32) for g in range(CHUNKS)] for a in range(PASSES)]
         w2_grouped = [kept("w2_grouped%d" % a, [P, N, 4], BF16) for a in range(PASSES)]
@@ -90,11 +94,12 @@ def tile_list_proof_board_kernel(tc, tab_words, tab_scales, offs, w1_words, w1_s
         released_first = kept("released0", [P, T2], F32)
 
         nc.vector.memset(zeros[:], 0.0)
-        nc.vector.memset(table_scales[:].rearrange("p a t -> p (a t)").bitcast(I32), 0)
+        nc.vector.memset(table_scales[:].bitcast(I32), 0)
         nc.vector.memset(w1_planes[:].rearrange("p a c -> p (a c)").bitcast(I32), 0)
         make_identity(nc, identity[:])
         for window in pages + [released_first]:
             nc.vector.memset(window[:].bitcast(I32), 0)
+        nc.vector.memset(picked_scales[1][:].bitcast(I32), 0)
 
         def load_table(a):
             nc.sync.dma_start(table[a][:].bitcast(I32), tab_words[a].rearrange("p t i -> p (t i)").bitcast(I32))
@@ -109,8 +114,7 @@ def tile_list_proof_board_kernel(tc, tab_words, tab_scales, offs, w1_words, w1_s
         nc.scalar.dma_start(vector_rows[0:ROW_TILES, :], b1.rearrange("(i p) -> i p", p=P))
         nc.scalar.dma_start(vector_rows[ROW_TILES:2 * ROW_TILES, :], gain.rearrange("(i p) -> i p", p=P))
         for q in range(4):
-            nc.scalar.dma_start(table_scales[32 * q:32 * q + 4, :, :].bitcast(I32),
-                                tab_scales[:, 4 * q:4 * q + 4, :].rearrange("a r t -> r a t").bitcast(I32))
+            nc.scalar.dma_start(table_scales[32 * q:32 * q + 8, :].bitcast(I32), tab_scales[:, 4 * q:4 * q + 4, :].bitcast(I32))
         nc.tensor.transpose(back_banks[0][:, 0, :], vector_rows[:], identity[:])
         load_table(1)
         nc.sync.dma_start(w1_codes[:].bitcast(I32), w1_words.rearrange("a p c -> p a c").bitcast(I32))
@@ -119,8 +123,10 @@ def tile_list_proof_board_kernel(tc, tab_words, tab_scales, offs, w1_words, w1_s
                                 w1_scales[:, 4 * q:4 * q + 4, :].rearrange("a r c -> r a c").bitcast(I32))
         nc.scalar.copy(vector_cols[:], back_banks[0][:, 0, 0:2 * ROW_TILES])
 
-        for a in range(PASSES):
-            nc.vector.tensor_copy(picked_scales[:, a, :], table_scales[:, a, :].indirect(idx[:]))
+        nc.vector.tensor_copy(picked_scales[0][:], table_scales[:].indirect(idx[:]))
+        for q in range(4):
+            nc.scalar.dma_start(picked_scales[1][32 * q:32 * q + 4, :].bitcast(I32),
+                                picked_scales[0][32 * q + 4:32 * q + 8, :].bitcast(I32))
         nc.vector.tensor_copy(picked[0][:], table[0][:].indirect(idx[:]))
         for half in range(2):
             nc.vector.tensor_copy(picked[1][:, BANK * half:BANK * (half + 1)],
@@ -144,7 +150,7 @@ def tile_list_proof_board_kernel(tc, tab_words, tab_scales, offs, w1_words, w1_s
                         lhsT=w1_codes[:, a, 2 * P * i:2 * P * (i + 1)].bitcast(FP4X4),
                         lhsT_scale=w1_planes[:, a, P * i:P * (i + 1)],
                         rhs=picked[a][:, cols].bitcast(FP8X4),
-                        rhs_scale=picked_scales[:, a, cols],
+                        rhs_scale=picked_scales[a][:, cols],
                         start=(a == 0), stop=(a == PASSES - 1))
 
         def apply_tanh(i, bank, c0, width):
@@ -191,8 +197,8 @@ def tile_list_proof_board_kernel(tc, tab_words, tab_scales, offs, w1_words, w1_s
                 copy = second_copy if b == 1 else nc.scalar.copy
                 copy(grouped_words[:, 2 * P * b:2 * P * (b + 1), :], banks[b][:].rearrange("p (u c) t -> p (c t) u", u=2))
 
-        def group_w2(a, half):
-            cols = slice(N // 2 * half, N // 2 * (half + 1))
+        def group_w2(a, piece):
+            cols = slice(N // W2_PIECES * piece, N // W2_PIECES * (piece + 1))
             nc.scalar.copy(w2_grouped[a][:, cols, :].rearrange("p (c k) j -> p c j k", k=4),
                            w2_raw[a][:, :, cols].rearrange("p j (c k) -> p c j k", k=4))
 
@@ -205,16 +211,16 @@ def tile_list_proof_board_kernel(tc, tab_words, tab_scales, offs, w1_words, w1_s
             place_scores(0, c0, width)
         multiply(1)
         score(1)
+        make_factor(1)
         multiply(2)
 
         for i in range(ROW_TILES):
             turn_board(i)
             if i + 2 < ROW_TILES:
                 score(i + 2)
+                make_factor(i + 2)
             if i > 0:
                 place_scores(i, 0, S)
-            if i < LAST:
-                make_factor(i + 1)
             if i < PASSES:
                 load_w2(i)
             turn_page(i)
@@ -223,7 +229,8 @@ def tile_list_proof_board_kernel(tc, tab_words, tab_scales, offs, w1_words, w1_s
             if i + 3 < ROW_TILES:
                 multiply(i + 3)
             if 1 <= i <= 4:
-                group_w2(*divmod(i - 1, 2))
+                for piece in (2 * (i - 1), 2 * (i - 1) + 1):
+                    group_w2(*divmod(piece, W2_PIECES))
             if TILES_PER_PASS <= i < TILES_PER_PASS + 2:
                 for g in range(2 * (i - TILES_PER_PASS), 2 * (i - TILES_PER_PASS + 1)):
                     turn_back(0, g, back_banks, nc.scalar.copy)
@@ -231,7 +238,7 @@ def tile_list_proof_board_kernel(tc, tab_words, tab_scales, offs, w1_words, w1_s
         last_h_at = slot_at[(LAST - 2) % 4]
         z_planes = [placed("z_planes0", [P, T2], U8, last_h_at), kept("z_planes1", [P, T2], U8)]
         w2_planes = placed("w2_planes", [P, PASSES, N], U8, last_h_at + 2)
-        y_sb = [placed("y%d" % j, [P, T2], F32, at) for j, at in enumerate((slot_at[2], slot_at[3], slot_at[0], 16))]
+        y_sb = [placed("y%d" % j, [P, T2], F32, at) for j, at in enumerate((slot_at[2], slot_at[3], slot_at[0], 15))]
         style_sb = [placed("style%d" % j, [P, M], F32, w2_at[0] + 4 * j) for j in range(OUT_TILES)]
         wgo_sb = placed("wgo_sb", [P, M], F32, 40)
         pulled = [placed("pulled%d" % s, [P, M], F32, factor_at + 4 * s) for s in range(2)]

@@ -29,6 +29,8 @@ CHUNKS = T2 // BANK
 BLOCKS = BANK // P
 OUT_TILES = N // P
 PAGES = 3
+FIRST = 256
+HALF = BANK // 2
 HEAD_FACTORS = 3
 W2_PIECES = 4
 KB = 1024
@@ -61,43 +63,44 @@ def tile_list_proof_board_kernel(tc, tab_words, tab_scales, offs, w1_words, w1_s
         def whole(bank):
             return bank[:].rearrange("p c t -> p (c t)")
 
-        slot_at = (0, 8.5, 23, 31.5)
-        w2_at = (44, 52)
-        factor_at = 116
-        vector_rows = placed("vector_rows", [P, P], F32, 39.75)
+        slot_at = (28, 36.5, 54, 71.5)
+        w2_at = (45, 62.5)
+        factor_at = 120
+        vector_rows = placed("vector_rows", [P, P], F32, 23.75)
         table = [placed("table0", [P, T], U32, 0), placed("table1", [P, T], U32, 24)]
         table_scales = placed("table_scales", [P, T], U8, 16)
-        w1_codes = placed("w1_codes", [P, PASSES, 2 * H], U8, 40)
-        picked = [placed("picked%d" % a, [P, S], U32, 108 + 4 * a) for a in range(PASSES)]
+        wgs_sb = placed("wgs_sb", [P, S], F32, 24)
+        w1_codes = placed("w1_codes", [P, PASSES, 2 * H], U8, 20)
+        picked = [placed("picked%d" % a, [P, S], U32, 112 + 4 * a) for a in range(PASSES)]
         factors = [placed("factor%d" % i, [P, S], F32,
                           factor_at + 4 * i if i < HEAD_FACTORS else slot_at[(i - 2) % 4] + 4.5)
                    for i in range(ROW_TILES)]
-        h_sb = [placed("h%d" % i, [P, S], F32, w2_at[i] if i < 2 else slot_at[(i - 2) % 4]) for i in range(ROW_TILES)]
+        h_sb = [placed("h%d" % i, [P, S], F32, w2_at[i] + 6 if i < 2 else slot_at[(i - 2) % 4]) for i in range(ROW_TILES)]
         board_sb = [placed("board%d" % i, [P, T2], F32, slot_at[i % 4]) for i in range(ROW_TILES)]
         page_identity = [placed("page_identity%d" % i, [P, P], F32, slot_at[i % 4] + 4) for i in range(ROW_TILES)]
         w2_raw = [placed("w2_raw%d" % a, [P, 4, N], F32, w2_at[a]) for a in range(PASSES)]
-        turned = [[placed("turned%d_%d" % (a, g), [P, 2, BLOCKS, 2 * P], BF16, 60 + 16 * a + 4 * g) for g in range(CHUNKS)]
+        turned = [[placed("turned%d_%d" % (a, g), [P, 2, BLOCKS, 2 * P], BF16, 80 + 16 * a + 4 * g) for g in range(CHUNKS)]
                   for a in range(PASSES)]
-        z_grouped = [[placed("z_grouped%d_%d" % (a, g), [P, BANK, 4], BF16, (92, factor_at + 8)[a] + 4 * g)
+        z_grouped = [[placed("z_grouped%d_%d" % (a, g), [P, BANK, 4], BF16, (0, factor_at + 8)[a] + 4 * g)
                       for g in range(CHUNKS)] for a in range(PASSES)]
 
         zeros = kept("zeros", [P, P], F32)
         identity = kept("identity", [P, P], F32)
         vector_cols = kept("vector_cols", [P, 2 * ROW_TILES], F32)
-        wgs_sb = kept("wgs_sb", [P, S], F32)
+        wgs_first = kept("wgs_first", [P, BANK], F32)
         picked_scales = [kept("picked_scales%d" % a, [P, S], U8) for a in range(PASSES)]
         w1_planes = kept("w1_planes", [P, PASSES, H], U8)
         z_codes = [[kept("z_codes%d_%d" % (a, g), [P, BANK], U32) for g in range(CHUNKS)] for a in range(PASSES)]
         w2_grouped = [kept("w2_grouped%d" % a, [P, N, 4], BF16) for a in range(PASSES)]
         w2_codes = kept("w2_codes", [P, PASSES, N], U32)
         pages = [kept("page%d" % s, [P, T2], F32) for s in range(PAGES)]
-        released_first = kept("released0", [P, T2], F32)
+        released = [kept("released%d" % s, [P, T2], F32) for s in range(2)]
 
         nc.vector.memset(zeros[:], 0.0)
         nc.vector.memset(table_scales[:].bitcast(I32), 0)
         nc.vector.memset(w1_planes[:].rearrange("p a c -> p (a c)").bitcast(I32), 0)
         make_identity(nc, identity[:])
-        for window in pages + [released_first]:
+        for window in pages + released:
             nc.vector.memset(window[:].bitcast(I32), 0)
         nc.vector.memset(picked_scales[1][:].bitcast(I32), 0)
 
@@ -108,7 +111,7 @@ def tile_list_proof_board_kernel(tc, tab_words, tab_scales, offs, w1_words, w1_s
         nc.sync.dma_start(idx2[:], offs2)
         nc.sync.dma_start(idx3[:], offs3)
         nc.sync.dma_start(idx4[:], offs4)
-        nc.sync.dma_start(wgs_sb[:], wgs)
+        nc.sync.dma_start(wgs_first[:], wgs[:, 0:BANK])
         load_table(0)
         nc.scalar.activation(vector_rows[:], zeros[:], TANH)
         nc.scalar.dma_start(vector_rows[0:ROW_TILES, :], b1.rearrange("(i p) -> i p", p=P))
@@ -138,8 +141,9 @@ def tile_list_proof_board_kernel(tc, tab_words, tab_scales, offs, w1_words, w1_s
         def load_w2(a):
             nc.sync.dma_start(w2_raw[a][:], w2[512 * a:512 * (a + 1), :].rearrange("(p j) n -> p j n", j=4))
 
-        def make_factor(i):
-            nc.scalar.activation(factors[i][:], wgs_sb[:], COPY, scale=vector_cols[:, ROW_TILES + i:ROW_TILES + i + 1])
+        def make_factor(i, c0=0, width=S, weights=wgs_sb):
+            nc.scalar.activation(factors[i][:, c0:c0 + width], weights[:, c0:c0 + width], COPY,
+                                 scale=vector_cols[:, ROW_TILES + i:ROW_TILES + i + 1])
 
         def first_product(i, bank, c0, width, group):
             for g0 in range(0, width, group):
@@ -187,27 +191,28 @@ def tile_list_proof_board_kernel(tc, tab_words, tab_scales, offs, w1_words, w1_s
                     turned[a][g][:, :, :, 64 * place:64 * (place + 1)].rearrange("t u c (w e) -> t u c w e", e=2),
                     sum_banks[g][:].rearrange("t c (w u e) -> t u c w e", u=2, e=2))
 
-        def turn_back(a, g, banks, second_copy):
+        def turn_back(a, g, banks, copies):
             words = turned[a][g][:].bitcast(F32)
             grouped_words = z_grouped[a][g][:].bitcast(F32)
             for b in range(2):
                 for u in range(2):
                     for c in range(2):
                         nc.tensor.transpose(banks[b][:, 2 * u + c, :], words[:, u, 2 * b + c, :], identity[:])
-                copy = second_copy if b == 1 else nc.scalar.copy
-                copy(grouped_words[:, 2 * P * b:2 * P * (b + 1), :], banks[b][:].rearrange("p (u c) t -> p (c t) u", u=2))
+                copies[b](grouped_words[:, 2 * P * b:2 * P * (b + 1), :], banks[b][:].rearrange("p (u c) t -> p (c t) u", u=2))
 
         def group_w2(a, piece):
             cols = slice(N // W2_PIECES * piece, N // W2_PIECES * (piece + 1))
             nc.scalar.copy(w2_grouped[a][:, cols, :].rearrange("p (c k) j -> p c j k", k=4),
                            w2_raw[a][:, :, cols].rearrange("p j (c k) -> p c j k", k=4))
 
-        for i in range(4):
+        nc.sync.dma_start(wgs_sb[:], wgs)
+        for i in range(2):
             load_board(i)
-        make_factor(0)
-        for bank, c0, width, group in ((mx_banks[0], 0, 256, P), (back_banks[1], 256, 256, P), (mx_banks[1], BANK, BANK, BANK)):
+        for bank, c0, width, group in ((mx_banks[0], 0, FIRST, P), (back_banks[1], FIRST, BANK - FIRST, P),
+                                       (mx_banks[1], BANK, BANK, BANK)):
             first_product(0, bank, c0, width, group)
             apply_tanh(0, bank, c0, width)
+            make_factor(0, c0, width, wgs_first if c0 < BANK else wgs_sb)
             place_scores(0, c0, width)
         multiply(1)
         score(1)
@@ -221,11 +226,11 @@ def tile_list_proof_board_kernel(tc, tab_words, tab_scales, offs, w1_words, w1_s
                 make_factor(i + 2)
             if i > 0:
                 place_scores(i, 0, S)
+            if i + 2 < ROW_TILES:
+                load_board(i + 2)
             if i < PASSES:
                 load_w2(i)
             turn_page(i)
-            if 2 <= i < ROW_TILES - 2:
-                load_board(i + 2)
             if i + 3 < ROW_TILES:
                 multiply(i + 3)
             if 1 <= i <= 4:
@@ -233,36 +238,35 @@ def tile_list_proof_board_kernel(tc, tab_words, tab_scales, offs, w1_words, w1_s
                     group_w2(*divmod(piece, W2_PIECES))
             if TILES_PER_PASS <= i < TILES_PER_PASS + 2:
                 for g in range(2 * (i - TILES_PER_PASS), 2 * (i - TILES_PER_PASS + 1)):
-                    turn_back(0, g, back_banks, nc.scalar.copy)
+                    turn_back(0, g, back_banks, (nc.scalar.copy, nc.scalar.copy))
 
         last_h_at = slot_at[(LAST - 2) % 4]
         z_planes = [placed("z_planes0", [P, T2], U8, last_h_at), kept("z_planes1", [P, T2], U8)]
         w2_planes = placed("w2_planes", [P, PASSES, N], U8, last_h_at + 2)
-        y_sb = [placed("y%d" % j, [P, T2], F32, at) for j, at in enumerate((slot_at[2], slot_at[3], slot_at[0], 15))]
-        style_sb = [placed("style%d" % j, [P, M], F32, w2_at[0] + 4 * j) for j in range(OUT_TILES)]
-        wgo_sb = placed("wgo_sb", [P, M], F32, 40)
+        y_sb = [placed("y%d" % j, [P, T2], F32, at) for j, at in enumerate((slot_at[2], factor_at + 16, slot_at[0], 80))]
+        style_sb = [placed("style%d" % j, [P, M], F32, w2_at[j // 2] + 4 * (j % 2)) for j in range(OUT_TILES)]
+        wgo_sb = placed("wgo_sb", [P, M], F32, 20)
         pulled = [placed("pulled%d" % s, [P, M], F32, factor_at + 4 * s) for s in range(2)]
         for j in range(OUT_TILES):
             nc.sync.dma_start(style_sb[j][:], style[P * j:P * (j + 1), :])
         nc.sync.dma_start(wgo_sb[:], wgo)
 
-        def quantize_z(a, g):
-            nc.vector.quantize_mx(out=z_codes[a][g][:].bitcast(FP8X4), scales=z_planes[a][:, BANK * g:BANK * (g + 1)],
-                                  in_=z_grouped[a][g][:].rearrange("p t j -> p (t j)"))
+        def quantize_z(a, g, c0=0, width=BANK):
+            nc.vector.quantize_mx(out=z_codes[a][g][:, c0:c0 + width].bitcast(FP8X4),
+                                  scales=z_planes[a][:, BANK * g + c0:BANK * g + c0 + width],
+                                  in_=z_grouped[a][g][:, c0:c0 + width, :].rearrange("p t j -> p (t j)"))
 
-        y_banks = [whole(bank) for bank in sum_banks]
-
-        def second_pass(j, g, a):
+        def second_pass(j, g, a, bank, c0=0, width=BANK):
             nc.tensor.matmul_mx(
-                out=y_banks[g],
+                out=whole(bank)[:, 0:width],
                 lhsT=w2_codes[:, a, P * j:P * (j + 1)].bitcast(FP8X4),
                 lhsT_scale=w2_planes[:, a, P * j:P * (j + 1)],
-                rhs=z_codes[a][g][:].bitcast(FP8X4),
-                rhs_scale=z_planes[a][:, BANK * g:BANK * (g + 1)],
+                rhs=z_codes[a][g][:, c0:c0 + width].bitcast(FP8X4),
+                rhs_scale=z_planes[a][:, BANK * g + c0:BANK * g + c0 + width],
                 start=(a == 0), stop=(a == PASSES - 1))
 
-        def empty_bank(j, g):
-            nc.scalar.copy(y_sb[j][:, BANK * g:BANK * (g + 1)], y_banks[g])
+        def empty_bank(j, g, bank, copy, c0=0, width=BANK):
+            copy(y_sb[j][:, BANK * g + c0:BANK * g + c0 + width], whole(bank)[:, 0:width])
 
         def pull(j):
             nc.vector.tensor_tensor(pulled[j % 2][:], y_sb[j][:].indirect(idx3[:]), style_sb[j][:], SUBTRACT)
@@ -270,36 +274,35 @@ def tile_list_proof_board_kernel(tc, tab_words, tab_scales, offs, w1_words, w1_s
         for a in range(PASSES):
             nc.vector.quantize_mx(out=w2_codes[:, a, :].bitcast(FP8X4), scales=w2_planes[:, a, :],
                                   in_=w2_grouped[a][:].rearrange("p n j -> p (n j)"))
+        end = CHUNKS - 1
+        s0, s1, s2, s3 = sum_banks
+        on_scalar, on_vector = nc.scalar.copy, nc.vector.tensor_copy
+        back_pairs = (back_banks, mx_banks, (s2, s3), back_banks)
+        back_copies = ((on_scalar, on_vector), (on_vector, on_scalar), (on_scalar, on_scalar), (on_scalar, on_vector))
+        pieces = ((0, s0, 0, BANK), (1, s1, 0, BANK), (2, mx_banks[0], 0, BANK), (end, mx_banks[1], 0, HALF), (end, s2, HALF, HALF))
         for g in range(CHUNKS):
-            quantize_z(0, g)
-        bank_pairs = (back_banks, mx_banks)
-        for g in range(CHUNKS):
-            outer = g in (0, CHUNKS - 1)
-            turn_back(1, g, bank_pairs[g % 2], nc.vector.tensor_copy if outer else nc.scalar.copy)
-            if g % 2 == 1:
-                second_pass(0, g - 1, 0)
-                second_pass(0, g, 0)
-            if g > 0:
-                quantize_z(1, g - 1)
-        quantize_z(1, CHUNKS - 1)
-        for g in range(CHUNKS):
-            second_pass(0, g, 1)
-        for g in range(CHUNKS):
-            empty_bank(0, g)
-        released = [released_first, placed("released1", [P, T2], F32, factor_at + 20)]
-        nc.vector.memset(released[1][:].bitcast(I32), 0)
+            turn_back(1, g, back_pairs[g], back_copies[g])
+        for g, bank, c0, width in pieces:
+            quantize_z(1, g, c0, width)
+        for g, bank, c0, width in pieces:
+            if c0 == 0:
+                quantize_z(0, g)
+            for a in range(PASSES):
+                second_pass(0, g, a, bank, c0, width)
+            empty_bank(0, g, bank, on_vector if c0 else on_scalar, c0, width)
 
         def release(j):
             nc.vector.tensor_tensor(released[j % 2][:].indirect(idx4[:]), pulled[j % 2][:], wgo_sb[:], MULT)
             nc.sync.dma_start(out[P * j:P * (j + 1), :], released[j % 2][:])
 
+        late_banks = back_banks + [mx_banks[1], s2]
         pull(0)
         release(0)
         for j in range(1, OUT_TILES):
             for g in range(CHUNKS):
                 for a in range(PASSES):
-                    second_pass(j, g, a)
-                empty_bank(j, g)
+                    second_pass(j, g, a, late_banks[g])
+                empty_bank(j, g, late_banks[g], nc.scalar.copy)
             pull(j)
             if j > 1:
                 release(j - 1)

@@ -33,6 +33,7 @@ FIRST = 256
 HALF = BANK // 2
 HEAD_FACTORS = 3
 W2_PIECES = 4
+EARLY_TILES = 2
 KB = 1024
 
 
@@ -66,11 +67,11 @@ def tile_list_proof_board_kernel(tc, tab_words, tab_scales, offs, w1_words, w1_s
         slot_at = (28, 36.5, 54, 71.5)
         w2_at = (45, 62.5)
         factor_at = 120
-        vector_rows = placed("vector_rows", [P, P], F32, 23.75)
         table = [placed("table0", [P, T], U32, 0), placed("table1", [P, T], U32, 24)]
-        table_scales = placed("table_scales", [P, T], U8, 16)
-        wgs_sb = placed("wgs_sb", [P, S], F32, 24)
-        w1_codes = placed("w1_codes", [P, PASSES, 2 * H], U8, 20)
+        table_scales = placed("table_scales", [P, T], U8, 24)
+        wgs_sb = placed("wgs_sb", [P, S], F32, 12)
+        w1_first = placed("w1_first", [P, PASSES, 2 * P * EARLY_TILES], U8, 20)
+        w1_rest = placed("w1_rest", [P, PASSES, 2 * (H - P * EARLY_TILES)], U8, 8)
         picked = [placed("picked%d" % a, [P, S], U32, 112 + 4 * a) for a in range(PASSES)]
         factors = [placed("factor%d" % i, [P, S], F32,
                           factor_at + 4 * i if i < HEAD_FACTORS else slot_at[(i - 2) % 4] + 4.5)
@@ -81,14 +82,16 @@ def tile_list_proof_board_kernel(tc, tab_words, tab_scales, offs, w1_words, w1_s
         w2_raw = [placed("w2_raw%d" % a, [P, 4, N], F32, w2_at[a]) for a in range(PASSES)]
         turned = [[placed("turned%d_%d" % (a, g), [P, 2, BLOCKS, 2 * P], BF16, 80 + 16 * a + 4 * g) for g in range(CHUNKS)]
                   for a in range(PASSES)]
-        z_grouped = [[placed("z_grouped%d_%d" % (a, g), [P, BANK, 4], BF16, (0, factor_at + 8)[a] + 4 * g)
+        z_grouped = [[placed("z_grouped%d_%d" % (a, g), [P, BANK, 4], BF16, (0, 4, 16, 24)[g] if a == 0 else factor_at + 8 + 4 * g)
                       for g in range(CHUNKS)] for a in range(PASSES)]
 
         zeros = kept("zeros", [P, P], F32)
         identity = kept("identity", [P, P], F32)
         vector_cols = kept("vector_cols", [P, 2 * ROW_TILES], F32)
         wgs_first = kept("wgs_first", [P, BANK], F32)
-        picked_scales = [kept("picked_scales%d" % a, [P, S], U8) for a in range(PASSES)]
+        vector_rows = kept("vector_rows", [P, P], F32)
+        picked_rows = kept("picked_rows", [P, S], U8)
+        picked_scales = kept("picked_scales", [P, PASSES, S], U8)
         w1_planes = kept("w1_planes", [P, PASSES, H], U8)
         z_codes = [[kept("z_codes%d_%d" % (a, g), [P, BANK], U32) for g in range(CHUNKS)] for a in range(PASSES)]
         w2_grouped = [kept("w2_grouped%d" % a, [P, N, 4], BF16) for a in range(PASSES)]
@@ -96,44 +99,51 @@ def tile_list_proof_board_kernel(tc, tab_words, tab_scales, offs, w1_words, w1_s
         pages = [kept("page%d" % s, [P, T2], F32) for s in range(PAGES)]
         released = [kept("released%d" % s, [P, T2], F32) for s in range(2)]
 
-        nc.vector.memset(zeros[:], 0.0)
         nc.vector.memset(table_scales[:].bitcast(I32), 0)
         nc.vector.memset(w1_planes[:].rearrange("p a c -> p (a c)").bitcast(I32), 0)
+        nc.vector.memset(zeros[:], 0.0)
+        nc.vector.memset(picked_scales[:].rearrange("p a c -> p (a c)").bitcast(I32), 0)
         make_identity(nc, identity[:])
-        for window in pages + released:
-            nc.vector.memset(window[:].bitcast(I32), 0)
-        nc.vector.memset(picked_scales[1][:].bitcast(I32), 0)
 
         def load_table(a):
             nc.sync.dma_start(table[a][:].bitcast(I32), tab_words[a].rearrange("p t i -> p (t i)").bitcast(I32))
 
+        w1_by_partition = w1_words.rearrange("a p c -> p a c")
         nc.sync.dma_start(idx[:], offs)
         nc.sync.dma_start(idx2[:], offs2)
         nc.sync.dma_start(idx3[:], offs3)
         nc.sync.dma_start(idx4[:], offs4)
+        nc.sync.dma_start(w1_first[:].bitcast(I32), w1_by_partition[:, :, 0:2 * P * EARLY_TILES].bitcast(I32))
         nc.sync.dma_start(wgs_first[:], wgs[:, 0:BANK])
         load_table(0)
-        nc.scalar.activation(vector_rows[:], zeros[:], TANH)
-        nc.scalar.dma_start(vector_rows[0:ROW_TILES, :], b1.rearrange("(i p) -> i p", p=P))
-        nc.scalar.dma_start(vector_rows[ROW_TILES:2 * ROW_TILES, :], gain.rearrange("(i p) -> i p", p=P))
-        for q in range(4):
-            nc.scalar.dma_start(table_scales[32 * q:32 * q + 8, :].bitcast(I32), tab_scales[:, 4 * q:4 * q + 4, :].bitcast(I32))
-        nc.tensor.transpose(back_banks[0][:, 0, :], vector_rows[:], identity[:])
-        load_table(1)
-        nc.sync.dma_start(w1_codes[:].bitcast(I32), w1_words.rearrange("a p c -> p a c").bitcast(I32))
+        nc.scalar.dma_start(table_scales[0:P:4, :].bitcast(I32), tab_scales.rearrange("a q t -> (a q) t").bitcast(I32))
         for q in range(4):
             nc.scalar.dma_start(w1_planes[32 * q:32 * q + 4, :, :].bitcast(I32),
                                 w1_scales[:, 4 * q:4 * q + 4, :].rearrange("a r c -> r a c").bitcast(I32))
-        nc.scalar.copy(vector_cols[:], back_banks[0][:, 0, 0:2 * ROW_TILES])
+        nc.scalar.activation(vector_rows[:], zeros[:], TANH)
+        nc.scalar.dma_start(vector_rows[0:ROW_TILES, :], b1.rearrange("(i p) -> i p", p=P))
+        nc.scalar.dma_start(vector_rows[ROW_TILES:2 * ROW_TILES, :], gain.rearrange("(i p) -> i p", p=P))
+        nc.tensor.transpose(back_banks[0][:, 0, :], vector_rows[:], identity[:])
 
-        nc.vector.tensor_copy(picked_scales[0][:], table_scales[:].indirect(idx[:]))
-        for q in range(4):
-            nc.scalar.dma_start(picked_scales[1][32 * q:32 * q + 4, :].bitcast(I32),
-                                picked_scales[0][32 * q + 4:32 * q + 8, :].bitcast(I32))
+        nc.vector.tensor_copy(picked_rows[:], table_scales[:].indirect(idx[:]))
+
+        def move_scales(a, q):
+            first = 64 * a + 16 * q
+            nc.scalar.dma_start(picked_scales[32 * q:32 * q + 4, a, :].bitcast(I32),
+                                picked_rows[first:first + 16:4, :].bitcast(I32))
+
+        move_scales(0, 0)
+        load_table(1)
+        for m in range(1, 8):
+            move_scales(*divmod(m, 4))
+        nc.scalar.copy(vector_cols[:], back_banks[0][:, 0, 0:2 * ROW_TILES])
         nc.vector.tensor_copy(picked[0][:], table[0][:].indirect(idx[:]))
         for half in range(2):
             nc.vector.tensor_copy(picked[1][:, BANK * half:BANK * (half + 1)],
                                   table[1][:].indirect(idx[:, 32 * half:32 * (half + 1)]))
+        for window in pages + released:
+            nc.vector.memset(window[:].bitcast(I32), 0)
+        nc.sync.dma_start(w1_rest[:].bitcast(I32), w1_by_partition[:, :, 2 * P * EARLY_TILES:].bitcast(I32))
 
         def load_board(i):
             nc.sync.dma_start(board_sb[i][:], board[P * i:P * (i + 1), :])
@@ -148,13 +158,14 @@ def tile_list_proof_board_kernel(tc, tab_words, tab_scales, offs, w1_words, w1_s
         def first_product(i, bank, c0, width, group):
             for g0 in range(0, width, group):
                 cols = slice(c0 + g0, c0 + g0 + group)
+                codes, tile_at = (w1_first, i) if i < EARLY_TILES else (w1_rest, i - EARLY_TILES)
                 for a in range(PASSES):
                     nc.tensor.matmul_mx(
                         out=whole(bank)[:, g0:g0 + group],
-                        lhsT=w1_codes[:, a, 2 * P * i:2 * P * (i + 1)].bitcast(FP4X4),
+                        lhsT=codes[:, a, 2 * P * tile_at:2 * P * (tile_at + 1)].bitcast(FP4X4),
                         lhsT_scale=w1_planes[:, a, P * i:P * (i + 1)],
                         rhs=picked[a][:, cols].bitcast(FP8X4),
-                        rhs_scale=picked_scales[a][:, cols],
+                        rhs_scale=picked_scales[:, a, cols],
                         start=(a == 0), stop=(a == PASSES - 1))
 
         def apply_tanh(i, bank, c0, width):
@@ -245,7 +256,7 @@ def tile_list_proof_board_kernel(tc, tab_words, tab_scales, offs, w1_words, w1_s
         w2_planes = placed("w2_planes", [P, PASSES, N], U8, last_h_at + 2)
         y_sb = [placed("y%d" % j, [P, T2], F32, at) for j, at in enumerate((slot_at[2], factor_at + 16, slot_at[0], 80))]
         style_sb = [placed("style%d" % j, [P, M], F32, w2_at[j // 2] + 4 * (j % 2)) for j in range(OUT_TILES)]
-        wgo_sb = placed("wgo_sb", [P, M], F32, 20)
+        wgo_sb = placed("wgo_sb", [P, M], F32, 8)
         pulled = [placed("pulled%d" % s, [P, M], F32, factor_at + 4 * s) for s in range(2)]
         for j in range(OUT_TILES):
             nc.sync.dma_start(style_sb[j][:], style[P * j:P * (j + 1), :])

@@ -64,17 +64,18 @@ def tile_list_proof_board_kernel(tc, tab_words, tab_scales, offs, w1_words, w1_s
         def whole(bank):
             return bank[:].rearrange("p c t -> p (c t)")
 
-        slot_at = (28, 36.5, 54, 71.5)
+        slot_at = (25, 33.5, 54, 71.5)
         w2_at = (45, 62.5)
         factor_at = 120
+        window_at = 144
         table = [placed("table0", [P, T], U32, 0), placed("table1", [P, T], U32, 24)]
-        table_scales = placed("table_scales", [P, T], U8, 24)
+        table_scales = placed("table_scales", [P, T], U8, 25)
         wgs_sb = placed("wgs_sb", [P, S], F32, 12)
-        w1_first = placed("w1_first", [P, PASSES, 2 * P * EARLY_TILES], U8, 20)
+        w1_first = placed("w1_first", [P, PASSES, 2 * P * EARLY_TILES], U8, 16)
         w1_rest = placed("w1_rest", [P, PASSES, 2 * (H - P * EARLY_TILES)], U8, 8)
         picked = [placed("picked%d" % a, [P, S], U32, 112 + 4 * a) for a in range(PASSES)]
         factors = [placed("factor%d" % i, [P, S], F32,
-                          factor_at + 4 * i if i < HEAD_FACTORS else slot_at[(i - 2) % 4] + 4.5)
+                          window_at + 8 * i if i < HEAD_FACTORS else slot_at[(i - 2) % 4] + 4.5)
                    for i in range(ROW_TILES)]
         h_sb = [placed("h%d" % i, [P, S], F32, w2_at[i] + 6 if i < 2 else slot_at[(i - 2) % 4]) for i in range(ROW_TILES)]
         board_sb = [placed("board%d" % i, [P, T2], F32, slot_at[i % 4]) for i in range(ROW_TILES)]
@@ -82,7 +83,7 @@ def tile_list_proof_board_kernel(tc, tab_words, tab_scales, offs, w1_words, w1_s
         w2_raw = [placed("w2_raw%d" % a, [P, 4, N], F32, w2_at[a]) for a in range(PASSES)]
         turned = [[placed("turned%d_%d" % (a, g), [P, 2, BLOCKS, 2 * P], BF16, 80 + 16 * a + 4 * g) for g in range(CHUNKS)]
                   for a in range(PASSES)]
-        z_grouped = [[placed("z_grouped%d_%d" % (a, g), [P, BANK, 4], BF16, (0, 4, 16, 24)[g] if a == 0 else factor_at + 8 + 4 * g)
+        z_grouped = [[placed("z_grouped%d_%d" % (a, g), [P, BANK, 4], BF16, (0, 4, factor_at, factor_at + 4)[g] if a == 0 else factor_at + 8 + 4 * g)
                       for g in range(CHUNKS)] for a in range(PASSES)]
 
         zeros = kept("zeros", [P, P], F32)
@@ -96,12 +97,12 @@ def tile_list_proof_board_kernel(tc, tab_words, tab_scales, offs, w1_words, w1_s
         z_codes = [[kept("z_codes%d_%d" % (a, g), [P, BANK], U32) for g in range(CHUNKS)] for a in range(PASSES)]
         w2_grouped = [kept("w2_grouped%d" % a, [P, N, 4], BF16) for a in range(PASSES)]
         w2_codes = kept("w2_codes", [P, PASSES, N], U32)
-        pages = [kept("page%d" % s, [P, T2], F32) for s in range(PAGES)]
-        released = [kept("released%d" % s, [P, T2], F32) for s in range(2)]
+        pages = [kept("page0", [P, T2], F32), placed("page1", [P, T2], F32, 17), placed("page2", [P, T2], F32, window_at)]
+        released = [placed("released%d" % s, [P, T2], F32, window_at + 8 * (s + 1)) for s in range(2)]
 
         nc.vector.memset(table_scales[:].bitcast(I32), 0)
-        nc.vector.memset(w1_planes[:].rearrange("p a c -> p (a c)").bitcast(I32), 0)
         nc.vector.memset(zeros[:], 0.0)
+        nc.vector.memset(w1_planes[:].rearrange("p a c -> p (a c)").bitcast(I32), 0)
         nc.vector.memset(picked_scales[:].rearrange("p a c -> p (a c)").bitcast(I32), 0)
         make_identity(nc, identity[:])
 
@@ -115,12 +116,12 @@ def tile_list_proof_board_kernel(tc, tab_words, tab_scales, offs, w1_words, w1_s
         nc.sync.dma_start(idx4[:], offs4)
         nc.sync.dma_start(w1_first[:].bitcast(I32), w1_by_partition[:, :, 0:2 * P * EARLY_TILES].bitcast(I32))
         nc.sync.dma_start(wgs_first[:], wgs[:, 0:BANK])
+        nc.sync.dma_start(table_scales[0:P:4, :].bitcast(I32), tab_scales.rearrange("a q t -> (a q) t").bitcast(I32))
         load_table(0)
-        nc.scalar.dma_start(table_scales[0:P:4, :].bitcast(I32), tab_scales.rearrange("a q t -> (a q) t").bitcast(I32))
+        nc.scalar.activation(vector_rows[:], zeros[:], TANH)
         for q in range(4):
             nc.scalar.dma_start(w1_planes[32 * q:32 * q + 4, :, :].bitcast(I32),
                                 w1_scales[:, 4 * q:4 * q + 4, :].rearrange("a r c -> r a c").bitcast(I32))
-        nc.scalar.activation(vector_rows[:], zeros[:], TANH)
         nc.scalar.dma_start(vector_rows[0:ROW_TILES, :], b1.rearrange("(i p) -> i p", p=P))
         nc.scalar.dma_start(vector_rows[ROW_TILES:2 * ROW_TILES, :], gain.rearrange("(i p) -> i p", p=P))
         nc.tensor.transpose(back_banks[0][:, 0, :], vector_rows[:], identity[:])
@@ -141,8 +142,8 @@ def tile_list_proof_board_kernel(tc, tab_words, tab_scales, offs, w1_words, w1_s
         for half in range(2):
             nc.vector.tensor_copy(picked[1][:, BANK * half:BANK * (half + 1)],
                                   table[1][:].indirect(idx[:, 32 * half:32 * (half + 1)]))
-        for window in pages + released:
-            nc.vector.memset(window[:].bitcast(I32), 0)
+        nc.vector.memset(pages[0][:].bitcast(I32), 0)
+        nc.gpsimd.memset(pages[1][:].bitcast(I32), 0)
         nc.sync.dma_start(w1_rest[:].bitcast(I32), w1_by_partition[:, :, 2 * P * EARLY_TILES:].bitcast(I32))
 
         def load_board(i):
@@ -225,6 +226,7 @@ def tile_list_proof_board_kernel(tc, tab_words, tab_scales, offs, w1_words, w1_s
             apply_tanh(0, bank, c0, width)
             make_factor(0, c0, width, wgs_first if c0 < BANK else wgs_sb)
             place_scores(0, c0, width)
+        nc.gpsimd.memset(pages[2][:].bitcast(I32), 0)
         multiply(1)
         score(1)
         make_factor(1)
@@ -237,6 +239,8 @@ def tile_list_proof_board_kernel(tc, tab_words, tab_scales, offs, w1_words, w1_s
                 make_factor(i + 2)
             if i > 0:
                 place_scores(i, 0, S)
+            if 1 <= i <= 2:
+                nc.gpsimd.memset(released[i - 1][:].bitcast(I32), 0)
             if i + 2 < ROW_TILES:
                 load_board(i + 2)
             if i < PASSES:

@@ -68,14 +68,14 @@ def tile_list_proof_board_kernel(tc, tab_words, tab_scales, offs, w1_words, w1_s
         w2_at = (45, 62.5)
         factor_at = 120
         window_at = 144
-        table = [placed("table0", [P, T], U32, 0), placed("table1", [P, T], U32, 24)]
-        table_scales = placed("table_scales", [P, T], U8, 25)
-        wgs_sb = placed("wgs_sb", [P, S], F32, 12)
-        w1_first = placed("w1_first", [P, PASSES, 2 * P * EARLY_TILES], U8, 16)
-        w1_rest = placed("w1_rest", [P, PASSES, 2 * (H - P * EARLY_TILES)], U8, 8)
+        table = [placed("table0", [P, T], U32, window_at + 8), placed("table1", [P, T], U32, 24)]
+        table_scales = placed("table_scales", [P, T], U8, 21)
+        wgs_sb = placed("wgs_sb", [P, S], F32, window_at + 19.5)
+        w1_first = placed("w1_first", [P, PASSES, 2 * P * EARLY_TILES], U8, 12)
+        w1_rest = placed("w1_rest", [P, PASSES, 2 * (H - P * EARLY_TILES)], U8, window_at + 16.5)
         picked = [placed("picked%d" % a, [P, S], U32, 112 + 4 * a) for a in range(PASSES)]
         factors = [placed("factor%d" % i, [P, S], F32,
-                          window_at + 8 * i if i < HEAD_FACTORS else slot_at[(i - 2) % 4] + 4.5)
+                          4 * i if i < HEAD_FACTORS else slot_at[(i - 2) % 4] + 4.5)
                    for i in range(ROW_TILES)]
         h_sb = [placed("h%d" % i, [P, S], F32, w2_at[i] + 6 if i < 2 else slot_at[(i - 2) % 4]) for i in range(ROW_TILES)]
         board_sb = [placed("board%d" % i, [P, T2], F32, slot_at[i % 4]) for i in range(ROW_TILES)]
@@ -83,7 +83,7 @@ def tile_list_proof_board_kernel(tc, tab_words, tab_scales, offs, w1_words, w1_s
         w2_raw = [placed("w2_raw%d" % a, [P, 4, N], F32, w2_at[a]) for a in range(PASSES)]
         turned = [[placed("turned%d_%d" % (a, g), [P, 2, BLOCKS, 2 * P], BF16, 80 + 16 * a + 4 * g) for g in range(CHUNKS)]
                   for a in range(PASSES)]
-        z_grouped = [[placed("z_grouped%d_%d" % (a, g), [P, BANK, 4], BF16, (0, 4, factor_at, factor_at + 4)[g] if a == 0 else factor_at + 8 + 4 * g)
+        z_grouped = [[placed("z_grouped%d_%d" % (a, g), [P, BANK, 4], BF16, (window_at + 8.5, window_at + 12.5, factor_at, factor_at + 4)[g] if a == 0 else factor_at + 8 + 4 * g)
                       for g in range(CHUNKS)] for a in range(PASSES)]
 
         zeros = kept("zeros", [P, P], F32)
@@ -97,8 +97,9 @@ def tile_list_proof_board_kernel(tc, tab_words, tab_scales, offs, w1_words, w1_s
         z_codes = [[kept("z_codes%d_%d" % (a, g), [P, BANK], U32) for g in range(CHUNKS)] for a in range(PASSES)]
         w2_grouped = [kept("w2_grouped%d" % a, [P, N, 4], BF16) for a in range(PASSES)]
         w2_codes = kept("w2_codes", [P, PASSES, N], U32)
-        pages = [kept("page0", [P, T2], F32), placed("page1", [P, T2], F32, 17), placed("page2", [P, T2], F32, window_at)]
-        released = [placed("released%d" % s, [P, T2], F32, window_at + 8 * (s + 1)) for s in range(2)]
+        pages = [kept("page0", [P, T2], F32), placed("page1", [P, T2], F32, window_at + 0.5),
+                 placed("page2", [P, T2], F32, window_at + 23.5)]
+        released = [placed("released%d" % s, [P, T2], F32, (13.5, slot_at[1] + 3)[s]) for s in range(2)]
 
         nc.vector.memset(table_scales[:].bitcast(I32), 0)
         nc.vector.memset(zeros[:], 0.0)
@@ -143,7 +144,8 @@ def tile_list_proof_board_kernel(tc, tab_words, tab_scales, offs, w1_words, w1_s
             nc.vector.tensor_copy(picked[1][:, BANK * half:BANK * (half + 1)],
                                   table[1][:].indirect(idx[:, 32 * half:32 * (half + 1)]))
         nc.vector.memset(pages[0][:].bitcast(I32), 0)
-        nc.gpsimd.memset(pages[1][:].bitcast(I32), 0)
+        for window in (released[0], pages[1], pages[2]):
+            nc.vector.memset(window[:].bitcast(I32), 0)
         nc.sync.dma_start(w1_rest[:].bitcast(I32), w1_by_partition[:, :, 2 * P * EARLY_TILES:].bitcast(I32))
 
         def load_board(i):
@@ -226,7 +228,6 @@ def tile_list_proof_board_kernel(tc, tab_words, tab_scales, offs, w1_words, w1_s
             apply_tanh(0, bank, c0, width)
             make_factor(0, c0, width, wgs_first if c0 < BANK else wgs_sb)
             place_scores(0, c0, width)
-        nc.gpsimd.memset(pages[2][:].bitcast(I32), 0)
         multiply(1)
         score(1)
         make_factor(1)
@@ -239,8 +240,6 @@ def tile_list_proof_board_kernel(tc, tab_words, tab_scales, offs, w1_words, w1_s
                 make_factor(i + 2)
             if i > 0:
                 place_scores(i, 0, S)
-            if 1 <= i <= 2:
-                nc.gpsimd.memset(released[i - 1][:].bitcast(I32), 0)
             if i + 2 < ROW_TILES:
                 load_board(i + 2)
             if i < PASSES:
@@ -260,7 +259,7 @@ def tile_list_proof_board_kernel(tc, tab_words, tab_scales, offs, w1_words, w1_s
         w2_planes = placed("w2_planes", [P, PASSES, N], U8, last_h_at + 2)
         y_sb = [placed("y%d" % j, [P, T2], F32, at) for j, at in enumerate((slot_at[2], factor_at + 16, slot_at[0], 80))]
         style_sb = [placed("style%d" % j, [P, M], F32, w2_at[j // 2] + 4 * (j % 2)) for j in range(OUT_TILES)]
-        wgo_sb = placed("wgo_sb", [P, M], F32, 8)
+        wgo_sb = placed("wgo_sb", [P, M], F32, window_at + 16.5)
         pulled = [placed("pulled%d" % s, [P, M], F32, factor_at + 4 * s) for s in range(2)]
         for j in range(OUT_TILES):
             nc.sync.dma_start(style_sb[j][:], style[P * j:P * (j + 1), :])
@@ -305,6 +304,8 @@ def tile_list_proof_board_kernel(tc, tab_words, tab_scales, offs, w1_words, w1_s
             for a in range(PASSES):
                 second_pass(0, g, a, bank, c0, width)
             empty_bank(0, g, bank, on_vector if c0 else on_scalar, c0, width)
+
+        nc.vector.memset(released[1][:].bitcast(I32), 0)
 
         def release(j):
             nc.vector.tensor_tensor(released[j % 2][:].indirect(idx4[:]), pulled[j % 2][:], wgo_sb[:], MULT)

@@ -68,6 +68,7 @@ def tile_list_proof_board_kernel(tc, tab_words, tab_scales, offs, w1_words, w1_s
         w2_at = (45, 62.5)
         factor_at = 120
         window_at = 144
+        codes_at = 176
         table = [placed("table0", [P, T], U32, window_at + 8), placed("table1", [P, T], U32, 24)]
         table_scales = placed("table_scales", [P, T], U8, 21)
         wgs_sb = placed("wgs_sb", [P, S], F32, window_at + 19.5)
@@ -94,12 +95,13 @@ def tile_list_proof_board_kernel(tc, tab_words, tab_scales, offs, w1_words, w1_s
         picked_rows = kept("picked_rows", [P, S], U8)
         picked_scales = kept("picked_scales", [P, PASSES, S], U8)
         w1_planes = kept("w1_planes", [P, PASSES, H], U8)
-        z_codes = [[kept("z_codes%d_%d" % (a, g), [P, BANK], U32) for g in range(CHUNKS)] for a in range(PASSES)]
+        z_codes = [[placed("z_codes%d_%d" % (a, g), [P, BANK], U32, codes_at + 4 * g + 2 * a) for g in range(CHUNKS)]
+                   for a in range(PASSES)]
         w2_grouped = [kept("w2_grouped%d" % a, [P, N, 4], BF16) for a in range(PASSES)]
         w2_codes = kept("w2_codes", [P, PASSES, N], U32)
         pages = [kept("page0", [P, T2], F32), placed("page1", [P, T2], F32, window_at + 0.5),
                  placed("page2", [P, T2], F32, window_at + 23.5)]
-        released = [placed("released%d" % s, [P, T2], F32, (13.5, slot_at[1] + 3)[s]) for s in range(2)]
+        released = [placed("released0", [P, T2], F32, 13.5), kept("released1", [P, T2], F32)]
 
         nc.vector.memset(table_scales[:].bitcast(I32), 0)
         nc.vector.memset(zeros[:], 0.0)
@@ -144,7 +146,7 @@ def tile_list_proof_board_kernel(tc, tab_words, tab_scales, offs, w1_words, w1_s
             nc.vector.tensor_copy(picked[1][:, BANK * half:BANK * (half + 1)],
                                   table[1][:].indirect(idx[:, 32 * half:32 * (half + 1)]))
         nc.vector.memset(pages[0][:].bitcast(I32), 0)
-        for window in (released[0], pages[1], pages[2]):
+        for window in (released[1], released[0], pages[1], pages[2]):
             nc.vector.memset(window[:].bitcast(I32), 0)
         nc.sync.dma_start(w1_rest[:].bitcast(I32), w1_by_partition[:, :, 2 * P * EARLY_TILES:].bitcast(I32))
 
@@ -260,7 +262,7 @@ def tile_list_proof_board_kernel(tc, tab_words, tab_scales, offs, w1_words, w1_s
         y_sb = [placed("y%d" % j, [P, T2], F32, at) for j, at in enumerate((slot_at[2], factor_at + 16, slot_at[0], 80))]
         style_sb = [placed("style%d" % j, [P, M], F32, w2_at[j // 2] + 4 * (j % 2)) for j in range(OUT_TILES)]
         wgo_sb = placed("wgo_sb", [P, M], F32, window_at + 16.5)
-        pulled = [placed("pulled%d" % s, [P, M], F32, factor_at + 4 * s) for s in range(2)]
+        pulled = [placed("pulled%d" % s, [P, M], F32, at) for s, at in enumerate((factor_at, codes_at + 8, codes_at + 12))]
         for j in range(OUT_TILES):
             nc.sync.dma_start(style_sb[j][:], style[P * j:P * (j + 1), :])
         nc.sync.dma_start(wgo_sb[:], wgo)
@@ -283,7 +285,7 @@ def tile_list_proof_board_kernel(tc, tab_words, tab_scales, offs, w1_words, w1_s
             copy(y_sb[j][:, BANK * g + c0:BANK * g + c0 + width], whole(bank)[:, 0:width])
 
         def pull(j):
-            nc.vector.tensor_tensor(pulled[j % 2][:], y_sb[j][:].indirect(idx3[:]), style_sb[j][:], SUBTRACT)
+            nc.vector.tensor_tensor(pulled[j % 3][:], y_sb[j][:].indirect(idx3[:]), style_sb[j][:], SUBTRACT)
 
         for a in range(PASSES):
             nc.vector.quantize_mx(out=w2_codes[:, a, :].bitcast(FP8X4), scales=w2_planes[:, a, :],
@@ -305,10 +307,8 @@ def tile_list_proof_board_kernel(tc, tab_words, tab_scales, offs, w1_words, w1_s
                 second_pass(0, g, a, bank, c0, width)
             empty_bank(0, g, bank, on_vector if c0 else on_scalar, c0, width)
 
-        nc.vector.memset(released[1][:].bitcast(I32), 0)
-
         def release(j):
-            nc.vector.tensor_tensor(released[j % 2][:].indirect(idx4[:]), pulled[j % 2][:], wgo_sb[:], MULT)
+            nc.vector.tensor_tensor(released[j % 2][:].indirect(idx4[:]), pulled[j % 3][:], wgo_sb[:], MULT)
             nc.sync.dma_start(out[P * j:P * (j + 1), :], released[j % 2][:])
 
         late_banks = back_banks + [mx_banks[1], s2]
@@ -319,7 +319,7 @@ def tile_list_proof_board_kernel(tc, tab_words, tab_scales, offs, w1_words, w1_s
                 for a in range(PASSES):
                     second_pass(j, g, a, late_banks[g])
                 empty_bank(j, g, late_banks[g], nc.scalar.copy)
+        for j in range(1, OUT_TILES):
             pull(j)
-            if j > 1:
-                release(j - 1)
-        release(OUT_TILES - 1)
+        for j in range(1, OUT_TILES):
+            release(j)

@@ -76,7 +76,7 @@ def tile_list_proof_board_kernel(tc, tab_words, tab_scales, offs, w1_words, w1_s
         w1_rest = placed("w1_rest", [P, PASSES, 2 * (H - P * EARLY_TILES)], U8, window_at + 16.5)
         picked = [placed("picked%d" % a, [P, S], U32, 112 + 4 * a) for a in range(PASSES)]
         factors = [placed("factor%d" % i, [P, S], F32,
-                          4 * i if i < HEAD_FACTORS else slot_at[(i - 2) % 4] + 4.5)
+                          (0, window_at + 24, 8)[i] if i < HEAD_FACTORS else slot_at[(i - 2) % 4] + 4.5)
                    for i in range(ROW_TILES)]
         h_sb = [placed("h%d" % i, [P, S], F32, w2_at[i] + 6 if i < 2 else slot_at[(i - 2) % 4]) for i in range(ROW_TILES)]
         board_sb = [placed("board%d" % i, [P, T2], F32, slot_at[i % 4]) for i in range(ROW_TILES)]
@@ -100,8 +100,8 @@ def tile_list_proof_board_kernel(tc, tab_words, tab_scales, offs, w1_words, w1_s
         w2_grouped = [kept("w2_grouped%d" % a, [P, N, 4], BF16) for a in range(PASSES)]
         w2_codes = kept("w2_codes", [P, PASSES, N], U32)
         pages = [kept("page0", [P, T2], F32), placed("page1", [P, T2], F32, window_at + 0.5),
-                 placed("page2", [P, T2], F32, window_at + 23.5)]
-        released = [placed("released0", [P, T2], F32, 13.5), kept("released1", [P, T2], F32)]
+                 placed("page2", [P, T2], F32, 0)]
+        released = [placed("released0", [P, T2], F32, 13.5), placed("released1", [P, T2], F32, window_at + 24)]
 
         nc.vector.memset(table_scales[:].bitcast(I32), 0)
         nc.vector.memset(zeros[:], 0.0)
@@ -123,18 +123,18 @@ def tile_list_proof_board_kernel(tc, tab_words, tab_scales, offs, w1_words, w1_s
         load_table(0)
         nc.scalar.activation(vector_rows[:], zeros[:], TANH)
         for q in range(4):
-            nc.scalar.dma_start(w1_planes[32 * q:32 * q + 4, :, :].bitcast(I32),
-                                w1_scales[:, 4 * q:4 * q + 4, :].rearrange("a r c -> r a c").bitcast(I32))
-        nc.scalar.dma_start(vector_rows[0:ROW_TILES, :], b1.rearrange("(i p) -> i p", p=P))
-        nc.scalar.dma_start(vector_rows[ROW_TILES:2 * ROW_TILES, :], gain.rearrange("(i p) -> i p", p=P))
+            nc.sync.dma_start(w1_planes[32 * q:32 * q + 4, :, :].bitcast(I32),
+                              w1_scales[:, 4 * q:4 * q + 4, :].rearrange("a r c -> r a c").bitcast(I32))
+        nc.sync.dma_start(vector_rows[0:ROW_TILES, :], b1.rearrange("(i p) -> i p", p=P))
+        nc.gpsimd.dma_start(vector_rows[ROW_TILES:2 * ROW_TILES, :], gain.rearrange("(i p) -> i p", p=P))
         nc.tensor.transpose(back_banks[0][:, 0, :], vector_rows[:], identity[:])
 
         nc.vector.tensor_copy(picked_rows[:], table_scales[:].indirect(idx[:]))
 
         def move_scales(a, q):
             first = 64 * a + 16 * q
-            nc.scalar.dma_start(picked_scales[32 * q:32 * q + 4, a, :].bitcast(I32),
-                                picked_rows[first:first + 16:4, :].bitcast(I32))
+            nc.sync.dma_start(picked_scales[32 * q:32 * q + 4, a, :].bitcast(I32),
+                              picked_rows[first:first + 16:4, :].bitcast(I32))
 
         move_scales(0, 0)
         load_table(1)
@@ -146,7 +146,7 @@ def tile_list_proof_board_kernel(tc, tab_words, tab_scales, offs, w1_words, w1_s
             nc.vector.tensor_copy(picked[1][:, BANK * half:BANK * (half + 1)],
                                   table[1][:].indirect(idx[:, 32 * half:32 * (half + 1)]))
         nc.vector.memset(pages[0][:].bitcast(I32), 0)
-        for window in (released[1], released[0], pages[1], pages[2]):
+        for window in (released[0], pages[1]):
             nc.vector.memset(window[:].bitcast(I32), 0)
         nc.sync.dma_start(w1_rest[:].bitcast(I32), w1_by_partition[:, :, 2 * P * EARLY_TILES:].bitcast(I32))
 
@@ -230,6 +230,7 @@ def tile_list_proof_board_kernel(tc, tab_words, tab_scales, offs, w1_words, w1_s
             apply_tanh(0, bank, c0, width)
             make_factor(0, c0, width, wgs_first if c0 < BANK else wgs_sb)
             place_scores(0, c0, width)
+        nc.gpsimd.memset(pages[2][:].bitcast(I32), 0)
         multiply(1)
         score(1)
         make_factor(1)
@@ -242,6 +243,8 @@ def tile_list_proof_board_kernel(tc, tab_words, tab_scales, offs, w1_words, w1_s
                 make_factor(i + 2)
             if i > 0:
                 place_scores(i, 0, S)
+            if i == 1:
+                nc.gpsimd.memset(released[1][:].bitcast(I32), 0)
             if i + 2 < ROW_TILES:
                 load_board(i + 2)
             if i < PASSES:

@@ -64,27 +64,29 @@ def tile_list_proof_board_kernel(tc, tab_words, tab_scales, offs, w1_words, w1_s
         def whole(bank):
             return bank[:].rearrange("p c t -> p (c t)")
 
-        slot_at = (25, 33.5, 54, 71.5)
-        w2_at = (45, 62.5)
-        factor_at = 120
-        window_at = 144
-        codes_at = 176
+        slot_at = (25, 37, 56, 73)
+        h_at = (23, 35, 56, 73)
+        w2_at = (47, 64)
+        turned_at = 81
+        factor_at = 121
+        window_at = 145
+        codes_at = 177
         table = [placed("table0", [P, T], U32, window_at + 8), placed("table1", [P, T], U32, 24)]
         table_scales = placed("table_scales", [P, T], U8, 21)
         wgs_sb = placed("wgs_sb", [P, S], F32, window_at + 19.5)
         w1_first = placed("w1_first", [P, PASSES, 2 * P * EARLY_TILES], U8, 12)
         w1_rest = placed("w1_rest", [P, PASSES, 2 * (H - P * EARLY_TILES)], U8, window_at + 16.5)
-        picked = [placed("picked%d" % a, [P, S], U32, 112 + 4 * a) for a in range(PASSES)]
+        picked = [placed("picked%d" % a, [P, S], U32, turned_at + 32 + 4 * a) for a in range(PASSES)]
         factors = [placed("factor%d" % i, [P, S], F32,
-                          (0, window_at + 24, 8)[i] if i < HEAD_FACTORS else slot_at[(i - 2) % 4] + 4.5)
+                          (0, window_at + 24, 8)[i] if i < HEAD_FACTORS else h_at[(i - 2) % 4] + 4)
                    for i in range(ROW_TILES)]
-        h_sb = [placed("h%d" % i, [P, S], F32, w2_at[i] + 6 if i < 2 else slot_at[(i - 2) % 4]) for i in range(ROW_TILES)]
+        h_sb = [placed("h%d" % i, [P, S], F32, w2_at[i] + 6 if i < 2 else h_at[(i - 2) % 4]) for i in range(ROW_TILES)]
         board_sb = [placed("board%d" % i, [P, T2], F32, slot_at[i % 4]) for i in range(ROW_TILES)]
-        page_identity = [placed("page_identity%d" % i, [P, P], F32, slot_at[i % 4] + 4) for i in range(ROW_TILES)]
+        page_identity = [placed("page_identity%d" % i, [P, P], F32, slot_at[i % 4]) for i in range(ROW_TILES)]
         w2_raw = [placed("w2_raw%d" % a, [P, 4, N], F32, w2_at[a]) for a in range(PASSES)]
-        turned = [[placed("turned%d_%d" % (a, g), [P, 2, BLOCKS, 2 * P], BF16, 80 + 16 * a + 4 * g) for g in range(CHUNKS)]
+        turned = [[placed("turned%d_%d" % (a, g), [P, 2, BLOCKS, 2 * P], BF16, turned_at + 16 * a + 4 * g) for g in range(CHUNKS)]
                   for a in range(PASSES)]
-        z_grouped = [[placed("z_grouped%d_%d" % (a, g), [P, BANK, 4], BF16, (window_at + 8.5, window_at + 12.5, factor_at, factor_at + 4)[g] if a == 0 else factor_at + 8 + 4 * g)
+        z_grouped = [[placed("z_grouped%d_%d" % (a, g), [P, BANK, 4], BF16, (slot_at[0] + 6, slot_at[1] + 6, slot_at[2] + 4, factor_at)[g] if a == 0 else factor_at + 8 + 4 * g)
                       for g in range(CHUNKS)] for a in range(PASSES)]
 
         zeros = kept("zeros", [P, P], F32)
@@ -194,7 +196,6 @@ def tile_list_proof_board_kernel(tc, tab_words, tab_scales, offs, w1_words, w1_s
                     t0 = BANK * g + P * c
                     nc.tensor.matmul(sum_banks[g][:, c, :], board_sb[i][:, t0:t0 + P], identity[:],
                                      start=(c == 0), stop=False, is_transpose=True)
-            nc.scalar.copy(page_identity[i][:], identity[:])
 
         def turn_page(i):
             a, place = divmod(i, TILES_PER_PASS)
@@ -207,14 +208,23 @@ def tile_list_proof_board_kernel(tc, tab_words, tab_scales, offs, w1_words, w1_s
                     turned[a][g][:, :, :, 64 * place:64 * (place + 1)].rearrange("t u c (w e) -> t u c w e", e=2),
                     sum_banks[g][:].rearrange("t c (w u e) -> t u c w e", u=2, e=2))
 
-        def turn_back(a, g, banks, copies):
+        def release_page(i):
+            nc.scalar.copy(page_identity[i][:], identity[:])
+
+        def turn_back_half(a, g, b, bank):
             words = turned[a][g][:].bitcast(F32)
+            for u in range(2):
+                for c in range(2):
+                    nc.tensor.transpose(bank[:, 2 * u + c, :], words[:, u, 2 * b + c, :], identity[:])
+
+        def group_half(a, g, b, bank, copy):
             grouped_words = z_grouped[a][g][:].bitcast(F32)
+            copy(grouped_words[:, 2 * P * b:2 * P * (b + 1), :], bank[:].rearrange("p (u c) t -> p (c t) u", u=2))
+
+        def turn_back(a, g, banks, copies):
             for b in range(2):
-                for u in range(2):
-                    for c in range(2):
-                        nc.tensor.transpose(banks[b][:, 2 * u + c, :], words[:, u, 2 * b + c, :], identity[:])
-                copies[b](grouped_words[:, 2 * P * b:2 * P * (b + 1), :], banks[b][:].rearrange("p (u c) t -> p (c t) u", u=2))
+                turn_back_half(a, g, b, banks[b])
+                group_half(a, g, b, banks[b], copies[b])
 
         def group_w2(a, piece):
             cols = slice(N // W2_PIECES * piece, N // W2_PIECES * (piece + 1))
@@ -236,11 +246,13 @@ def tile_list_proof_board_kernel(tc, tab_words, tab_scales, offs, w1_words, w1_s
         make_factor(1)
         multiply(2)
 
+        turn_board(0)
+        release_page(0)
+        make_factor(2)
+
         for i in range(ROW_TILES):
-            turn_board(i)
-            if i + 2 < ROW_TILES:
-                score(i + 2)
-                make_factor(i + 2)
+            g = i - (TILES_PER_PASS - 1)
+            turns_back = 0 <= g < CHUNKS
             if i > 0:
                 place_scores(i, 0, S)
             if i == 1:
@@ -250,19 +262,30 @@ def tile_list_proof_board_kernel(tc, tab_words, tab_scales, offs, w1_words, w1_s
             if i < PASSES:
                 load_w2(i)
             turn_page(i)
+            if turns_back:
+                for b in range(2):
+                    turn_back_half(0, g, b, back_banks[b])
+            if i < LAST:
+                turn_board(i + 1)
+            if i + 2 < ROW_TILES:
+                score(i + 2)
+            if i < LAST:
+                release_page(i + 1)
             if i + 3 < ROW_TILES:
                 multiply(i + 3)
-            if 1 <= i <= 4:
-                for piece in (2 * (i - 1), 2 * (i - 1) + 1):
-                    group_w2(*divmod(piece, W2_PIECES))
-            if TILES_PER_PASS <= i < TILES_PER_PASS + 2:
-                for g in range(2 * (i - TILES_PER_PASS), 2 * (i - TILES_PER_PASS + 1)):
-                    turn_back(0, g, back_banks, (nc.scalar.copy, nc.scalar.copy))
+            if turns_back:
+                for b in range(2):
+                    group_half(0, g, b, back_banks[b], nc.scalar.copy)
+            if i + 3 < ROW_TILES:
+                make_factor(i + 3)
+            if 1 <= i <= PASSES:
+                for piece in range(W2_PIECES):
+                    group_w2(i - 1, piece)
 
-        last_h_at = slot_at[(LAST - 2) % 4]
+        last_h_at = h_at[(LAST - 2) % 4]
         z_planes = [placed("z_planes0", [P, T2], U8, last_h_at), kept("z_planes1", [P, T2], U8)]
         w2_planes = placed("w2_planes", [P, PASSES, N], U8, last_h_at + 2)
-        y_sb = [placed("y%d" % j, [P, T2], F32, at) for j, at in enumerate((slot_at[2], factor_at + 16, slot_at[0], 80))]
+        y_sb = [placed("y%d" % j, [P, T2], F32, at) for j, at in enumerate((slot_at[2], factor_at + 16, slot_at[0], turned_at))]
         style_sb = [placed("style%d" % j, [P, M], F32, w2_at[j // 2] + 4 * (j % 2)) for j in range(OUT_TILES)]
         wgo_sb = placed("wgo_sb", [P, M], F32, window_at + 16.5)
         pulled = [placed("pulled%d" % s, [P, M], F32, at) for s, at in enumerate((factor_at, codes_at + 8, codes_at + 12))]

@@ -31,9 +31,9 @@ OUT_TILES = N // P
 PAGES = 3
 FIRST = 256
 HALF = BANK // 2
-HEAD_FACTORS = 3
 W2_PIECES = 4
 EARLY_TILES = 2
+SCALE_ROW = 96
 KB = 1024
 
 
@@ -72,14 +72,16 @@ def tile_list_proof_board_kernel(tc, tab_words, tab_scales, offs, w1_words, w1_s
         window_at = 145
         codes_at = 177
         table = [placed("table0", [P, T], U32, window_at + 8), placed("table1", [P, T], U32, 24)]
-        table_scales = placed("table_scales", [P, T], U8, 21)
-        wgs_sb = placed("wgs_sb", [P, S], F32, window_at + 19.5)
+        table_scales = placed("table_scales", [P, T], U8, 20.5)
+        wgs_halves = [kept("wgs_half0", [P, BANK], F32), placed("wgs_half1", [P, BANK], F32, 21)]
         w1_first = placed("w1_first", [P, PASSES, 2 * P * EARLY_TILES], U8, 12)
         w1_rest = placed("w1_rest", [P, PASSES, 2 * (H - P * EARLY_TILES)], U8, window_at + 16.5)
         picked = [placed("picked%d" % a, [P, S], U32, turned_at + 32 + 4 * a) for a in range(PASSES)]
-        factors = [placed("factor%d" % i, [P, S], F32,
-                          (0, window_at + 24, 8)[i] if i < HEAD_FACTORS else h_at[(i - 2) % 4] + 4)
-                   for i in range(ROW_TILES)]
+        first_pieces = ((0, FIRST), (FIRST, BANK - FIRST), (BANK, BANK))
+        first_factors = [placed("first_factor%d" % c0, [P, width], F32, at)
+                         for (c0, width), at in zip(first_pieces, (8, window_at + 23.5, 6.5))]
+        factors = [None] + [placed("factor%d" % i, [P, S], F32, window_at + 24 if i == 1 else h_at[(i - 2) % 4] + 4)
+                            for i in range(1, ROW_TILES)]
         h_sb = [placed("h%d" % i, [P, S], F32, w2_at[i] + 6 if i < 2 else h_at[(i - 2) % 4]) for i in range(ROW_TILES)]
         board_sb = [placed("board%d" % i, [P, T2], F32, slot_at[i % 4]) for i in range(ROW_TILES)]
         page_identity = [placed("page_identity%d" % i, [P, P], F32, slot_at[i % 4]) for i in range(ROW_TILES)]
@@ -92,7 +94,6 @@ def tile_list_proof_board_kernel(tc, tab_words, tab_scales, offs, w1_words, w1_s
         zeros = kept("zeros", [P, P], F32)
         identity = kept("identity", [P, P], F32)
         vector_cols = kept("vector_cols", [P, 2 * ROW_TILES], F32)
-        wgs_first = kept("wgs_first", [P, BANK], F32)
         vector_rows = kept("vector_rows", [P, P], F32)
         picked_rows = kept("picked_rows", [P, S], U8)
         picked_scales = kept("picked_scales", [P, PASSES, S], U8)
@@ -101,13 +102,13 @@ def tile_list_proof_board_kernel(tc, tab_words, tab_scales, offs, w1_words, w1_s
                    for a in range(PASSES)]
         w2_grouped = [kept("w2_grouped%d" % a, [P, N, 4], BF16) for a in range(PASSES)]
         w2_codes = kept("w2_codes", [P, PASSES, N], U32)
-        pages = [kept("page0", [P, T2], F32), placed("page1", [P, T2], F32, window_at + 0.5),
+        pages = [placed("page0", [P, T2], F32, 13), placed("page1", [P, T2], F32, window_at + 0.5),
                  placed("page2", [P, T2], F32, 0)]
-        released = [placed("released0", [P, T2], F32, 13.5), placed("released1", [P, T2], F32, window_at + 24)]
+        released = [placed("released0", [P, T2], F32, window_at + 9), placed("released1", [P, T2], F32, window_at + 24)]
 
-        nc.vector.memset(table_scales[:].bitcast(I32), 0)
-        nc.vector.memset(zeros[:], 0.0)
         nc.vector.memset(w1_planes[:].rearrange("p a c -> p (a c)").bitcast(I32), 0)
+        nc.vector.memset(zeros[:], 0.0)
+        nc.vector.memset(table_scales[0:SCALE_ROW, :].bitcast(I32), 0)
         nc.vector.memset(picked_scales[:].rearrange("p a c -> p (a c)").bitcast(I32), 0)
         make_identity(nc, identity[:])
 
@@ -115,40 +116,39 @@ def tile_list_proof_board_kernel(tc, tab_words, tab_scales, offs, w1_words, w1_s
             nc.sync.dma_start(table[a][:].bitcast(I32), tab_words[a].rearrange("p t i -> p (t i)").bitcast(I32))
 
         w1_by_partition = w1_words.rearrange("a p c -> p a c")
+        nc.sync.dma_start(table_scales[SCALE_ROW:P, :].bitcast(I32), tab_scales.rearrange("a q t -> (a q) t").bitcast(I32))
         nc.sync.dma_start(idx[:], offs)
         nc.sync.dma_start(idx2[:], offs2)
         nc.sync.dma_start(idx3[:], offs3)
         nc.sync.dma_start(idx4[:], offs4)
         nc.sync.dma_start(w1_first[:].bitcast(I32), w1_by_partition[:, :, 0:2 * P * EARLY_TILES].bitcast(I32))
-        nc.sync.dma_start(wgs_first[:], wgs[:, 0:BANK])
-        nc.sync.dma_start(table_scales[0:P:4, :].bitcast(I32), tab_scales.rearrange("a q t -> (a q) t").bitcast(I32))
+        nc.sync.dma_start(wgs_halves[0][:], wgs[:, 0:BANK])
         load_table(0)
         nc.scalar.activation(vector_rows[:], zeros[:], TANH)
         for q in range(4):
             nc.sync.dma_start(w1_planes[32 * q:32 * q + 4, :, :].bitcast(I32),
                               w1_scales[:, 4 * q:4 * q + 4, :].rearrange("a r c -> r a c").bitcast(I32))
-        nc.sync.dma_start(vector_rows[0:ROW_TILES, :], b1.rearrange("(i p) -> i p", p=P))
+        nc.gpsimd.dma_start(vector_rows[0:ROW_TILES, :], b1.rearrange("(i p) -> i p", p=P))
         nc.gpsimd.dma_start(vector_rows[ROW_TILES:2 * ROW_TILES, :], gain.rearrange("(i p) -> i p", p=P))
         nc.tensor.transpose(back_banks[0][:, 0, :], vector_rows[:], identity[:])
 
         nc.vector.tensor_copy(picked_rows[:], table_scales[:].indirect(idx[:]))
 
         def move_scales(a, q):
-            first = 64 * a + 16 * q
+            first = SCALE_ROW + 16 * a + 4 * q
             nc.sync.dma_start(picked_scales[32 * q:32 * q + 4, a, :].bitcast(I32),
-                              picked_rows[first:first + 16:4, :].bitcast(I32))
+                              picked_rows[first:first + 4, :].bitcast(I32))
 
-        move_scales(0, 0)
-        load_table(1)
-        for m in range(1, 8):
+        for m in range(8):
+            if m == 2:
+                load_table(1)
             move_scales(*divmod(m, 4))
+        nc.sync.dma_start(wgs_halves[1][:], wgs[:, BANK:S])
         nc.scalar.copy(vector_cols[:], back_banks[0][:, 0, 0:2 * ROW_TILES])
         nc.vector.tensor_copy(picked[0][:], table[0][:].indirect(idx[:]))
-        for half in range(2):
-            nc.vector.tensor_copy(picked[1][:, BANK * half:BANK * (half + 1)],
-                                  table[1][:].indirect(idx[:, 32 * half:32 * (half + 1)]))
-        nc.vector.memset(pages[0][:].bitcast(I32), 0)
-        for window in (released[0], pages[1]):
+        for c0, c1 in ((0, FIRST), (FIRST, S)):
+            nc.vector.tensor_copy(picked[1][:, c0:c1], table[1][:].indirect(idx[:, c0 // 16:c1 // 16]))
+        for window in pages[0:2]:
             nc.vector.memset(window[:].bitcast(I32), 0)
         nc.sync.dma_start(w1_rest[:].bitcast(I32), w1_by_partition[:, :, 2 * P * EARLY_TILES:].bitcast(I32))
 
@@ -158,9 +158,13 @@ def tile_list_proof_board_kernel(tc, tab_words, tab_scales, offs, w1_words, w1_s
         def load_w2(a):
             nc.sync.dma_start(w2_raw[a][:], w2[512 * a:512 * (a + 1), :].rearrange("(p j) n -> p j n", j=4))
 
-        def make_factor(i, c0=0, width=S, weights=wgs_sb):
-            nc.scalar.activation(factors[i][:, c0:c0 + width], weights[:, c0:c0 + width], COPY,
+        def make_factor(i, factor, weights):
+            nc.scalar.activation(factor, weights, COPY,
                                  scale=vector_cols[:, ROW_TILES + i:ROW_TILES + i + 1])
+
+        def make_factors(i):
+            for half in range(2):
+                make_factor(i, factors[i][:, BANK * half:BANK * (half + 1)], wgs_halves[half][:])
 
         def first_product(i, bank, c0, width, group):
             for g0 in range(0, width, group):
@@ -186,9 +190,9 @@ def tile_list_proof_board_kernel(tc, tab_words, tab_scales, offs, w1_words, w1_s
             for half in range(2):
                 apply_tanh(i, mx_banks[half], BANK * half, BANK)
 
-        def place_scores(i, c0, width):
+        def place_scores(i, c0, width, factor):
             nc.vector.tensor_tensor(pages[i % PAGES][:].indirect(idx2[:, c0 // 16:(c0 + width) // 16]),
-                                    h_sb[i][:, c0:c0 + width], factors[i][:, c0:c0 + width], MULT)
+                                    h_sb[i][:, c0:c0 + width], factor, MULT)
 
         def turn_board(i):
             for g in range(CHUNKS):
@@ -231,30 +235,29 @@ def tile_list_proof_board_kernel(tc, tab_words, tab_scales, offs, w1_words, w1_s
             nc.scalar.copy(w2_grouped[a][:, cols, :].rearrange("p (c k) j -> p c j k", k=4),
                            w2_raw[a][:, :, cols].rearrange("p j (c k) -> p c j k", k=4))
 
-        nc.sync.dma_start(wgs_sb[:], wgs)
         for i in range(2):
             load_board(i)
-        for bank, c0, width, group in ((mx_banks[0], 0, FIRST, P), (back_banks[1], FIRST, BANK - FIRST, P),
-                                       (mx_banks[1], BANK, BANK, BANK)):
+        for (c0, width), factor, bank, group in zip(first_pieces, first_factors, (mx_banks[0], back_banks[1], mx_banks[1]),
+                                                    (P, P, BANK)):
             first_product(0, bank, c0, width, group)
             apply_tanh(0, bank, c0, width)
-            make_factor(0, c0, width, wgs_first if c0 < BANK else wgs_sb)
-            place_scores(0, c0, width)
+            make_factor(0, factor[:], wgs_halves[c0 // BANK][:, c0 % BANK:c0 % BANK + width])
+            place_scores(0, c0, width, factor[:])
         nc.gpsimd.memset(pages[2][:].bitcast(I32), 0)
         multiply(1)
         score(1)
-        make_factor(1)
+        make_factors(1)
         multiply(2)
 
         turn_board(0)
         release_page(0)
-        make_factor(2)
+        make_factors(2)
 
         for i in range(ROW_TILES):
             g = i - (TILES_PER_PASS - 1)
             turns_back = 0 <= g < CHUNKS
             if i > 0:
-                place_scores(i, 0, S)
+                place_scores(i, 0, S, factors[i][:])
             if i == 1:
                 nc.gpsimd.memset(released[1][:].bitcast(I32), 0)
             if i + 2 < ROW_TILES:
@@ -273,11 +276,13 @@ def tile_list_proof_board_kernel(tc, tab_words, tab_scales, offs, w1_words, w1_s
                 release_page(i + 1)
             if i + 3 < ROW_TILES:
                 multiply(i + 3)
+            if i + 3 == LAST:
+                nc.gpsimd.memset(released[0][:].bitcast(I32), 0)
             if turns_back:
                 for b in range(2):
                     group_half(0, g, b, back_banks[b], nc.scalar.copy)
             if i + 3 < ROW_TILES:
-                make_factor(i + 3)
+                make_factors(i + 3)
             if 1 <= i <= PASSES:
                 for piece in range(W2_PIECES):
                     group_w2(i - 1, piece)
@@ -287,7 +292,7 @@ def tile_list_proof_board_kernel(tc, tab_words, tab_scales, offs, w1_words, w1_s
         w2_planes = placed("w2_planes", [P, PASSES, N], U8, last_h_at + 2)
         y_sb = [placed("y%d" % j, [P, T2], F32, at) for j, at in enumerate((slot_at[2], factor_at + 16, slot_at[0], turned_at))]
         style_sb = [placed("style%d" % j, [P, M], F32, w2_at[j // 2] + 4 * (j % 2)) for j in range(OUT_TILES)]
-        wgo_sb = placed("wgo_sb", [P, M], F32, window_at + 16.5)
+        wgo_sb = placed("wgo_sb", [P, M], F32, window_at + 17.5)
         pulled = [placed("pulled%d" % s, [P, M], F32, at) for s, at in enumerate((factor_at, codes_at + 8, codes_at + 12))]
         for j in range(OUT_TILES):
             nc.sync.dma_start(style_sb[j][:], style[P * j:P * (j + 1), :])

@@ -106,6 +106,7 @@ def tile_list_proof_board_kernel(tc, tab_words, tab_scales, offs, w1_words, w1_s
                  placed("page2", [P, T2], F32, 0)]
         released = [placed("released0", [P, T2], F32, window_at + 9), placed("released1", [P, T2], F32, window_at + 24)]
 
+        nc.vector.memset(vector_rows[0:64, :], 0.0)
         nc.vector.memset(w1_planes[:].rearrange("p a c -> p (a c)").bitcast(I32), 0)
         nc.vector.memset(zeros[:], 0.0)
         nc.vector.memset(table_scales[0:SCALE_ROW, :].bitcast(I32), 0)
@@ -116,7 +117,7 @@ def tile_list_proof_board_kernel(tc, tab_words, tab_scales, offs, w1_words, w1_s
             nc.sync.dma_start(table[a][:].bitcast(I32), tab_words[a].rearrange("p t i -> p (t i)").bitcast(I32))
 
         w1_by_partition = w1_words.rearrange("a p c -> p a c")
-        nc.sync.dma_start(table_scales[SCALE_ROW:P, :].bitcast(I32), tab_scales.rearrange("a q t -> (a q) t").bitcast(I32))
+        nc.sync.dma_start(table_scales[SCALE_ROW:P, :].bitcast(I32), tab_scales.rearrange("a q t -> q a t").bitcast(I32))
         nc.sync.dma_start(idx[:], offs)
         nc.sync.dma_start(idx2[:], offs2)
         nc.sync.dma_start(idx3[:], offs3)
@@ -124,25 +125,24 @@ def tile_list_proof_board_kernel(tc, tab_words, tab_scales, offs, w1_words, w1_s
         nc.sync.dma_start(w1_first[:].bitcast(I32), w1_by_partition[:, :, 0:2 * P * EARLY_TILES].bitcast(I32))
         nc.sync.dma_start(wgs_halves[0][:], wgs[:, 0:BANK])
         load_table(0)
-        nc.scalar.activation(vector_rows[:], zeros[:], TANH)
+        nc.sync.dma_start(vector_rows[0:ROW_TILES, :], b1.rearrange("(i p) -> i p", p=P))
+        nc.sync.dma_start(vector_rows[ROW_TILES:2 * ROW_TILES, :], gain.rearrange("(i p) -> i p", p=P))
+        nc.scalar.activation(vector_rows[64:P, :], zeros[64:P, :], TANH)
         for q in range(4):
             nc.sync.dma_start(w1_planes[32 * q:32 * q + 4, :, :].bitcast(I32),
                               w1_scales[:, 4 * q:4 * q + 4, :].rearrange("a r c -> r a c").bitcast(I32))
-        nc.gpsimd.dma_start(vector_rows[0:ROW_TILES, :], b1.rearrange("(i p) -> i p", p=P))
-        nc.gpsimd.dma_start(vector_rows[ROW_TILES:2 * ROW_TILES, :], gain.rearrange("(i p) -> i p", p=P))
         nc.tensor.transpose(back_banks[0][:, 0, :], vector_rows[:], identity[:])
 
         nc.vector.tensor_copy(picked_rows[:], table_scales[:].indirect(idx[:]))
 
-        def move_scales(a, q):
-            first = SCALE_ROW + 16 * a + 4 * q
-            nc.sync.dma_start(picked_scales[32 * q:32 * q + 4, a, :].bitcast(I32),
-                              picked_rows[first:first + 4, :].bitcast(I32))
+        def move_scales(q):
+            first = SCALE_ROW + 8 * q
+            nc.sync.dma_start(picked_scales[32 * q:32 * q + 4, :, :].bitcast(I32),
+                              picked_rows[first:first + 8, :].bitcast(I32))
 
-        for m in range(8):
-            if m == 2:
-                load_table(1)
-            move_scales(*divmod(m, 4))
+        load_table(1)
+        for q in range(4):
+            move_scales(q)
         nc.sync.dma_start(wgs_halves[1][:], wgs[:, BANK:S])
         nc.scalar.copy(vector_cols[:], back_banks[0][:, 0, 0:2 * ROW_TILES])
         nc.vector.tensor_copy(picked[0][:], table[0][:].indirect(idx[:]))

@@ -31,8 +31,7 @@ OUT_TILES = N // P
 PAGES = 3
 FIRST = 256
 HALF = BANK // 2
-W2_PIECES = 4
-EARLY_TILES = 2
+W2_TILES = (1, 2, 4, 5)
 SCALE_ROW = 96
 KB = 1024
 
@@ -71,18 +70,22 @@ def tile_list_proof_board_kernel(tc, tab_words, tab_scales, offs, w1_words, w1_s
         factor_at = 121
         window_at = 145
         codes_at = 177
-        table = [placed("table0", [P, T], U32, window_at + 8), placed("table1", [P, T], U32, 24)]
+        table = [placed("table0", [P, T], U32, window_at + 8), placed("table1", [P, T], U32, 24.25)]
         table_scales = placed("table_scales", [P, T], U8, 20.5)
-        wgs_halves = [kept("wgs_half0", [P, BANK], F32), placed("wgs_half1", [P, BANK], F32, 21)]
-        w1_first = placed("w1_first", [P, PASSES, 2 * P * EARLY_TILES], U8, 12)
-        w1_rest = placed("w1_rest", [P, PASSES, 2 * (H - P * EARLY_TILES)], U8, window_at + 16.5)
+        wgs_first = kept("wgs_first", [P, FIRST], F32)
+        wgs_next = placed("wgs_next", [P, S - FIRST], F32, 21.0625)
+        wgs_sb = placed("wgs_sb", [P, S], F32, window_at + 9)
+        w1_parts = [(first, placed("w1_part%d" % first, [P, PASSES, 2 * P * tiles], U8, at))
+                    for first, tiles, at in ((0, 1, 20.5625), (1, 3, window_at + 15), (4, 1, window_at + 18.5),
+                                             (5, 1, window_at + 21), (6, 2, window_at + 17.5))]
         picked = [placed("picked%d" % a, [P, S], U32, turned_at + 32 + 4 * a) for a in range(PASSES)]
         first_pieces = ((0, FIRST), (FIRST, BANK - FIRST), (BANK, BANK))
         first_factors = [placed("first_factor%d" % c0, [P, width], F32, at)
-                         for (c0, width), at in zip(first_pieces, (8, window_at + 23.5, 6.5))]
+                         for (c0, width), at in zip(first_pieces, (window_at + 23.5, 7.5, w2_at[0] + 7.5))]
         factors = [None] + [placed("factor%d" % i, [P, S], F32, window_at + 24 if i == 1 else h_at[(i - 2) % 4] + 4)
                             for i in range(1, ROW_TILES)]
-        h_sb = [placed("h%d" % i, [P, S], F32, w2_at[i] + 6 if i < 2 else h_at[(i - 2) % 4]) for i in range(ROW_TILES)]
+        first_h = [placed("first_h%d" % c0, [P, width], F32, at) for (c0, width), at in zip(first_pieces, (9, 21.0625, 22.0625))]
+        h_sb = [None] + [placed("h%d" % i, [P, S], F32, w2_at[1] + 6 if i == 1 else h_at[(i - 2) % 4]) for i in range(1, ROW_TILES)]
         board_sb = [placed("board%d" % i, [P, T2], F32, slot_at[i % 4]) for i in range(ROW_TILES)]
         page_identity = [placed("page_identity%d" % i, [P, P], F32, slot_at[i % 4]) for i in range(ROW_TILES)]
         w2_raw = [placed("w2_raw%d" % a, [P, 4, N], F32, w2_at[a]) for a in range(PASSES)]
@@ -97,17 +100,18 @@ def tile_list_proof_board_kernel(tc, tab_words, tab_scales, offs, w1_words, w1_s
         vector_rows = kept("vector_rows", [P, P], F32)
         picked_rows = kept("picked_rows", [P, S], U8)
         picked_scales = kept("picked_scales", [P, PASSES, S], U8)
-        w1_planes = kept("w1_planes", [P, PASSES, H], U8)
+        w1_planes = [kept("w1_planes0", [P, PASSES, P], U8), placed("w1_planes1", [P, PASSES, H - P], U8, window_at + 13)]
         z_codes = [[placed("z_codes%d_%d" % (a, g), [P, BANK], U32, codes_at + 4 * g + 2 * a) for g in range(CHUNKS)]
                    for a in range(PASSES)]
-        w2_grouped = [kept("w2_grouped%d" % a, [P, N, 4], BF16) for a in range(PASSES)]
+        w2_grouped = [placed("w2_grouped%d" % part, [P, HALF, 4], BF16, at)
+                      for part, at in enumerate((window_at + 18.75, window_at + 21.25, turned_at + 4, turned_at + 8))]
         w2_codes = kept("w2_codes", [P, PASSES, N], U32)
-        pages = [placed("page0", [P, T2], F32, 13), placed("page1", [P, T2], F32, window_at + 0.5),
+        pages = [placed("page0", [P, T2], F32, 12.5625), placed("page1", [P, T2], F32, window_at + 0.5),
                  placed("page2", [P, T2], F32, 0)]
         released = [placed("released0", [P, T2], F32, window_at + 9), placed("released1", [P, T2], F32, window_at + 24)]
 
         nc.vector.memset(vector_rows[0:64, :], 0.0)
-        nc.vector.memset(w1_planes[:].rearrange("p a c -> p (a c)").bitcast(I32), 0)
+        nc.vector.memset(w1_planes[0][:].rearrange("p a c -> p (a c)").bitcast(I32), 0)
         nc.vector.memset(zeros[:], 0.0)
         nc.vector.memset(table_scales[0:SCALE_ROW, :].bitcast(I32), 0)
         nc.vector.memset(picked_scales[:].rearrange("p a c -> p (a c)").bitcast(I32), 0)
@@ -122,15 +126,21 @@ def tile_list_proof_board_kernel(tc, tab_words, tab_scales, offs, w1_words, w1_s
         nc.sync.dma_start(idx2[:], offs2)
         nc.sync.dma_start(idx3[:], offs3)
         nc.sync.dma_start(idx4[:], offs4)
-        nc.sync.dma_start(w1_first[:].bitcast(I32), w1_by_partition[:, :, 0:2 * P * EARLY_TILES].bitcast(I32))
-        nc.sync.dma_start(wgs_halves[0][:], wgs[:, 0:BANK])
+
+        def load_w1(first, part):
+            nc.sync.dma_start(part[:].bitcast(I32), w1_by_partition[:, :, 2 * P * first:2 * P * first + part.shape[2]].bitcast(I32))
+
+        def load_w1_scales(planes, c0, c1):
+            for q in range(4):
+                nc.sync.dma_start(planes[32 * q:32 * q + 4, :, :].bitcast(I32),
+                                  w1_scales[:, 4 * q:4 * q + 4, c0:c1].rearrange("a r c -> r a c").bitcast(I32))
+
+        nc.sync.dma_start(wgs_first[:], wgs[:, 0:FIRST])
         load_table(0)
         nc.sync.dma_start(vector_rows[0:ROW_TILES, :], b1.rearrange("(i p) -> i p", p=P))
         nc.sync.dma_start(vector_rows[ROW_TILES:2 * ROW_TILES, :], gain.rearrange("(i p) -> i p", p=P))
         nc.scalar.activation(vector_rows[64:P, :], zeros[64:P, :], TANH)
-        for q in range(4):
-            nc.sync.dma_start(w1_planes[32 * q:32 * q + 4, :, :].bitcast(I32),
-                              w1_scales[:, 4 * q:4 * q + 4, :].rearrange("a r c -> r a c").bitcast(I32))
+        load_w1_scales(w1_planes[0], 0, P)
         nc.tensor.transpose(back_banks[0][:, 0, :], vector_rows[:], identity[:])
 
         nc.vector.tensor_copy(picked_rows[:], table_scales[:].indirect(idx[:]))
@@ -141,16 +151,22 @@ def tile_list_proof_board_kernel(tc, tab_words, tab_scales, offs, w1_words, w1_s
                               picked_rows[first:first + 8, :].bitcast(I32))
 
         load_table(1)
+        load_w1(*w1_parts[0])
         for q in range(4):
             move_scales(q)
-        nc.sync.dma_start(wgs_halves[1][:], wgs[:, BANK:S])
+        nc.sync.dma_start(wgs_next[:], wgs[:, FIRST:S])
         nc.scalar.copy(vector_cols[:], back_banks[0][:, 0, 0:2 * ROW_TILES])
         nc.vector.tensor_copy(picked[0][:], table[0][:].indirect(idx[:]))
         for c0, c1 in ((0, FIRST), (FIRST, S)):
             nc.vector.tensor_copy(picked[1][:, c0:c1], table[1][:].indirect(idx[:, c0 // 16:c1 // 16]))
         for window in pages[0:2]:
             nc.vector.memset(window[:].bitcast(I32), 0)
-        nc.sync.dma_start(w1_rest[:].bitcast(I32), w1_by_partition[:, :, 2 * P * EARLY_TILES:].bitcast(I32))
+        nc.vector.memset(w1_planes[1][:].rearrange("p a c -> p (a c)").bitcast(I32), 0)
+        load_w1_scales(w1_planes[1], P, H)
+        load_w1(*w1_parts[1])
+        nc.sync.dma_start(wgs_sb[:], wgs)
+        for first, part in w1_parts[2:]:
+            load_w1(first, part)
 
         def load_board(i):
             nc.sync.dma_start(board_sb[i][:], board[P * i:P * (i + 1), :])
@@ -163,24 +179,24 @@ def tile_list_proof_board_kernel(tc, tab_words, tab_scales, offs, w1_words, w1_s
                                  scale=vector_cols[:, ROW_TILES + i:ROW_TILES + i + 1])
 
         def make_factors(i):
-            for half in range(2):
-                make_factor(i, factors[i][:, BANK * half:BANK * (half + 1)], wgs_halves[half][:])
+            make_factor(i, factors[i][:], wgs_sb[:])
 
         def first_product(i, bank, c0, width, group):
             for g0 in range(0, width, group):
                 cols = slice(c0 + g0, c0 + g0 + group)
-                codes, tile_at = (w1_first, i) if i < EARLY_TILES else (w1_rest, i - EARLY_TILES)
+                first, codes = [entry for entry in w1_parts if entry[0] <= i][-1]
+                tile_at = i - first
                 for a in range(PASSES):
                     nc.tensor.matmul_mx(
                         out=whole(bank)[:, g0:g0 + group],
                         lhsT=codes[:, a, 2 * P * tile_at:2 * P * (tile_at + 1)].bitcast(FP4X4),
-                        lhsT_scale=w1_planes[:, a, P * i:P * (i + 1)],
+                        lhsT_scale=w1_planes[0][:, a, :] if i == 0 else w1_planes[1][:, a, P * (i - 1):P * i],
                         rhs=picked[a][:, cols].bitcast(FP8X4),
                         rhs_scale=picked_scales[:, a, cols],
                         start=(a == 0), stop=(a == PASSES - 1))
 
-        def apply_tanh(i, bank, c0, width):
-            nc.scalar.activation(h_sb[i][:, c0:c0 + width], whole(bank)[:, 0:width], TANH, bias=vector_cols[:, i:i + 1])
+        def apply_tanh(i, bank, h, width):
+            nc.scalar.activation(h, whole(bank)[:, 0:width], TANH, bias=vector_cols[:, i:i + 1])
 
         def multiply(i):
             for half in range(2):
@@ -188,11 +204,11 @@ def tile_list_proof_board_kernel(tc, tab_words, tab_scales, offs, w1_words, w1_s
 
         def score(i):
             for half in range(2):
-                apply_tanh(i, mx_banks[half], BANK * half, BANK)
+                apply_tanh(i, mx_banks[half], h_sb[i][:, BANK * half:BANK * (half + 1)], BANK)
 
-        def place_scores(i, c0, width, factor):
+        def place_scores(i, c0, width, h, factor):
             nc.vector.tensor_tensor(pages[i % PAGES][:].indirect(idx2[:, c0 // 16:(c0 + width) // 16]),
-                                    h_sb[i][:, c0:c0 + width], factor, MULT)
+                                    h, factor, MULT)
 
         def turn_board(i):
             for g in range(CHUNKS):
@@ -230,19 +246,22 @@ def tile_list_proof_board_kernel(tc, tab_words, tab_scales, offs, w1_words, w1_s
                 turn_back_half(a, g, b, banks[b])
                 group_half(a, g, b, banks[b], copies[b])
 
-        def group_w2(a, piece):
-            cols = slice(N // W2_PIECES * piece, N // W2_PIECES * (piece + 1))
-            nc.scalar.copy(w2_grouped[a][:, cols, :].rearrange("p (c k) j -> p c j k", k=4),
-                           w2_raw[a][:, :, cols].rearrange("p j (c k) -> p c j k", k=4))
+        def group_w2(part):
+            raw, first = w2_raw[part // 2], HALF * (part % 2)
+            for c0 in range(0, HALF, P):
+                nc.scalar.copy(w2_grouped[part][:, c0:c0 + P, :].rearrange("p (c k) j -> p c j k", k=4),
+                               raw[:, :, first + c0:first + c0 + P].rearrange("p j (c k) -> p c j k", k=4))
 
         for i in range(2):
             load_board(i)
-        for (c0, width), factor, bank, group in zip(first_pieces, first_factors, (mx_banks[0], back_banks[1], mx_banks[1]),
-                                                    (P, P, BANK)):
+        make_factor(0, first_factors[0][:], wgs_first[:])
+        for (c0, width), factor in zip(first_pieces[1:], first_factors[1:]):
+            make_factor(0, factor[:], wgs_next[:, c0 - FIRST:c0 - FIRST + width])
+        for (c0, width), h, factor, bank, group in zip(first_pieces, first_h, first_factors,
+                                                       (mx_banks[0], back_banks[1], mx_banks[1]), (P, P, BANK)):
             first_product(0, bank, c0, width, group)
-            apply_tanh(0, bank, c0, width)
-            make_factor(0, factor[:], wgs_halves[c0 // BANK][:, c0 % BANK:c0 % BANK + width])
-            place_scores(0, c0, width, factor[:])
+            apply_tanh(0, bank, h[:], width)
+            place_scores(0, c0, width, h[:], factor[:])
         nc.gpsimd.memset(pages[2][:].bitcast(I32), 0)
         multiply(1)
         score(1)
@@ -257,11 +276,11 @@ def tile_list_proof_board_kernel(tc, tab_words, tab_scales, offs, w1_words, w1_s
             g = i - (TILES_PER_PASS - 1)
             turns_back = 0 <= g < CHUNKS
             if i > 0:
-                place_scores(i, 0, S, factors[i][:])
-            if i == 1:
-                nc.gpsimd.memset(released[1][:].bitcast(I32), 0)
+                place_scores(i, 0, S, h_sb[i][:], factors[i][:])
             if i + 2 < ROW_TILES:
                 load_board(i + 2)
+            if i == 1:
+                nc.gpsimd.memset(released[1][:].bitcast(I32), 0)
             if i < PASSES:
                 load_w2(i)
             turn_page(i)
@@ -276,23 +295,22 @@ def tile_list_proof_board_kernel(tc, tab_words, tab_scales, offs, w1_words, w1_s
                 release_page(i + 1)
             if i + 3 < ROW_TILES:
                 multiply(i + 3)
-            if i + 3 == LAST:
-                nc.gpsimd.memset(released[0][:].bitcast(I32), 0)
             if turns_back:
                 for b in range(2):
                     group_half(0, g, b, back_banks[b], nc.scalar.copy)
             if i + 3 < ROW_TILES:
                 make_factors(i + 3)
-            if 1 <= i <= PASSES:
-                for piece in range(W2_PIECES):
-                    group_w2(i - 1, piece)
+            if i + 3 == LAST:
+                nc.gpsimd.memset(released[0][:].bitcast(I32), 0)
+            if i in W2_TILES:
+                group_w2(W2_TILES.index(i))
 
         last_h_at = h_at[(LAST - 2) % 4]
         z_planes = [placed("z_planes0", [P, T2], U8, last_h_at), kept("z_planes1", [P, T2], U8)]
         w2_planes = placed("w2_planes", [P, PASSES, N], U8, last_h_at + 2)
         y_sb = [placed("y%d" % j, [P, T2], F32, at) for j, at in enumerate((slot_at[2], factor_at + 16, slot_at[0], turned_at))]
         style_sb = [placed("style%d" % j, [P, M], F32, w2_at[j // 2] + 4 * (j % 2)) for j in range(OUT_TILES)]
-        wgo_sb = placed("wgo_sb", [P, M], F32, window_at + 17.5)
+        wgo_sb = placed("wgo_sb", [P, M], F32, turned_at + 32)
         pulled = [placed("pulled%d" % s, [P, M], F32, at) for s, at in enumerate((factor_at, codes_at + 8, codes_at + 12))]
         for j in range(OUT_TILES):
             nc.sync.dma_start(style_sb[j][:], style[P * j:P * (j + 1), :])
@@ -318,9 +336,10 @@ def tile_list_proof_board_kernel(tc, tab_words, tab_scales, offs, w1_words, w1_s
         def pull(j):
             nc.vector.tensor_tensor(pulled[j % 3][:], y_sb[j][:].indirect(idx3[:]), style_sb[j][:], SUBTRACT)
 
-        for a in range(PASSES):
-            nc.vector.quantize_mx(out=w2_codes[:, a, :].bitcast(FP8X4), scales=w2_planes[:, a, :],
-                                  in_=w2_grouped[a][:].rearrange("p n j -> p (n j)"))
+        for part in range(4):
+            a, cols = part // 2, slice(HALF * (part % 2), HALF * (part % 2 + 1))
+            nc.vector.quantize_mx(out=w2_codes[:, a, cols].bitcast(FP8X4), scales=w2_planes[:, a, cols],
+                                  in_=w2_grouped[part][:].rearrange("p n j -> p (n j)"))
         end = CHUNKS - 1
         s0, s1, s2, s3 = sum_banks
         on_scalar, on_vector = nc.scalar.copy, nc.vector.tensor_copy

@@ -309,8 +309,9 @@ def tile_list_proof_board_kernel(tc, tab_words, tab_scales, offs, w1_words, w1_s
         z_planes = [placed("z_planes0", [P, T2], U8, last_h_at), kept("z_planes1", [P, T2], U8)]
         w2_planes = placed("w2_planes", [P, PASSES, N], U8, last_h_at + 2)
         y_sb = [placed("y%d" % j, [P, T2], F32, at) for j, at in enumerate((slot_at[2], factor_at + 16, slot_at[0], turned_at))]
-        style_sb = [placed("style%d" % j, [P, M], F32, w2_at[j // 2] + 4 * (j % 2)) for j in range(OUT_TILES)]
-        wgo_sb = placed("wgo_sb", [P, M], F32, turned_at + 32)
+        style_sb = [placed("style%d" % j, [P, M], F32, at)
+                    for j, at in enumerate((window_at + 0.5, window_at + 4.5, slot_at[3] - 3.75, slot_at[3] + 0.25))]
+        wgo_sb = placed("wgo_sb", [P, M], F32, last_h_at + 4)
         pulled = [placed("pulled%d" % s, [P, M], F32, at) for s, at in enumerate((factor_at, codes_at + 8, codes_at + 12))]
         for j in range(OUT_TILES):
             nc.sync.dma_start(style_sb[j][:], style[P * j:P * (j + 1), :])

@@ -31,8 +31,9 @@ OUT_TILES = N // P
 PAGES = 3
 FIRST = 256
 HALF = BANK // 2
-W2_TILES = (1, 2, 4, 5)
+W2_TILES = (1, 4, 2, 5)
 SCALE_ROW = 96
+EARLY_CHUNKS = 4
 KB = 1024
 
 
@@ -91,7 +92,7 @@ def tile_list_proof_board_kernel(tc, tab_words, tab_scales, offs, w1_words, w1_s
         w2_raw = [placed("w2_raw%d" % a, [P, 4, N], F32, w2_at[a]) for a in range(PASSES)]
         turned = [[placed("turned%d_%d" % (a, g), [P, 2, BLOCKS, 2 * P], BF16, turned_at + 16 * a + 4 * g) for g in range(CHUNKS)]
                   for a in range(PASSES)]
-        z_grouped = [[placed("z_grouped%d_%d" % (a, g), [P, BANK, 4], BF16, (slot_at[0] + 6, slot_at[1] + 6, slot_at[2] + 4, factor_at)[g] if a == 0 else factor_at + 8 + 4 * g)
+        z_grouped = [[placed("z_grouped%d_%d" % (a, g), [P, BANK, 4], BF16, (slot_at[0] + 6, factor_at, slot_at[1] + 6, slot_at[2] + 4)[g] if a == 0 else factor_at + 8 + 4 * g)
                       for g in range(CHUNKS)] for a in range(PASSES)]
 
         zeros = kept("zeros", [P, P], F32)
@@ -101,11 +102,23 @@ def tile_list_proof_board_kernel(tc, tab_words, tab_scales, offs, w1_words, w1_s
         picked_rows = kept("picked_rows", [P, S], U8)
         picked_scales = kept("picked_scales", [P, PASSES, S], U8)
         w1_planes = [kept("w1_planes0", [P, PASSES, P], U8), placed("w1_planes1", [P, PASSES, H - P], U8, window_at + 13)]
-        z_codes = [[placed("z_codes%d_%d" % (a, g), [P, BANK], U32, codes_at + 4 * g + 2 * a) for g in range(CHUNKS)]
-                   for a in range(PASSES)]
+        codes_a = [placed("codes_a%d" % g, [P, BANK], U32, codes_at + 2 * g) for g in range(CHUNKS)]
+        codes_b = placed("codes_b", [P, T2], U32, codes_at + 8)
+        planes_b = kept("planes_b", [P, T2], U8)
+        spare_at = codes_at + 16
+        last_turned = [placed("last_turned%d" % g, [P, 2, 2 * P], BF16, spare_at + 8 + g) for g in range(CHUNKS)]
+        last_grouped = [placed("last_grouped%d" % g, [P, P, 4], BF16, spare_at + 12 + g) for g in range(CHUNKS)]
+        last_codes = placed("last_codes", [P, BANK], U32, factor_at + 20)
+        last_planes = kept("last_planes", [P, BANK], U8)
+        padded_codes = placed("padded_codes", [P, BANK], U32, 9)
+        padded_planes = placed("padded_planes", [P, BANK], U8, 8.4375)
         w2_grouped = [placed("w2_grouped%d" % part, [P, HALF, 4], BF16, at)
-                      for part, at in enumerate((window_at + 18.75, window_at + 21.25, turned_at + 4, turned_at + 8))]
-        w2_codes = kept("w2_codes", [P, PASSES, N], U32)
+                      for part, at in enumerate((window_at + 18.75, turned_at + 4, window_at + 21.25, turned_at + 8))]
+        late_codes_at = slot_at[2] + 4
+        w2_cuts = ((0, 0, P, spare_at + 16), (1, 0, P, spare_at + 16.5), (0, P, P, late_codes_at), (0, HALF, HALF, late_codes_at + 0.5),
+                   (1, P, P, late_codes_at + 1.5), (1, HALF, P, late_codes_at + 2), (1, 3 * P, P, window_at + 0.5))
+        w2_parts = [(a, c0, width, placed("w2_codes%d" % n, [P, width], U32, at), kept("w2_plane%d" % n, [P, width], U8))
+                    for n, (a, c0, width, at) in enumerate(w2_cuts)]
         pages = [placed("page0", [P, T2], F32, 12.5625), placed("page1", [P, T2], F32, window_at + 0.5),
                  placed("page2", [P, T2], F32, 0)]
         released = [placed("released0", [P, T2], F32, window_at + 9), placed("released1", [P, T2], F32, window_at + 24)]
@@ -142,6 +155,9 @@ def tile_list_proof_board_kernel(tc, tab_words, tab_scales, offs, w1_words, w1_s
         nc.scalar.activation(vector_rows[64:P, :], zeros[64:P, :], TANH)
         load_w1_scales(w1_planes[0], 0, P)
         nc.tensor.transpose(back_banks[0][:, 0, :], vector_rows[:], identity[:])
+        for g in range(CHUNKS):
+            for u in range(2):
+                nc.scalar.copy(turned[1][g][:].bitcast(F32)[:, u, :, 96:P], zeros[:].rearrange("p (c w) -> p c w", c=BLOCKS))
 
         nc.vector.tensor_copy(picked_rows[:], table_scales[:].indirect(idx[:]))
 
@@ -224,8 +240,10 @@ def tile_list_proof_board_kernel(tc, tab_words, tab_scales, offs, w1_words, w1_s
                     t0 = BANK * g + P * c
                     nc.tensor.matmul(sum_banks[g][:, c, :], pages[i % PAGES][:, t0:t0 + P], page_identity[i][:],
                                      start=False, stop=(c == BLOCKS - 1), is_transpose=True)
+                rounded = last_turned[g][:].rearrange("t u (c w) -> t u c w", c=BLOCKS) if i == LAST else \
+                    turned[a][g][:, :, :, 64 * place:64 * (place + 1)]
                 nc.scalar.copy(
-                    turned[a][g][:, :, :, 64 * place:64 * (place + 1)].rearrange("t u c (w e) -> t u c w e", e=2),
+                    rounded.rearrange("t u c (w e) -> t u c w e", e=2),
                     sum_banks[g][:].rearrange("t c (w u e) -> t u c w e", u=2, e=2))
 
         def release_page(i):
@@ -252,6 +270,18 @@ def tile_list_proof_board_kernel(tc, tab_words, tab_scales, offs, w1_words, w1_s
                 nc.scalar.copy(w2_grouped[part][:, c0:c0 + P, :].rearrange("p (c k) j -> p c j k", k=4),
                                raw[:, :, first + c0:first + c0 + P].rearrange("p j (c k) -> p c j k", k=4))
 
+        def quantize_w2(n):
+            a, c0, width, codes, plane = w2_parts[n]
+            part, at = divmod(c0, HALF)
+            nc.vector.quantize_mx(out=codes[:].bitcast(FP8X4), scales=plane[:],
+                                  in_=w2_grouped[2 * a + part][:, at:at + width, :].rearrange("p n j -> p (n j)"))
+
+        def pad_last_rows():
+            codes, plane = w2_parts[1][3:]
+            for c in range(BLOCKS):
+                nc.gpsimd.dma_start(padded_codes[32 * c:32 * (c + 1), P * c:P * (c + 1)].bitcast(I32), codes[96:P, :].bitcast(I32))
+                nc.gpsimd.dma_start(padded_planes[32 * c:32 * c + 4, P * c:P * (c + 1)].bitcast(I32), plane[96:100, :].bitcast(I32))
+
         for i in range(2):
             load_board(i)
         make_factor(0, first_factors[0][:], wgs_first[:])
@@ -262,7 +292,8 @@ def tile_list_proof_board_kernel(tc, tab_words, tab_scales, offs, w1_words, w1_s
             first_product(0, bank, c0, width, group)
             apply_tanh(0, bank, h[:], width)
             place_scores(0, c0, width, h[:], factor[:])
-        nc.gpsimd.memset(pages[2][:].bitcast(I32), 0)
+        for cleared in (pages[2], padded_codes, padded_planes):
+            nc.gpsimd.memset(cleared[:].bitcast(I32), 0)
         multiply(1)
         score(1)
         make_factors(1)
@@ -273,8 +304,8 @@ def tile_list_proof_board_kernel(tc, tab_words, tab_scales, offs, w1_words, w1_s
         make_factors(2)
 
         for i in range(ROW_TILES):
-            g = i - (TILES_PER_PASS - 1)
-            turns_back = 0 <= g < CHUNKS
+            g = {3: 0, 4: 2, 5: 3}.get(i)
+            turns_back = g is not None
             if i > 0:
                 place_scores(i, 0, S, h_sb[i][:], factors[i][:])
             if i + 2 < ROW_TILES:
@@ -287,6 +318,9 @@ def tile_list_proof_board_kernel(tc, tab_words, tab_scales, offs, w1_words, w1_s
             if turns_back:
                 for b in range(2):
                     turn_back_half(0, g, b, back_banks[b])
+            if i == LAST - 1:
+                for chunk in range(EARLY_CHUNKS):
+                    turn_back(1, chunk, (back_banks, mx_banks)[chunk % 2], (nc.scalar.copy, nc.scalar.copy))
             if i < LAST:
                 turn_board(i + 1)
             if i + 2 < ROW_TILES:
@@ -298,78 +332,107 @@ def tile_list_proof_board_kernel(tc, tab_words, tab_scales, offs, w1_words, w1_s
             if turns_back:
                 for b in range(2):
                     group_half(0, g, b, back_banks[b], nc.scalar.copy)
+            if i == 3:
+                turn_back(0, 1, back_banks, (nc.scalar.copy, nc.scalar.copy))
             if i + 3 < ROW_TILES:
                 make_factors(i + 3)
             if i + 3 == LAST:
                 nc.gpsimd.memset(released[0][:].bitcast(I32), 0)
             if i in W2_TILES:
                 group_w2(W2_TILES.index(i))
+            if i == W2_TILES[0]:
+                quantize_w2(0)
+            if i == W2_TILES[2]:
+                quantize_w2(1)
+                pad_last_rows()
 
         last_h_at = h_at[(LAST - 2) % 4]
-        z_planes = [placed("z_planes0", [P, T2], U8, last_h_at), kept("z_planes1", [P, T2], U8)]
-        w2_planes = placed("w2_planes", [P, PASSES, N], U8, last_h_at + 2)
-        y_sb = [placed("y%d" % j, [P, T2], F32, at) for j, at in enumerate((slot_at[2], factor_at + 16, slot_at[0], turned_at))]
+        planes_a = [placed("planes_a%d" % g, [P, BANK], U8, at)
+                    for g, at in enumerate((last_h_at, last_h_at + 0.5, spare_at + 15, spare_at + 15.5))]
+        y_sb = [placed("y%d" % j, [P, T2], F32, at) for j, at in enumerate((spare_at, factor_at + 16, slot_at[0], turned_at))]
         style_sb = [placed("style%d" % j, [P, M], F32, at)
                     for j, at in enumerate((window_at + 0.5, window_at + 4.5, slot_at[3] - 3.75, slot_at[3] + 0.25))]
         wgo_sb = placed("wgo_sb", [P, M], F32, last_h_at + 4)
-        pulled = [placed("pulled%d" % s, [P, M], F32, at) for s, at in enumerate((factor_at, codes_at + 8, codes_at + 12))]
+        pulled = [placed("pulled%d" % s, [P, M], F32, at)
+                  for s, at in enumerate((factor_at, late_codes_at + 2.25, spare_at + 17))]
         for j in range(OUT_TILES):
             nc.sync.dma_start(style_sb[j][:], style[P * j:P * (j + 1), :])
         nc.sync.dma_start(wgo_sb[:], wgo)
 
-        def quantize_z(a, g, c0=0, width=BANK):
-            nc.vector.quantize_mx(out=z_codes[a][g][:, c0:c0 + width].bitcast(FP8X4),
-                                  scales=z_planes[a][:, BANK * g + c0:BANK * g + c0 + width],
-                                  in_=z_grouped[a][g][:, c0:c0 + width, :].rearrange("p t j -> p (t j)"))
+        def quantize_z(a, g):
+            chunk = slice(BANK * g, BANK * (g + 1))
+            nc.vector.quantize_mx(out=(codes_a[g][:] if a == 0 else codes_b[:, chunk]).bitcast(FP8X4),
+                                  scales=planes_a[g][:] if a == 0 else planes_b[:, chunk],
+                                  in_=z_grouped[a][g][:].rearrange("p t j -> p (t j)"))
 
-        def second_pass(j, g, a, bank, c0=0, width=BANK):
+        def second_pass(j, g, a, bank, start, stop):
+            c0, codes, plane = [(part[1], part[3], part[4]) for part in w2_parts if part[0] == a and part[1] <= P * j][-1]
+            cols = slice(P * j - c0, P * (j + 1) - c0)
+            chunk = slice(BANK * g, BANK * (g + 1))
             nc.tensor.matmul_mx(
-                out=whole(bank)[:, 0:width],
-                lhsT=w2_codes[:, a, P * j:P * (j + 1)].bitcast(FP8X4),
-                lhsT_scale=w2_planes[:, a, P * j:P * (j + 1)],
-                rhs=z_codes[a][g][:, c0:c0 + width].bitcast(FP8X4),
-                rhs_scale=z_planes[a][:, BANK * g + c0:BANK * g + c0 + width],
-                start=(a == 0), stop=(a == PASSES - 1))
+                out=whole(bank), lhsT=codes[:, cols].bitcast(FP8X4), lhsT_scale=plane[:, cols],
+                rhs=(codes_a[g][:] if a == 0 else codes_b[:, chunk]).bitcast(FP8X4),
+                rhs_scale=planes_a[g][:] if a == 0 else planes_b[:, chunk],
+                start=start, stop=stop)
 
-        def empty_bank(j, g, bank, copy, c0=0, width=BANK):
-            copy(y_sb[j][:, BANK * g + c0:BANK * g + c0 + width], whole(bank)[:, 0:width])
+        def empty_bank(j, g, bank):
+            nc.scalar.copy(y_sb[j][:, BANK * g:BANK * (g + 1)], whole(bank))
+
+        late_banks = back_banks + mx_banks
+        for g in range(EARLY_CHUNKS, CHUNKS):
+            turn_back(1, g, (back_banks, mx_banks)[g % 2], (nc.scalar.copy, nc.scalar.copy))
+        for g in range(2):
+            quantize_z(0, g)
+        for g in range(CHUNKS):
+            quantize_z(1, g)
+        for g in range(CHUNKS):
+            cols = slice(P * g, P * (g + 1))
+            for u in range(2):
+                nc.tensor.transpose(late_banks[g][:, u, :], last_turned[g][:].bitcast(F32)[:, u, :], identity[:])
+            nc.scalar.copy(last_grouped[g][:].bitcast(F32), late_banks[g][:, 0:2, :].rearrange("p u t -> p t u"))
+            nc.vector.quantize_mx(out=last_codes[:, cols].bitcast(FP8X4), scales=last_planes[:, cols],
+                                  in_=last_grouped[g][:].rearrange("p t j -> p (t j)"))
+        for g in range(2, CHUNKS):
+            quantize_z(0, g)
+        for g in range(CHUNKS):
+            if g < 2:
+                second_pass(0, g, 0, sum_banks[g], True, False)
+            second_pass(0, g, 1, sum_banks[g], g >= 2, False)
+        for g in range(CHUNKS):
+            for c in range(BLOCKS):
+                block = slice(P * c, P * (c + 1))
+                nc.tensor.matmul_mx(
+                    out=sum_banks[g][:, c, :], lhsT=padded_codes[:, block].bitcast(FP8X4), lhsT_scale=padded_planes[:, block],
+                    rhs=last_codes[:, P * g:P * (g + 1)].bitcast(FP8X4), rhs_scale=last_planes[:, P * g:P * (g + 1)],
+                    start=False, stop=(g < 2 and c == BLOCKS - 1))
+            if g >= 2:
+                second_pass(0, g, 0, sum_banks[g], False, True)
+            empty_bank(0, g, sum_banks[g])
+        for n in range(2, len(w2_parts) - 1):
+            quantize_w2(n)
+        for c in range(BLOCKS):
+            nc.sync.dma_start(
+                codes_b[96:P, :].bitcast(I32).rearrange("w (g c t) -> w g c t", g=CHUNKS, c=BLOCKS)[:, :, c, :],
+                last_codes[32 * c:32 * (c + 1), :].bitcast(I32).rearrange("w (g t) -> w g t", g=CHUNKS))
+            nc.sync.dma_start(
+                planes_b[96:100, :].bitcast(I32).rearrange("r (g c t) -> r g c t", g=CHUNKS, c=BLOCKS)[:, :, c, :],
+                last_planes[32 * c:32 * c + 4, :].bitcast(I32).rearrange("r (g t) -> r g t", g=CHUNKS))
 
         def pull(j):
             nc.vector.tensor_tensor(pulled[j % 3][:], y_sb[j][:].indirect(idx3[:]), style_sb[j][:], SUBTRACT)
-
-        for part in range(4):
-            a, cols = part // 2, slice(HALF * (part % 2), HALF * (part % 2 + 1))
-            nc.vector.quantize_mx(out=w2_codes[:, a, cols].bitcast(FP8X4), scales=w2_planes[:, a, cols],
-                                  in_=w2_grouped[part][:].rearrange("p n j -> p (n j)"))
-        end = CHUNKS - 1
-        s0, s1, s2, s3 = sum_banks
-        on_scalar, on_vector = nc.scalar.copy, nc.vector.tensor_copy
-        back_pairs = (back_banks, mx_banks, (s2, s3), back_banks)
-        back_copies = ((on_scalar, on_vector), (on_vector, on_scalar), (on_scalar, on_scalar), (on_scalar, on_vector))
-        pieces = ((0, s0, 0, BANK), (1, s1, 0, BANK), (2, mx_banks[0], 0, BANK), (end, mx_banks[1], 0, HALF), (end, s2, HALF, HALF))
-        for g in range(CHUNKS):
-            turn_back(1, g, back_pairs[g], back_copies[g])
-        for g, bank, c0, width in pieces:
-            quantize_z(1, g, c0, width)
-        for g, bank, c0, width in pieces:
-            if c0 == 0:
-                quantize_z(0, g)
-            for a in range(PASSES):
-                second_pass(0, g, a, bank, c0, width)
-            empty_bank(0, g, bank, on_vector if c0 else on_scalar, c0, width)
 
         def release(j):
             nc.vector.tensor_tensor(released[j % 2][:].indirect(idx4[:]), pulled[j % 3][:], wgo_sb[:], MULT)
             nc.sync.dma_start(out[P * j:P * (j + 1), :], released[j % 2][:])
 
-        late_banks = back_banks + [mx_banks[1], s2]
         pull(0)
+        quantize_w2(len(w2_parts) - 1)
         release(0)
         for j in range(1, OUT_TILES):
             for g in range(CHUNKS):
                 for a in range(PASSES):
-                    second_pass(j, g, a, late_banks[g])
-                empty_bank(j, g, late_banks[g], nc.scalar.copy)
+                    second_pass(j, g, a, late_banks[g], a == 0, a == PASSES - 1)
+                empty_bank(j, g, late_banks[g])
         for j in range(1, OUT_TILES):
             pull(j)
         for j in range(1, OUT_TILES):

@@ -115,8 +115,9 @@ def tile_list_proof_board_kernel(tc, tab_words, tab_scales, offs, w1_words, w1_s
         w2_grouped = [placed("w2_grouped%d" % part, [P, HALF, 4], BF16, at)
                       for part, at in enumerate((window_at + 18.75, turned_at + 4, window_at + 21.25, turned_at + 8))]
         late_codes_at = slot_at[2] + 4
+        style_at = (turned_at + 32, w2_at[0], w2_at[0] + 4, w2_at[1] + 4)
         w2_cuts = ((0, 0, P, spare_at + 16), (1, 0, P, spare_at + 16.5), (0, P, P, late_codes_at), (0, HALF, HALF, late_codes_at + 0.5),
-                   (1, P, P, late_codes_at + 1.5), (1, HALF, P, late_codes_at + 2), (1, 3 * P, P, window_at + 0.5))
+                   (1, P, P, late_codes_at + 1.5), (1, HALF, P, late_codes_at + 2), (1, 3 * P, P, style_at[0]))
         w2_parts = [(a, c0, width, placed("w2_codes%d" % n, [P, width], U32, at), kept("w2_plane%d" % n, [P, width], U8))
                     for n, (a, c0, width, at) in enumerate(w2_cuts)]
         pages = [placed("page0", [P, T2], F32, 12.5625), placed("page1", [P, T2], F32, window_at + 0.5),
@@ -351,10 +352,10 @@ def tile_list_proof_board_kernel(tc, tab_words, tab_scales, offs, w1_words, w1_s
                     for g, at in enumerate((last_h_at, last_h_at + 0.5, spare_at + 15, spare_at + 15.5))]
         y_sb = [placed("y%d" % j, [P, T2], F32, at) for j, at in enumerate((spare_at, factor_at + 16, slot_at[0], turned_at))]
         style_sb = [placed("style%d" % j, [P, M], F32, at)
-                    for j, at in enumerate((window_at + 0.5, window_at + 4.5, slot_at[3] - 3.75, slot_at[3] + 0.25))]
-        wgo_sb = placed("wgo_sb", [P, M], F32, last_h_at + 4)
+                    for j, at in enumerate(style_at)]
+        wgo_sb = placed("wgo_sb", [P, M], F32, turned_at + 36)
         pulled = [placed("pulled%d" % s, [P, M], F32, at)
-                  for s, at in enumerate((factor_at, late_codes_at + 2.25, spare_at + 17))]
+                  for s, at in enumerate((factor_at, spare_at + 17, style_at[1] - 2, style_at[1] + 2))]
         for j in range(OUT_TILES):
             nc.sync.dma_start(style_sb[j][:], style[P * j:P * (j + 1), :])
         nc.sync.dma_start(wgo_sb[:], wgo)
@@ -419,21 +420,27 @@ def tile_list_proof_board_kernel(tc, tab_words, tab_scales, offs, w1_words, w1_s
                 last_planes[32 * c:32 * c + 4, :].bitcast(I32).rearrange("r (g t) -> r g t", g=CHUNKS))
 
         def pull(j):
-            nc.vector.tensor_tensor(pulled[j % 3][:], y_sb[j][:].indirect(idx3[:]), style_sb[j][:], SUBTRACT)
+            nc.vector.tensor_tensor(pulled[j][:], y_sb[j][:].indirect(idx3[:]), style_sb[j][:], SUBTRACT)
 
         def release(j):
-            nc.vector.tensor_tensor(released[j % 2][:].indirect(idx4[:]), pulled[j % 3][:], wgo_sb[:], MULT)
+            nc.vector.tensor_tensor(released[j % 2][:].indirect(idx4[:]), pulled[j][:], wgo_sb[:], MULT)
             nc.sync.dma_start(out[P * j:P * (j + 1), :], released[j % 2][:])
+
+        def output_tile(j):
+            for a in range(PASSES):
+                for g in range(CHUNKS):
+                    second_pass(j, g, a, late_banks[g], a == 0, a == PASSES - 1)
+                    if a == PASSES - 1:
+                        empty_bank(j, g, late_banks[g])
 
         pull(0)
         quantize_w2(len(w2_parts) - 1)
         release(0)
         for j in range(1, OUT_TILES):
-            for g in range(CHUNKS):
-                for a in range(PASSES):
-                    second_pass(j, g, a, late_banks[g], a == 0, a == PASSES - 1)
-                empty_bank(j, g, late_banks[g])
-        for j in range(1, OUT_TILES):
+            output_tile(j)
+        pull(1)
+        release(1)
+        for j in range(2, OUT_TILES):
             pull(j)
-        for j in range(1, OUT_TILES):
+        for j in range(2, OUT_TILES):
             release(j)

@@ -227,10 +227,13 @@ def tile_list_proof_board_kernel(tc, tab_words, tab_scales, offs, w1_words, w1_s
             nc.vector.tensor_tensor(pages[i % PAGES][:].indirect(idx2[:, c0 // 16:(c0 + width) // 16]),
                                     h, factor, MULT)
 
+        def block_start(i, g, c):
+            return BANK * c + P * g if i == LAST else BANK * g + P * c
+
         def turn_board(i):
             for g in range(CHUNKS):
                 for c in range(BLOCKS):
-                    t0 = BANK * g + P * c
+                    t0 = block_start(i, g, c)
                     nc.tensor.matmul(sum_banks[g][:, c, :], board_sb[i][:, t0:t0 + P], identity[:],
                                      start=(c == 0), stop=False, is_transpose=True)
 
@@ -238,7 +241,7 @@ def tile_list_proof_board_kernel(tc, tab_words, tab_scales, offs, w1_words, w1_s
             a, place = divmod(i, TILES_PER_PASS)
             for g in range(CHUNKS):
                 for c in range(BLOCKS):
-                    t0 = BANK * g + P * c
+                    t0 = block_start(i, g, c)
                     nc.tensor.matmul(sum_banks[g][:, c, :], pages[i % PAGES][:, t0:t0 + P], page_identity[i][:],
                                      start=False, stop=(c == BLOCKS - 1), is_transpose=True)
                 rounded = last_turned[g][:].rearrange("t u (c w) -> t u c w", c=BLOCKS) if i == LAST else \
@@ -355,7 +358,7 @@ def tile_list_proof_board_kernel(tc, tab_words, tab_scales, offs, w1_words, w1_s
                     for j, at in enumerate(style_at)]
         wgo_sb = placed("wgo_sb", [P, M], F32, turned_at + 36)
         pulled = [placed("pulled%d" % s, [P, M], F32, at)
-                  for s, at in enumerate((factor_at, spare_at + 17, style_at[1] - 2, style_at[1] + 2))]
+                  for s, at in enumerate((factor_at, late_codes_at + 2.25, spare_at + 17, factor_at))]
         for j in range(OUT_TILES):
             nc.sync.dma_start(style_sb[j][:], style[P * j:P * (j + 1), :])
         nc.sync.dma_start(wgo_sb[:], wgo)
@@ -376,8 +379,8 @@ def tile_list_proof_board_kernel(tc, tab_words, tab_scales, offs, w1_words, w1_s
                 rhs_scale=planes_a[g][:] if a == 0 else planes_b[:, chunk],
                 start=start, stop=stop)
 
-        def empty_bank(j, g, bank):
-            nc.scalar.copy(y_sb[j][:, BANK * g:BANK * (g + 1)], whole(bank))
+        def empty_bank(j, g, bank, copy=nc.scalar.copy):
+            copy(y_sb[j][:, BANK * g:BANK * (g + 1)], whole(bank))
 
         late_banks = back_banks + mx_banks
         for g in range(EARLY_CHUNKS, CHUNKS):
@@ -400,24 +403,19 @@ def tile_list_proof_board_kernel(tc, tab_words, tab_scales, offs, w1_words, w1_s
                 second_pass(0, g, 0, sum_banks[g], True, False)
             second_pass(0, g, 1, sum_banks[g], g >= 2, False)
         for g in range(CHUNKS):
-            for c in range(BLOCKS):
-                block = slice(P * c, P * (c + 1))
-                nc.tensor.matmul_mx(
-                    out=sum_banks[g][:, c, :], lhsT=padded_codes[:, block].bitcast(FP8X4), lhsT_scale=padded_planes[:, block],
-                    rhs=last_codes[:, P * g:P * (g + 1)].bitcast(FP8X4), rhs_scale=last_planes[:, P * g:P * (g + 1)],
-                    start=False, stop=(g < 2 and c == BLOCKS - 1))
+            block = slice(P * g, P * (g + 1))
+            nc.tensor.matmul_mx(
+                out=whole(sum_banks[g]), lhsT=padded_codes[:, block].bitcast(FP8X4), lhsT_scale=padded_planes[:, block],
+                rhs=last_codes[:].bitcast(FP8X4), rhs_scale=last_planes[:], start=False, stop=(g < 2))
             if g >= 2:
                 second_pass(0, g, 0, sum_banks[g], False, True)
-            empty_bank(0, g, sum_banks[g])
+            empty_bank(0, g, sum_banks[g], nc.vector.tensor_copy if g == 2 else nc.scalar.copy)
         for n in range(2, len(w2_parts) - 1):
             quantize_w2(n)
-        for c in range(BLOCKS):
-            nc.sync.dma_start(
-                codes_b[96:P, :].bitcast(I32).rearrange("w (g c t) -> w g c t", g=CHUNKS, c=BLOCKS)[:, :, c, :],
-                last_codes[32 * c:32 * (c + 1), :].bitcast(I32).rearrange("w (g t) -> w g t", g=CHUNKS))
-            nc.sync.dma_start(
-                planes_b[96:100, :].bitcast(I32).rearrange("r (g c t) -> r g c t", g=CHUNKS, c=BLOCKS)[:, :, c, :],
-                last_planes[32 * c:32 * c + 4, :].bitcast(I32).rearrange("r (g t) -> r g t", g=CHUNKS))
+        for g in range(CHUNKS):
+            chunk = slice(BANK * g, BANK * (g + 1))
+            nc.sync.dma_start(codes_b[96:P, chunk].bitcast(I32), last_codes[32 * g:32 * (g + 1), :].bitcast(I32))
+            nc.sync.dma_start(planes_b[96:100, chunk].bitcast(I32), last_planes[32 * g:32 * g + 4, :].bitcast(I32))
 
         def pull(j):
             nc.vector.tensor_tensor(pulled[j][:], y_sb[j][:].indirect(idx3[:]), style_sb[j][:], SUBTRACT)
@@ -438,9 +436,7 @@ def tile_list_proof_board_kernel(tc, tab_words, tab_scales, offs, w1_words, w1_s
         release(0)
         for j in range(1, OUT_TILES):
             output_tile(j)
-        pull(1)
-        release(1)
-        for j in range(2, OUT_TILES):
+        for j in range(1, OUT_TILES):
             pull(j)
-        for j in range(2, OUT_TILES):
+        for j in range(1, OUT_TILES):
             release(j)

@@ -33,7 +33,7 @@ FIRST = 256
 HALF = BANK // 2
 W2_TILES = (1, 4, 2, 5)
 SCALE_ROW = 96
-EARLY_CHUNKS = 4
+EARLY_CHUNKS = 3
 KB = 1024
 
 
@@ -110,13 +110,14 @@ def tile_list_proof_board_kernel(tc, tab_words, tab_scales, offs, w1_words, w1_s
         last_grouped = [placed("last_grouped%d" % g, [P, P, 4], BF16, spare_at + 12 + g) for g in range(CHUNKS)]
         last_codes = placed("last_codes", [P, BANK], U32, factor_at + 20)
         last_planes = kept("last_planes", [P, BANK], U8)
-        padded_codes = placed("padded_codes", [P, BANK], U32, 9)
-        padded_planes = placed("padded_planes", [P, BANK], U8, 8.4375)
+        padded_rows = placed("padded_rows", [P, 4 * BANK], BF16, 8.4375)
+        padded_codes = kept("padded_codes", [P, BANK], U32)
+        padded_planes = placed("padded_planes", [P, BANK], U8, h_at[1] + 1)
         w2_grouped = [placed("w2_grouped%d" % part, [P, HALF, 4], BF16, at)
                       for part, at in enumerate((window_at + 18.75, turned_at + 4, window_at + 21.25, turned_at + 8))]
         late_codes_at = slot_at[2] + 4
         style_at = (turned_at + 32, w2_at[0], w2_at[0] + 4, w2_at[1] + 4)
-        w2_cuts = ((0, 0, P, spare_at + 16), (1, 0, P, spare_at + 16.5), (0, P, P, late_codes_at), (0, HALF, HALF, late_codes_at + 0.5),
+        w2_cuts = ((0, 0, P, h_at[1] + 2), (1, 0, P, h_at[1] + 2.5), (0, P, P, late_codes_at), (0, HALF, HALF, late_codes_at + 0.5),
                    (1, P, P, late_codes_at + 1.5), (1, HALF, P, late_codes_at + 2), (1, 3 * P, P, style_at[0]))
         w2_parts = [(a, c0, width, placed("w2_codes%d" % n, [P, width], U32, at), kept("w2_plane%d" % n, [P, width], U8))
                     for n, (a, c0, width, at) in enumerate(w2_cuts)]
@@ -281,10 +282,9 @@ def tile_list_proof_board_kernel(tc, tab_words, tab_scales, offs, w1_words, w1_s
                                   in_=w2_grouped[2 * a + part][:, at:at + width, :].rearrange("p n j -> p (n j)"))
 
         def pad_last_rows():
-            codes, plane = w2_parts[1][3:]
             for c in range(BLOCKS):
-                nc.gpsimd.dma_start(padded_codes[32 * c:32 * (c + 1), P * c:P * (c + 1)].bitcast(I32), codes[96:P, :].bitcast(I32))
-                nc.gpsimd.dma_start(padded_planes[32 * c:32 * c + 4, P * c:P * (c + 1)].bitcast(I32), plane[96:100, :].bitcast(I32))
+                nc.sync.dma_start(padded_rows[32 * c:32 * (c + 1), BANK * c:BANK * (c + 1)],
+                                  w2_grouped[2][96:P, 0:P, :].rearrange("p n j -> p (n j)"))
 
         for i in range(2):
             load_board(i)
@@ -296,7 +296,7 @@ def tile_list_proof_board_kernel(tc, tab_words, tab_scales, offs, w1_words, w1_s
             first_product(0, bank, c0, width, group)
             apply_tanh(0, bank, h[:], width)
             place_scores(0, c0, width, h[:], factor[:])
-        for cleared in (pages[2], padded_codes, padded_planes):
+        for cleared in (pages[2], padded_rows):
             nc.gpsimd.memset(cleared[:].bitcast(I32), 0)
         multiply(1)
         score(1)
@@ -323,14 +323,19 @@ def tile_list_proof_board_kernel(tc, tab_words, tab_scales, offs, w1_words, w1_s
                 for b in range(2):
                     turn_back_half(0, g, b, back_banks[b])
             if i == LAST - 1:
-                for chunk in range(EARLY_CHUNKS):
+                for chunk in range(EARLY_CHUNKS - 1):
                     turn_back(1, chunk, (back_banks, mx_banks)[chunk % 2], (nc.scalar.copy, nc.scalar.copy))
+                for b in range(2):
+                    turn_back_half(1, EARLY_CHUNKS - 1, b, back_banks[b])
             if i < LAST:
                 turn_board(i + 1)
             if i + 2 < ROW_TILES:
                 score(i + 2)
             if i < LAST:
                 release_page(i + 1)
+            if i == LAST - 1:
+                for b in range(2):
+                    group_half(1, EARLY_CHUNKS - 1, b, back_banks[b], nc.scalar.copy)
             if i + 3 < ROW_TILES:
                 multiply(i + 3)
             if turns_back:
@@ -344,10 +349,7 @@ def tile_list_proof_board_kernel(tc, tab_words, tab_scales, offs, w1_words, w1_s
                 nc.gpsimd.memset(released[0][:].bitcast(I32), 0)
             if i in W2_TILES:
                 group_w2(W2_TILES.index(i))
-            if i == W2_TILES[0]:
-                quantize_w2(0)
             if i == W2_TILES[2]:
-                quantize_w2(1)
                 pad_last_rows()
 
         last_h_at = h_at[(LAST - 2) % 4]
@@ -385,8 +387,11 @@ def tile_list_proof_board_kernel(tc, tab_words, tab_scales, offs, w1_words, w1_s
         late_banks = back_banks + mx_banks
         for g in range(EARLY_CHUNKS, CHUNKS):
             turn_back(1, g, (back_banks, mx_banks)[g % 2], (nc.scalar.copy, nc.scalar.copy))
+        for n in range(2):
+            quantize_w2(n)
         for g in range(2):
             quantize_z(0, g)
+        nc.vector.quantize_mx(out=padded_codes[:].bitcast(FP8X4), scales=padded_planes[:], in_=padded_rows[:])
         for g in range(CHUNKS):
             quantize_z(1, g)
         for g in range(CHUNKS):

@@ -31,9 +31,8 @@ OUT_TILES = N // P
 PAGES = 3
 FIRST = 256
 HALF = BANK // 2
-W2_TILES = (1, 4, 2, 5)
+W2_TILES = (1, 5, 2, 5)
 SCALE_ROW = 96
-EARLY_CHUNKS = 3
 KB = 1024
 
 
@@ -88,11 +87,12 @@ def tile_list_proof_board_kernel(tc, tab_words, tab_scales, offs, w1_words, w1_s
         first_h = [placed("first_h%d" % c0, [P, width], F32, at) for (c0, width), at in zip(first_pieces, (9, 21.0625, 22.0625))]
         h_sb = [None] + [placed("h%d" % i, [P, S], F32, w2_at[1] + 6 if i == 1 else h_at[(i - 2) % 4]) for i in range(1, ROW_TILES)]
         board_sb = [placed("board%d" % i, [P, T2], F32, slot_at[i % 4]) for i in range(ROW_TILES)]
-        page_identity = [placed("page_identity%d" % i, [P, P], F32, slot_at[i % 4]) for i in range(ROW_TILES)]
+        page_identity = [placed("page_identity%d" % i, [P, P], F32, turned_at + 24 if i == LAST else slot_at[i % 4])
+                         for i in range(ROW_TILES)]
         w2_raw = [placed("w2_raw%d" % a, [P, 4, N], F32, w2_at[a]) for a in range(PASSES)]
         turned = [[placed("turned%d_%d" % (a, g), [P, 2, BLOCKS, 2 * P], BF16, turned_at + 16 * a + 4 * g) for g in range(CHUNKS)]
                   for a in range(PASSES)]
-        z_grouped = [[placed("z_grouped%d_%d" % (a, g), [P, BANK, 4], BF16, (slot_at[0] + 6, factor_at, slot_at[1] + 6, slot_at[2] + 4)[g] if a == 0 else factor_at + 8 + 4 * g)
+        z_grouped = [[placed("z_grouped%d_%d" % (a, g), [P, BANK, 4], BF16, (slot_at[0] + 6, factor_at, slot_at[1] + 6, factor_at + 4)[g] if a == 0 else factor_at + 8 + 4 * g)
                       for g in range(CHUNKS)] for a in range(PASSES)]
 
         zeros = kept("zeros", [P, P], F32)
@@ -110,12 +110,11 @@ def tile_list_proof_board_kernel(tc, tab_words, tab_scales, offs, w1_words, w1_s
         last_grouped = [placed("last_grouped%d" % g, [P, P, 4], BF16, spare_at + 12 + g) for g in range(CHUNKS)]
         last_codes = placed("last_codes", [P, BANK], U32, factor_at + 20)
         last_planes = kept("last_planes", [P, BANK], U8)
-        padded_rows = placed("padded_rows", [P, 4 * BANK], BF16, 8.4375)
-        padded_codes = kept("padded_codes", [P, BANK], U32)
-        padded_planes = placed("padded_planes", [P, BANK], U8, h_at[1] + 1)
+        padded_codes = placed("padded_codes", [P, BANK], U32, 9)
+        padded_planes = placed("padded_planes", [P, BANK], U8, 8.4375)
         w2_grouped = [placed("w2_grouped%d" % part, [P, HALF, 4], BF16, at)
-                      for part, at in enumerate((window_at + 18.75, turned_at + 4, window_at + 21.25, turned_at + 8))]
-        late_codes_at = slot_at[2] + 4
+                      for part, at in enumerate((window_at + 18.75, turned_at + 12, window_at + 21.25, turned_at + 14))]
+        late_codes_at = factor_at + 4
         style_at = (turned_at + 32, w2_at[0], w2_at[0] + 4, w2_at[1] + 4)
         w2_cuts = ((0, 0, P, h_at[1] + 2), (1, 0, P, h_at[1] + 2.5), (0, P, P, late_codes_at), (0, HALF, HALF, late_codes_at + 0.5),
                    (1, P, P, late_codes_at + 1.5), (1, HALF, P, late_codes_at + 2), (1, 3 * P, P, style_at[0]))
@@ -228,6 +227,11 @@ def tile_list_proof_board_kernel(tc, tab_words, tab_scales, offs, w1_words, w1_s
             nc.vector.tensor_tensor(pages[i % PAGES][:].indirect(idx2[:, c0 // 16:(c0 + width) // 16]),
                                     h, factor, MULT)
 
+        late_banks = back_banks + mx_banks
+
+        def banks_of(i):
+            return late_banks if i == LAST else sum_banks
+
         def block_start(i, g, c):
             return BANK * c + P * g if i == LAST else BANK * g + P * c
 
@@ -235,7 +239,7 @@ def tile_list_proof_board_kernel(tc, tab_words, tab_scales, offs, w1_words, w1_s
             for g in range(CHUNKS):
                 for c in range(BLOCKS):
                     t0 = block_start(i, g, c)
-                    nc.tensor.matmul(sum_banks[g][:, c, :], board_sb[i][:, t0:t0 + P], identity[:],
+                    nc.tensor.matmul(banks_of(i)[g][:, c, :], board_sb[i][:, t0:t0 + P], identity[:],
                                      start=(c == 0), stop=False, is_transpose=True)
 
         def turn_page(i):
@@ -243,13 +247,13 @@ def tile_list_proof_board_kernel(tc, tab_words, tab_scales, offs, w1_words, w1_s
             for g in range(CHUNKS):
                 for c in range(BLOCKS):
                     t0 = block_start(i, g, c)
-                    nc.tensor.matmul(sum_banks[g][:, c, :], pages[i % PAGES][:, t0:t0 + P], page_identity[i][:],
+                    nc.tensor.matmul(banks_of(i)[g][:, c, :], pages[i % PAGES][:, t0:t0 + P], page_identity[i][:],
                                      start=False, stop=(c == BLOCKS - 1), is_transpose=True)
                 rounded = last_turned[g][:].rearrange("t u (c w) -> t u c w", c=BLOCKS) if i == LAST else \
                     turned[a][g][:, :, :, 64 * place:64 * (place + 1)]
                 nc.scalar.copy(
                     rounded.rearrange("t u c (w e) -> t u c w e", e=2),
-                    sum_banks[g][:].rearrange("t c (w u e) -> t u c w e", u=2, e=2))
+                    banks_of(i)[g][:].rearrange("t c (w u e) -> t u c w e", u=2, e=2))
 
         def release_page(i):
             nc.scalar.copy(page_identity[i][:], identity[:])
@@ -282,9 +286,10 @@ def tile_list_proof_board_kernel(tc, tab_words, tab_scales, offs, w1_words, w1_s
                                   in_=w2_grouped[2 * a + part][:, at:at + width, :].rearrange("p n j -> p (n j)"))
 
         def pad_last_rows():
+            codes, plane = w2_parts[1][3:]
             for c in range(BLOCKS):
-                nc.sync.dma_start(padded_rows[32 * c:32 * (c + 1), BANK * c:BANK * (c + 1)],
-                                  w2_grouped[2][96:P, 0:P, :].rearrange("p n j -> p (n j)"))
+                nc.sync.dma_start(padded_codes[32 * c:32 * (c + 1), P * c:P * (c + 1)].bitcast(I32), codes[96:P, :].bitcast(I32))
+                nc.sync.dma_start(padded_planes[32 * c:32 * c + 4, P * c:P * (c + 1)].bitcast(I32), plane[96:100, :].bitcast(I32))
 
         for i in range(2):
             load_board(i)
@@ -296,7 +301,7 @@ def tile_list_proof_board_kernel(tc, tab_words, tab_scales, offs, w1_words, w1_s
             first_product(0, bank, c0, width, group)
             apply_tanh(0, bank, h[:], width)
             place_scores(0, c0, width, h[:], factor[:])
-        for cleared in (pages[2], padded_rows):
+        for cleared in (pages[2], padded_codes, padded_planes):
             nc.gpsimd.memset(cleared[:].bitcast(I32), 0)
         multiply(1)
         score(1)
@@ -308,8 +313,8 @@ def tile_list_proof_board_kernel(tc, tab_words, tab_scales, offs, w1_words, w1_s
         make_factors(2)
 
         for i in range(ROW_TILES):
-            g = {3: 0, 4: 2, 5: 3}.get(i)
-            turns_back = g is not None
+            g = 2 * (i - 3)
+            turns_back = i in (3, 4)
             if i > 0:
                 place_scores(i, 0, S, h_sb[i][:], factors[i][:])
             if i + 2 < ROW_TILES:
@@ -323,34 +328,38 @@ def tile_list_proof_board_kernel(tc, tab_words, tab_scales, offs, w1_words, w1_s
                 for b in range(2):
                     turn_back_half(0, g, b, back_banks[b])
             if i == LAST - 1:
-                for chunk in range(EARLY_CHUNKS - 1):
-                    turn_back(1, chunk, (back_banks, mx_banks)[chunk % 2], (nc.scalar.copy, nc.scalar.copy))
+                pairs = (sum_banks[:2], sum_banks[2:])
+                on_scalar = (nc.scalar.copy, nc.scalar.copy)
+                for chunk in range(2):
+                    turn_back(1, chunk, pairs[chunk], on_scalar)
                 for b in range(2):
-                    turn_back_half(1, EARLY_CHUNKS - 1, b, back_banks[b])
-            if i < LAST:
+                    turn_back_half(1, 2, b, pairs[0][b])
+                release_page(LAST)
+                for b in range(2):
+                    group_half(1, 2, b, pairs[0][b], nc.scalar.copy)
+                turn_back(1, 3, pairs[1], on_scalar)
+            if i < LAST - 1:
                 turn_board(i + 1)
             if i + 2 < ROW_TILES:
                 score(i + 2)
-            if i < LAST:
+            if i == LAST - 2:
+                turn_board(LAST)
+            if i < LAST - 1:
                 release_page(i + 1)
-            if i == LAST - 1:
-                for b in range(2):
-                    group_half(1, EARLY_CHUNKS - 1, b, back_banks[b], nc.scalar.copy)
             if i + 3 < ROW_TILES:
                 multiply(i + 3)
             if turns_back:
                 for b in range(2):
                     group_half(0, g, b, back_banks[b], nc.scalar.copy)
-            if i == 3:
-                turn_back(0, 1, back_banks, (nc.scalar.copy, nc.scalar.copy))
+            if turns_back:
+                turn_back(0, g + 1, back_banks, (nc.scalar.copy, nc.scalar.copy))
             if i + 3 < ROW_TILES:
                 make_factors(i + 3)
             if i + 3 == LAST:
                 nc.gpsimd.memset(released[0][:].bitcast(I32), 0)
-            if i in W2_TILES:
-                group_w2(W2_TILES.index(i))
-            if i == W2_TILES[2]:
-                pad_last_rows()
+            for part in range(4):
+                if W2_TILES[part] == i:
+                    group_w2(part)
 
         last_h_at = h_at[(LAST - 2) % 4]
         planes_a = [placed("planes_a%d" % g, [P, BANK], U8, at)
@@ -360,7 +369,7 @@ def tile_list_proof_board_kernel(tc, tab_words, tab_scales, offs, w1_words, w1_s
                     for j, at in enumerate(style_at)]
         wgo_sb = placed("wgo_sb", [P, M], F32, turned_at + 36)
         pulled = [placed("pulled%d" % s, [P, M], F32, at)
-                  for s, at in enumerate((factor_at, late_codes_at + 2.25, spare_at + 17, factor_at))]
+                  for s, at in enumerate((spare_at + 21, late_codes_at + 2.25, spare_at + 17, spare_at + 21))]
         for j in range(OUT_TILES):
             nc.sync.dma_start(style_sb[j][:], style[P * j:P * (j + 1), :])
         nc.sync.dma_start(wgo_sb[:], wgo)
@@ -384,14 +393,11 @@ def tile_list_proof_board_kernel(tc, tab_words, tab_scales, offs, w1_words, w1_s
         def empty_bank(j, g, bank, copy=nc.scalar.copy):
             copy(y_sb[j][:, BANK * g:BANK * (g + 1)], whole(bank))
 
-        late_banks = back_banks + mx_banks
-        for g in range(EARLY_CHUNKS, CHUNKS):
-            turn_back(1, g, (back_banks, mx_banks)[g % 2], (nc.scalar.copy, nc.scalar.copy))
-        for n in range(2):
+        for n in reversed(range(2)):
             quantize_w2(n)
+        pad_last_rows()
         for g in range(2):
             quantize_z(0, g)
-        nc.vector.quantize_mx(out=padded_codes[:].bitcast(FP8X4), scales=padded_planes[:], in_=padded_rows[:])
         for g in range(CHUNKS):
             quantize_z(1, g)
         for g in range(CHUNKS):

@@ -92,7 +92,8 @@ def tile_list_proof_board_kernel(tc, tab_words, tab_scales, offs, w1_words, w1_s
         w2_raw = [placed("w2_raw%d" % a, [P, 4, N], F32, w2_at[a]) for a in range(PASSES)]
         turned = [[placed("turned%d_%d" % (a, g), [P, 2, BLOCKS, 2 * P], BF16, turned_at + 16 * a + 4 * g) for g in range(CHUNKS)]
                   for a in range(PASSES)]
-        z_grouped = [[placed("z_grouped%d_%d" % (a, g), [P, BANK, 4], BF16, (slot_at[0] + 6, factor_at, slot_at[1] + 6, factor_at + 4)[g] if a == 0 else factor_at + 8 + 4 * g)
+        z_grouped = [[placed("z_grouped%d_%d" % (a, g), [P, BANK, 4], BF16, (slot_at[0] + 6, factor_at, slot_at[1] + 6, factor_at + 4)[g] if a == 0 else
+                             (factor_at + 8, factor_at + 12, factor_at + 16, turned_at + 24)[g])
                       for g in range(CHUNKS)] for a in range(PASSES)]
 
         zeros = kept("zeros", [P, P], F32)
@@ -114,7 +115,7 @@ def tile_list_proof_board_kernel(tc, tab_words, tab_scales, offs, w1_words, w1_s
         padded_planes = placed("padded_planes", [P, BANK], U8, 8.4375)
         w2_grouped = [placed("w2_grouped%d" % part, [P, HALF, 4], BF16, at)
                       for part, at in enumerate((window_at + 18.75, turned_at + 12, window_at + 21.25, turned_at + 14))]
-        late_codes_at = factor_at + 4
+        late_codes_at = turned_at + 24
         style_at = (turned_at + 32, w2_at[0], w2_at[0] + 4, w2_at[1] + 4)
         w2_cuts = ((0, 0, P, h_at[1] + 2), (1, 0, P, h_at[1] + 2.5), (0, P, P, late_codes_at), (0, HALF, HALF, late_codes_at + 0.5),
                    (1, P, P, late_codes_at + 1.5), (1, HALF, P, late_codes_at + 2), (1, 3 * P, P, style_at[0]))
@@ -297,7 +298,7 @@ def tile_list_proof_board_kernel(tc, tab_words, tab_scales, offs, w1_words, w1_s
         for (c0, width), factor in zip(first_pieces[1:], first_factors[1:]):
             make_factor(0, factor[:], wgs_next[:, c0 - FIRST:c0 - FIRST + width])
         for (c0, width), h, factor, bank, group in zip(first_pieces, first_h, first_factors,
-                                                       (mx_banks[0], back_banks[1], mx_banks[1]), (P, P, BANK)):
+                                                       (mx_banks[0], back_banks[1], mx_banks[1]), (FIRST, FIRST, BANK)):
             first_product(0, bank, c0, width, group)
             apply_tanh(0, bank, h[:], width)
             place_scores(0, c0, width, h[:], factor[:])
@@ -337,7 +338,8 @@ def tile_list_proof_board_kernel(tc, tab_words, tab_scales, offs, w1_words, w1_s
                 release_page(LAST)
                 for b in range(2):
                     group_half(1, 2, b, pairs[0][b], nc.scalar.copy)
-                turn_back(1, 3, pairs[1], on_scalar)
+                for b in range(2):
+                    turn_back_half(1, 3, b, pairs[1][b])
             if i < LAST - 1:
                 turn_board(i + 1)
             if i + 2 < ROW_TILES:
@@ -363,7 +365,7 @@ def tile_list_proof_board_kernel(tc, tab_words, tab_scales, offs, w1_words, w1_s
 
         last_h_at = h_at[(LAST - 2) % 4]
         planes_a = [placed("planes_a%d" % g, [P, BANK], U8, at)
-                    for g, at in enumerate((last_h_at, last_h_at + 0.5, spare_at + 15, spare_at + 15.5))]
+                    for g, at in enumerate((last_h_at, last_h_at + 0.5, last_h_at + 1, last_h_at + 1.5))]
         y_sb = [placed("y%d" % j, [P, T2], F32, at) for j, at in enumerate((spare_at, factor_at + 16, slot_at[0], turned_at))]
         style_sb = [placed("style%d" % j, [P, M], F32, at)
                     for j, at in enumerate(style_at)]
@@ -396,10 +398,8 @@ def tile_list_proof_board_kernel(tc, tab_words, tab_scales, offs, w1_words, w1_s
         for n in reversed(range(2)):
             quantize_w2(n)
         pad_last_rows()
-        for g in range(2):
-            quantize_z(0, g)
-        for g in range(CHUNKS):
-            quantize_z(1, g)
+        for a, g in ((0, 0), (0, 1), (1, 0), (1, 1), (1, 2), (0, 2), (0, 3)):
+            quantize_z(a, g)
         for g in range(CHUNKS):
             cols = slice(P * g, P * (g + 1))
             for u in range(2):
@@ -407,20 +407,23 @@ def tile_list_proof_board_kernel(tc, tab_words, tab_scales, offs, w1_words, w1_s
             nc.scalar.copy(last_grouped[g][:].bitcast(F32), late_banks[g][:, 0:2, :].rearrange("p u t -> p t u"))
             nc.vector.quantize_mx(out=last_codes[:, cols].bitcast(FP8X4), scales=last_planes[:, cols],
                                   in_=last_grouped[g][:].rearrange("p t j -> p (t j)"))
-        for g in range(2, CHUNKS):
-            quantize_z(0, g)
+        end = CHUNKS - 1
+        for b in range(2):
+            group_half(1, end, b, sum_banks[2 + b], nc.scalar.copy)
+        quantize_z(1, end)
+        first_banks = sum_banks[:2] + back_banks
         for g in range(CHUNKS):
-            if g < 2:
-                second_pass(0, g, 0, sum_banks[g], True, False)
-            second_pass(0, g, 1, sum_banks[g], g >= 2, False)
+            second_pass(0, g, 0, first_banks[g], True, False)
+            if g < end:
+                second_pass(0, g, 1, first_banks[g], False, False)
         for g in range(CHUNKS):
             block = slice(P * g, P * (g + 1))
             nc.tensor.matmul_mx(
-                out=whole(sum_banks[g]), lhsT=padded_codes[:, block].bitcast(FP8X4), lhsT_scale=padded_planes[:, block],
-                rhs=last_codes[:].bitcast(FP8X4), rhs_scale=last_planes[:], start=False, stop=(g < 2))
-            if g >= 2:
-                second_pass(0, g, 0, sum_banks[g], False, True)
-            empty_bank(0, g, sum_banks[g], nc.vector.tensor_copy if g == 2 else nc.scalar.copy)
+                out=whole(first_banks[g]), lhsT=padded_codes[:, block].bitcast(FP8X4), lhsT_scale=padded_planes[:, block],
+                rhs=last_codes[:].bitcast(FP8X4), rhs_scale=last_planes[:], start=False, stop=(g < end))
+            if g == end:
+                second_pass(0, g, 1, first_banks[g], False, True)
+            empty_bank(0, g, first_banks[g], nc.vector.tensor_copy if g == 2 else nc.scalar.copy)
         for n in range(2, len(w2_parts) - 1):
             quantize_w2(n)
         for g in range(CHUNKS):
@@ -435,12 +438,14 @@ def tile_list_proof_board_kernel(tc, tab_words, tab_scales, offs, w1_words, w1_s
             nc.vector.tensor_tensor(released[j % 2][:].indirect(idx4[:]), pulled[j][:], wgo_sb[:], MULT)
             nc.sync.dma_start(out[P * j:P * (j + 1), :], released[j % 2][:])
 
+        later_banks = mx_banks + sum_banks[2:]
+
         def output_tile(j):
             for a in range(PASSES):
                 for g in range(CHUNKS):
-                    second_pass(j, g, a, late_banks[g], a == 0, a == PASSES - 1)
+                    second_pass(j, g, a, later_banks[g], a == 0, a == PASSES - 1)
                     if a == PASSES - 1:
-                        empty_bank(j, g, late_banks[g])
+                        empty_bank(j, g, later_banks[g])
 
         pull(0)
         quantize_w2(len(w2_parts) - 1)

@@ -411,7 +411,7 @@ def tile_list_proof_board_kernel(tc, tab_words, tab_scales, offs, w1_words, w1_s
         for b in range(2):
             group_half(1, end, b, sum_banks[2 + b], nc.scalar.copy)
         quantize_z(1, end)
-        first_banks = sum_banks[:2] + back_banks
+        first_banks = late_banks
         for g in range(CHUNKS):
             second_pass(0, g, 0, first_banks[g], True, False)
             if g < end:
@@ -438,7 +438,7 @@ def tile_list_proof_board_kernel(tc, tab_words, tab_scales, offs, w1_words, w1_s
             nc.vector.tensor_tensor(released[j % 2][:].indirect(idx4[:]), pulled[j][:], wgo_sb[:], MULT)
             nc.sync.dma_start(out[P * j:P * (j + 1), :], released[j % 2][:])
 
-        later_banks = mx_banks + sum_banks[2:]
+        later_banks = sum_banks
 
         def output_tile(j):
             for a in range(PASSES):

@@ -82,7 +82,7 @@ def tile_list_proof_board_kernel(tc, tab_words, tab_scales, offs, w1_words, w1_s
         first_pieces = ((0, FIRST), (FIRST, BANK - FIRST), (BANK, BANK))
         first_factors = [placed("first_factor%d" % c0, [P, width], F32, at)
                          for (c0, width), at in zip(first_pieces, (window_at + 23.5, 7.5, w2_at[0] + 7.5))]
-        factors = [None] + [placed("factor%d" % i, [P, S], F32, window_at + 24 if i == 1 else h_at[(i - 2) % 4] + 4)
+        factors = [None] + [placed("factor%d" % i, [P, S], F32, {1: window_at + 24, LAST: turned_at + 36}.get(i, h_at[(i - 2) % 4] + 4))
                             for i in range(1, ROW_TILES)]
         first_h = [placed("first_h%d" % c0, [P, width], F32, at) for (c0, width), at in zip(first_pieces, (9, 21.0625, 22.0625))]
         h_sb = [None] + [placed("h%d" % i, [P, S], F32, w2_at[1] + 6 if i == 1 else h_at[(i - 2) % 4]) for i in range(1, ROW_TILES)]
@@ -114,7 +114,7 @@ def tile_list_proof_board_kernel(tc, tab_words, tab_scales, offs, w1_words, w1_s
         padded_codes = placed("padded_codes", [P, BANK], U32, 9)
         padded_planes = placed("padded_planes", [P, BANK], U8, 8.4375)
         w2_grouped = [placed("w2_grouped%d" % part, [P, HALF, 4], BF16, at)
-                      for part, at in enumerate((window_at + 18.75, turned_at + 12, window_at + 21.25, turned_at + 14))]
+                      for part, at in enumerate((window_at + 18.75, slot_at[2] + 1, window_at + 21.25, slot_at[3]))]
         late_codes_at = turned_at + 24
         style_at = (turned_at + 32, w2_at[0], w2_at[0] + 4, w2_at[1] + 4)
         w2_cuts = ((0, 0, P, h_at[1] + 2), (1, 0, P, h_at[1] + 2.5), (0, P, P, late_codes_at), (0, HALF, HALF, late_codes_at + 0.5),
@@ -355,8 +355,10 @@ def tile_list_proof_board_kernel(tc, tab_words, tab_scales, offs, w1_words, w1_s
                     group_half(0, g, b, back_banks[b], nc.scalar.copy)
             if turns_back:
                 turn_back(0, g + 1, back_banks, (nc.scalar.copy, nc.scalar.copy))
-            if i + 3 < ROW_TILES:
+            if i + 3 < LAST:
                 make_factors(i + 3)
+            if i + 2 == LAST:
+                make_factors(LAST)
             if i + 3 == LAST:
                 nc.gpsimd.memset(released[0][:].bitcast(I32), 0)
             for part in range(4):
@@ -369,7 +371,7 @@ def tile_list_proof_board_kernel(tc, tab_words, tab_scales, offs, w1_words, w1_s
         y_sb = [placed("y%d" % j, [P, T2], F32, at) for j, at in enumerate((spare_at, factor_at + 16, slot_at[0], turned_at))]
         style_sb = [placed("style%d" % j, [P, M], F32, at)
                     for j, at in enumerate(style_at)]
-        wgo_sb = placed("wgo_sb", [P, M], F32, turned_at + 36)
+        wgo_sb = placed("wgo_sb", [P, M], F32, slot_at[2] + 4)
         pulled = [placed("pulled%d" % s, [P, M], F32, at)
                   for s, at in enumerate((spare_at + 21, late_codes_at + 2.25, spare_at + 17, spare_at + 21))]
         for j in range(OUT_TILES):

from contextlib import ExitStack

import concourse.mybir as mybir
from concourse.masks import make_identity

K, H, N, T, S, T2, M = 1024, 1024, 512, 4096, 1024, 2048, 1024
FLOPS = 2 * K * H * S + 2 * H * N * T2

F32 = mybir.dt.float32
BF16 = mybir.dt.bfloat16
I32 = mybir.dt.int32
U32 = mybir.dt.uint32
U16 = mybir.dt.uint16
U8 = mybir.dt.uint8
FP8X4 = mybir.dt.float8_e4m3fn_x4
FP4X4 = mybir.dt.float4_e2m1fn_x4
MULT = mybir.AluOpType.mult
SUBTRACT = mybir.AluOpType.subtract
TANH = mybir.ActivationFunctionType.Tanh
COPY = mybir.ActivationFunctionType.Copy

P = 128
BANK = 512
PASSES = 2
ROW_TILES = H // P
LAST = ROW_TILES - 1
TILES_PER_PASS = ROW_TILES // PASSES
CHUNKS = T2 // BANK
BLOCKS = BANK // P
OUT_TILES = N // P
PAGES = 3
FIRST = 256
HALF = BANK // 2
W2_TILES = (1, 5, 2, 5)
SCALE_ROW = 96
KB = 1024


def tile_list_proof_board_kernel(tc, tab_words, tab_scales, offs, w1_words, w1_scales, b1, gain, offs2, wgs,
                                           board, w2, offs3, style, offs4, wgo, out):
    nc = tc.nc
    with ExitStack() as ctx:
        lists = ctx.enter_context(tc.tile_pool(name="lists", bufs=1))
        keep = ctx.enter_context(tc.tile_pool(name="keep", bufs=1))
        shared = ctx.enter_context(tc.tile_pool(name="shared", bufs=1))
        psum = ctx.enter_context(tc.psum_pool(name="psum", bufs=1))

        def kept(name, shape, dtype):
            return keep.tile(shape, dtype, name=name, align_bytes=64)

        def placed(name, shape, dtype, kb):
            return shared.tile(shape, dtype, name=name, align_bytes=64, offset=int(kb * KB))

        idx = lists.tile([P, S // 16], U16, name="idx")
        idx2 = lists.tile([P, S // 16], U16, name="idx2")
        idx3 = lists.tile([P, M // 16], U16, name="idx3")
        idx4 = lists.tile([P, M // 16], U16, name="idx4")

        sum_banks = [psum.tile([P, BLOCKS, P], F32, name="sum_bank%d" % g) for g in range(CHUNKS)]
        back_banks = [psum.tile([P, BLOCKS, P], F32, name="back_bank%d" % b) for b in range(2)]
        mx_banks = [psum.tile([P, BLOCKS, P], F32, name="mx_bank%d" % b) for b in range(2)]

        def whole(bank):
            return bank[:].rearrange("p c t -> p (c t)")

        slot_at = (25, 37, 56, 73)
        h_at = (23, 35, 56, 73)
        w2_at = (47, 64)
        turned_at = 81
        factor_at = 121
        window_at = 145
        codes_at = 177
        table = [placed("table0", [P, T], U32, window_at + 8), placed("table1", [P, T], U32, 24.25)]
        table_scales = placed("table_scales", [P, T], U8, 20.5)
        wgs_first = kept("wgs_first", [P, FIRST], F32)
        wgs_next = placed("wgs_next", [P, S - FIRST], F32, 21.0625)
        wgs_sb = placed("wgs_sb", [P, S], F32, window_at + 9)
        w1_parts = [(first, placed("w1_part%d" % first, [P, PASSES, 2 * P * tiles], U8, at))
                    for first, tiles, at in ((0, 1, 20.5625), (1, 3, window_at + 15), (4, 1, window_at + 18.5),
                                             (5, 1, window_at + 21), (6, 2, window_at + 17.5))]
        picked = [placed("picked%d" % a, [P, S], U32, turned_at + 32 + 4 * a) for a in range(PASSES)]
        first_pieces = ((0, FIRST), (FIRST, BANK - FIRST), (BANK, BANK))
        first_factors = [placed("first_factor%d" % c0, [P, width], F32, at)
                         for (c0, width), at in zip(first_pieces, (window_at + 23.5, 7.5, w2_at[0] + 7.5))]
        factors = [None] + [placed("factor%d" % i, [P, S], F32, {1: window_at + 24, LAST: turned_at + 36}.get(i, h_at[(i - 2) % 4] + 4))
                            for i in range(1, ROW_TILES)]
        first_h = [placed("first_h%d" % c0, [P, width], F32, at) for (c0, width), at in zip(first_pieces, (9, 21.0625, 22.0625))]
        h_sb = [None] + [placed("h%d" % i, [P, S], F32, w2_at[1] + 6 if i == 1 else h_at[(i - 2) % 4]) for i in range(1, ROW_TILES)]
        board_sb = [placed("board%d" % i, [P, T2], F32, slot_at[i % 4]) for i in range(ROW_TILES)]
        page_identity = [placed("page_identity%d" % i, [P, P], F32, turned_at + 24 if i == LAST else slot_at[i % 4])
                         for i in range(ROW_TILES)]
        w2_raw = [placed("w2_raw%d" % a, [P, 4, N], F32, w2_at[a]) for a in range(PASSES)]
        turned = [[placed("turned%d_%d" % (a, g), [P, 2, BLOCKS, 2 * P], BF16, turned_at + 16 * a + 4 * g) for g in range(CHUNKS)]
                  for a in range(PASSES)]
        z_grouped = [[placed("z_grouped%d_%d" % (a, g), [P, BANK, 4], BF16, (slot_at[0] + 6, factor_at, slot_at[1] + 6, factor_at + 4)[g] if a == 0 else
                             (factor_at + 8, factor_at + 12, factor_at + 16, turned_at + 24)[g])
                      for g in range(CHUNKS)] for a in range(PASSES)]

        zeros = kept("zeros", [P, P], F32)
        identity = kept("identity", [P, P], F32)
        vector_cols = kept("vector_cols", [P, 2 * ROW_TILES], F32)
        vector_rows = kept("vector_rows", [P, P], F32)
        picked_rows = kept("picked_rows", [P, S], U8)
        picked_scales = kept("picked_scales", [P, PASSES, S], U8)
        w1_planes = [kept("w1_planes0", [P, PASSES, P], U8), placed("w1_planes1", [P, PASSES, H - P], U8, window_at + 13)]
        codes_a = [placed("codes_a%d" % g, [P, BANK], U32, codes_at + 2 * g) for g in range(CHUNKS)]
        codes_b = placed("codes_b", [P, T2], U32, codes_at + 8)
        planes_b = kept("planes_b", [P, T2], U8)
        spare_at = codes_at + 16
        last_turned = [placed("last_turned%d" % g, [P, 2, 2 * P], BF16, spare_at + 8 + g) for g in range(CHUNKS)]
        last_grouped = [placed("last_grouped%d" % g, [P, P, 4], BF16, spare_at + 12 + g) for g in range(CHUNKS)]
        last_codes = placed("last_codes", [P, BANK], U32, factor_at + 20)
        last_planes = kept("last_planes", [P, BANK], U8)
        padded_codes = placed("padded_codes", [P, BANK], U32, 9)
        padded_planes = placed("padded_planes", [P, BANK], U8, 8.4375)
        w2_grouped = [placed("w2_grouped%d" % part, [P, HALF, 4], BF16, at)
                      for part, at in enumerate((window_at + 18.75, slot_at[2] + 1, window_at + 21.25, slot_at[3]))]
        late_codes_at = turned_at + 24
        style_at = (turned_at + 32, w2_at[0], w2_at[0] + 4, w2_at[1] + 4)
        w2_cuts = ((0, 0, P, h_at[1] + 2), (1, 0, P, h_at[1] + 2.5), (0, P, P, late_codes_at), (0, HALF, HALF, late_codes_at + 0.5),
                   (1, P, P, late_codes_at + 1.5), (1, HALF, P, late_codes_at + 2), (1, 3 * P, P, style_at[0]))
        w2_parts = [(a, c0, width, placed("w2_codes%d" % n, [P, width], U32, at), kept("w2_plane%d" % n, [P, width], U8))
                    for n, (a, c0, width, at) in enumerate(w2_cuts)]
        pages = [placed("page0", [P, T2], F32, 12.5625), placed("page1", [P, T2], F32, window_at + 0.5),
                 placed("page2", [P, T2], F32, 0)]
        released = [placed("released0", [P, T2], F32, window_at + 9), placed("released1", [P, T2], F32, window_at + 24)]

        nc.vector.memset(vector_rows[0:64, :], 0.0)
        nc.vector.memset(w1_planes[0][:].rearrange("p a c -> p (a c)").bitcast(I32), 0)
        nc.vector.memset(zeros[:], 0.0)
        nc.vector.memset(table_scales[0:SCALE_ROW, :].bitcast(I32), 0)
        nc.vector.memset(picked_scales[:].rearrange("p a c -> p (a c)").bitcast(I32), 0)
        make_identity(nc, identity[:])

        def load_table(a):
            nc.sync.dma_start(table[a][:].bitcast(I32), tab_words[a].rearrange("p t i -> p (t i)").bitcast(I32))

        w1_by_partition = w1_words.rearrange("a p c -> p a c")
        nc.sync.dma_start(table_scales[SCALE_ROW:P, :].bitcast(I32), tab_scales.rearrange("a q t -> q a t").bitcast(I32))
        nc.sync.dma_start(idx[:], offs)
        nc.sync.dma_start(idx2[:], offs2)
        nc.sync.dma_start(idx3[:], offs3)
        nc.sync.dma_start(idx4[:], offs4)

        def load_w1(first, part):
            nc.sync.dma_start(part[:].bitcast(I32), w1_by_partition[:, :, 2 * P * first:2 * P * first + part.shape[2]].bitcast(I32))

        def load_w1_scales(planes, c0, c1):
            for q in range(4):
                nc.sync.dma_start(planes[32 * q:32 * q + 4, :, :].bitcast(I32),
                                  w1_scales[:, 4 * q:4 * q + 4, c0:c1].rearrange("a r c -> r a c").bitcast(I32))

        nc.sync.dma_start(wgs_first[:], wgs[:, 0:FIRST])
        load_table(0)
        nc.sync.dma_start(vector_rows[0:ROW_TILES, :], b1.rearrange("(i p) -> i p", p=P))
        nc.sync.dma_start(vector_rows[ROW_TILES:2 * ROW_TILES, :], gain.rearrange("(i p) -> i p", p=P))
        nc.scalar.activation(vector_rows[64:P, :], zeros[64:P, :], TANH)
        load_w1_scales(w1_planes[0], 0, P)
        nc.tensor.transpose(back_banks[0][:, 0, :], vector_rows[:], identity[:])
        for g in range(CHUNKS):
            for u in range(2):
                nc.scalar.copy(turned[1][g][:].bitcast(F32)[:, u, :, 96:P], zeros[:].rearrange("p (c w) -> p c w", c=BLOCKS))

        nc.vector.tensor_copy(picked_rows[:], table_scales[:].indirect(idx[:]))

        def move_scales(q):
            first = SCALE_ROW + 8 * q
            nc.sync.dma_start(picked_scales[32 * q:32 * q + 4, :, :].bitcast(I32),
                              picked_rows[first:first + 8, :].bitcast(I32))

        load_table(1)
        load_w1(*w1_parts[0])
        for q in range(4):
            move_scales(q)
        nc.sync.dma_start(wgs_next[:], wgs[:, FIRST:S])
        nc.scalar.copy(vector_cols[:], back_banks[0][:, 0, 0:2 * ROW_TILES])
        nc.vector.tensor_copy(picked[0][:], table[0][:].indirect(idx[:]))
        for c0, c1 in ((0, FIRST), (FIRST, S)):
            nc.vector.tensor_copy(picked[1][:, c0:c1], table[1][:].indirect(idx[:, c0 // 16:c1 // 16]))
        for window in pages[0:2]:
            nc.vector.memset(window[:].bitcast(I32), 0)
        nc.vector.memset(w1_planes[1][:].rearrange("p a c -> p (a c)").bitcast(I32), 0)
        load_w1_scales(w1_planes[1], P, H)
        load_w1(*w1_parts[1])
        nc.sync.dma_start(wgs_sb[:], wgs)
        for first, part in w1_parts[2:]:
            load_w1(first, part)

        def load_board(i):
            nc.sync.dma_start(board_sb[i][:], board[P * i:P * (i + 1), :])

        def load_w2(a):
            nc.sync.dma_start(w2_raw[a][:], w2[512 * a:512 * (a + 1), :].rearrange("(p j) n -> p j n", j=4))

        def make_factor(i, factor, weights):
            nc.scalar.activation(factor, weights, COPY,
                                 scale=vector_cols[:, ROW_TILES + i:ROW_TILES + i + 1])

        def make_factors(i):
            make_factor(i, factors[i][:], wgs_sb[:])

        def first_product(i, bank, c0, width, group):
            for g0 in range(0, width, group):
                cols = slice(c0 + g0, c0 + g0 + group)
                first, codes = [entry for entry in w1_parts if entry[0] <= i][-1]
                tile_at = i - first
                for a in range(PASSES):
                    nc.tensor.matmul_mx(
                        out=whole(bank)[:, g0:g0 + group],
                        lhsT=codes[:, a, 2 * P * tile_at:2 * P * (tile_at + 1)].bitcast(FP4X4),
                        lhsT_scale=w1_planes[0][:, a, :] if i == 0 else w1_planes[1][:, a, P * (i - 1):P * i],
                        rhs=picked[a][:, cols].bitcast(FP8X4),
                        rhs_scale=picked_scales[:, a, cols],
                        start=(a == 0), stop=(a == PASSES - 1))

        def apply_tanh(i, bank, h, width):
            nc.scalar.activation(h, whole(bank)[:, 0:width], TANH, bias=vector_cols[:, i:i + 1])

        def multiply(i):
            for half in range(2):
                first_product(i, mx_banks[half], BANK * half, BANK, BANK)

        def score(i):
            for half in range(2):
                apply_tanh(i, mx_banks[half], h_sb[i][:, BANK * half:BANK * (half + 1)], BANK)

        def place_scores(i, c0, width, h, factor):
            nc.vector.tensor_tensor(pages[i % PAGES][:].indirect(idx2[:, c0 // 16:(c0 + width) // 16]),
                                    h, factor, MULT)

        late_banks = back_banks + mx_banks

        def banks_of(i):
            return late_banks if i == LAST else sum_banks

        def block_start(i, g, c):
            return BANK * c + P * g if i == LAST else BANK * g + P * c

        def turn_board(i):
            for g in range(CHUNKS):
                for c in range(BLOCKS):
                    t0 = block_start(i, g, c)
                    nc.tensor.matmul(banks_of(i)[g][:, c, :], board_sb[i][:, t0:t0 + P], identity[:],
                                     start=(c == 0), stop=False, is_transpose=True)

        def turn_page(i):
            a, place = divmod(i, TILES_PER_PASS)
            for g in range(CHUNKS):
                for c in range(BLOCKS):
                    t0 = block_start(i, g, c)
                    nc.tensor.matmul(banks_of(i)[g][:, c, :], pages[i % PAGES][:, t0:t0 + P], page_identity[i][:],
                                     start=False, stop=(c == BLOCKS - 1), is_transpose=True)
                rounded = last_turned[g][:].rearrange("t u (c w) -> t u c w", c=BLOCKS) if i == LAST else \
                    turned[a][g][:, :, :, 64 * place:64 * (place + 1)]
                nc.scalar.copy(
                    rounded.rearrange("t u c (w e) -> t u c w e", e=2),
                    banks_of(i)[g][:].rearrange("t c (w u e) -> t u c w e", u=2, e=2))

        def release_page(i):
            nc.scalar.copy(page_identity[i][:], identity[:])

        def turn_back_half(a, g, b, bank):
            words = turned[a][g][:].bitcast(F32)
            for u in range(2):
                for c in range(2):
                    nc.tensor.transpose(bank[:, 2 * u + c, :], words[:, u, 2 * b + c, :], identity[:])

        def group_half(a, g, b, bank, copy):
            grouped_words = z_grouped[a][g][:].bitcast(F32)
            copy(grouped_words[:, 2 * P * b:2 * P * (b + 1), :], bank[:].rearrange("p (u c) t -> p (c t) u", u=2))

        def turn_back(a, g, banks, copies):
            for b in range(2):
                turn_back_half(a, g, b, banks[b])
                group_half(a, g, b, banks[b], copies[b])

        def group_w2(part):
            raw, first = w2_raw[part // 2], HALF * (part % 2)
            for c0 in range(0, HALF, P):
                nc.scalar.copy(w2_grouped[part][:, c0:c0 + P, :].rearrange("p (c k) j -> p c j k", k=4),
                               raw[:, :, first + c0:first + c0 + P].rearrange("p j (c k) -> p c j k", k=4))

        def quantize_w2(n):
            a, c0, width, codes, plane = w2_parts[n]
            part, at = divmod(c0, HALF)
            nc.vector.quantize_mx(out=codes[:].bitcast(FP8X4), scales=plane[:],
                                  in_=w2_grouped[2 * a + part][:, at:at + width, :].rearrange("p n j -> p (n j)"))

        def pad_last_rows():
            codes, plane = w2_parts[1][3:]
            for c in range(BLOCKS):
                nc.sync.dma_start(padded_codes[32 * c:32 * (c + 1), P * c:P * (c + 1)].bitcast(I32), codes[96:P, :].bitcast(I32))
                nc.sync.dma_start(padded_planes[32 * c:32 * c + 4, P * c:P * (c + 1)].bitcast(I32), plane[96:100, :].bitcast(I32))

        for i in range(2):
            load_board(i)
        make_factor(0, first_factors[0][:], wgs_first[:])
        for (c0, width), factor in zip(first_pieces[1:], first_factors[1:]):
            make_factor(0, factor[:], wgs_next[:, c0 - FIRST:c0 - FIRST + width])
        for (c0, width), h, factor, bank, group in zip(first_pieces, first_h, first_factors,
                                                       (mx_banks[0], back_banks[1], mx_banks[1]), (FIRST, FIRST, BANK)):
            first_product(0, bank, c0, width, group)
            apply_tanh(0, bank, h[:], width)
            place_scores(0, c0, width, h[:], factor[:])
        for cleared in (pages[2], padded_codes, padded_planes):
            nc.gpsimd.memset(cleared[:].bitcast(I32), 0)
        multiply(1)
        score(1)
        make_factors(1)
        multiply(2)

        turn_board(0)
        release_page(0)
        make_factors(2)

        for i in range(ROW_TILES):
            g = 2 * (i - 3)
            turns_back = i in (3, 4)
            if i > 0:
                place_scores(i, 0, S, h_sb[i][:], factors[i][:])
            if i + 2 < ROW_TILES:
                load_board(i + 2)
            if i == 1:
                nc.gpsimd.memset(released[1][:].bitcast(I32), 0)
            if i < PASSES:
                load_w2(i)
            turn_page(i)
            if turns_back:
                for b in range(2):
                    turn_back_half(0, g, b, back_banks[b])
            if i == LAST - 1:
                pairs = (sum_banks[:2], sum_banks[2:])
                on_scalar = (nc.scalar.copy, nc.scalar.copy)
                for chunk in range(2):
                    turn_back(1, chunk, pairs[chunk], on_scalar)
                for b in range(2):
                    turn_back_half(1, 2, b, pairs[0][b])
                release_page(LAST)
                for b in range(2):
                    group_half(1, 2, b, pairs[0][b], nc.scalar.copy)
                for b in range(2):
                    turn_back_half(1, 3, b, pairs[1][b])
            if i < LAST - 1:
                turn_board(i + 1)
            if i + 2 < ROW_TILES:
                score(i + 2)
            if i == LAST - 2:
                turn_board(LAST)
            if i < LAST - 1:
                release_page(i + 1)
            if i + 3 < ROW_TILES:
                multiply(i + 3)
            if turns_back:
                for b in range(2):
                    group_half(0, g, b, back_banks[b], nc.scalar.copy)
            if turns_back:
                turn_back(0, g + 1, back_banks, (nc.scalar.copy, nc.scalar.copy))
            if i + 3 < LAST:
                make_factors(i + 3)
            if i + 2 == LAST:
                make_factors(LAST)
            if i + 3 == LAST:
                nc.gpsimd.memset(released[0][:].bitcast(I32), 0)
            for part in range(4):
                if W2_TILES[part] == i:
                    group_w2(part)

        last_h_at = h_at[(LAST - 2) % 4]
        planes_a = [placed("planes_a%d" % g, [P, BANK], U8, at)
                    for g, at in enumerate((last_h_at, last_h_at + 0.5, last_h_at + 1, last_h_at + 1.5))]
        y_sb = [placed("y%d" % j, [P, T2], F32, at) for j, at in enumerate((spare_at, factor_at + 16, slot_at[0], turned_at))]
        style_sb = [placed("style%d" % j, [P, M], F32, at)
                    for j, at in enumerate(style_at)]
        wgo_sb = placed("wgo_sb", [P, M], F32, slot_at[2] + 4)
        pulled = [placed("pulled%d" % s, [P, M], F32, at)
                  for s, at in enumerate((spare_at + 21, late_codes_at + 2.25, spare_at + 17, spare_at + 21))]
        for j in range(OUT_TILES):
            nc.sync.dma_start(style_sb[j][:], style[P * j:P * (j + 1), :])
        nc.sync.dma_start(wgo_sb[:], wgo)

        def quantize_z(a, g):
            chunk = slice(BANK * g, BANK * (g + 1))
            nc.vector.quantize_mx(out=(codes_a[g][:] if a == 0 else codes_b[:, chunk]).bitcast(FP8X4),
                                  scales=planes_a[g][:] if a == 0 else planes_b[:, chunk],
                                  in_=z_grouped[a][g][:].rearrange("p t j -> p (t j)"))

        def second_pass(j, g, a, bank, start, stop):
            c0, codes, plane = [(part[1], part[3], part[4]) for part in w2_parts if part[0] == a and part[1] <= P * j][-1]
            cols = slice(P * j - c0, P * (j + 1) - c0)
            chunk = slice(BANK * g, BANK * (g + 1))
            nc.tensor.matmul_mx(
                out=whole(bank), lhsT=codes[:, cols].bitcast(FP8X4), lhsT_scale=plane[:, cols],
                rhs=(codes_a[g][:] if a == 0 else codes_b[:, chunk]).bitcast(FP8X4),
                rhs_scale=planes_a[g][:] if a == 0 else planes_b[:, chunk],
                start=start, stop=stop)

        def empty_bank(j, g, bank, copy=nc.scalar.copy):
            copy(y_sb[j][:, BANK * g:BANK * (g + 1)], whole(bank))

        for n in reversed(range(2)):
            quantize_w2(n)
        pad_last_rows()
        for a, g in ((0, 0), (0, 1), (1, 0), (1, 1), (1, 2), (0, 2), (0, 3)):
            quantize_z(a, g)
        for g in range(CHUNKS):
            cols = slice(P * g, P * (g + 1))
            for u in range(2):
                nc.tensor.transpose(late_banks[g][:, u, :], last_turned[g][:].bitcast(F32)[:, u, :], identity[:])
            nc.scalar.copy(last_grouped[g][:].bitcast(F32), late_banks[g][:, 0:2, :].rearrange("p u t -> p t u"))
            nc.vector.quantize_mx(out=last_codes[:, cols].bitcast(FP8X4), scales=last_planes[:, cols],
                                  in_=last_grouped[g][:].rearrange("p t j -> p (t j)"))
        end = CHUNKS - 1
        for b in range(2):
            group_half(1, end, b, sum_banks[2 + b], nc.scalar.copy)
        quantize_z(1, end)
        first_banks = late_banks
        for g in range(CHUNKS):
            second_pass(0, g, 0, first_banks[g], True, False)
            if g < end:
                second_pass(0, g, 1, first_banks[g], False, False)
        for g in range(CHUNKS):
            block = slice(P * g, P * (g + 1))
            nc.tensor.matmul_mx(
                out=whole(first_banks[g]), lhsT=padded_codes[:, block].bitcast(FP8X4), lhsT_scale=padded_planes[:, block],
                rhs=last_codes[:].bitcast(FP8X4), rhs_scale=last_planes[:], start=False, stop=(g < end))
            if g == end:
                second_pass(0, g, 1, first_banks[g], False, True)
            empty_bank(0, g, first_banks[g], nc.vector.tensor_copy if g == 2 else nc.scalar.copy)
        for n in range(2, len(w2_parts) - 1):
            quantize_w2(n)
        for g in range(CHUNKS):
            chunk = slice(BANK * g, BANK * (g + 1))
            nc.sync.dma_start(codes_b[96:P, chunk].bitcast(I32), last_codes[32 * g:32 * (g + 1), :].bitcast(I32))
            nc.sync.dma_start(planes_b[96:100, chunk].bitcast(I32), last_planes[32 * g:32 * g + 4, :].bitcast(I32))

        def pull(j):
            nc.vector.tensor_tensor(pulled[j][:], y_sb[j][:].indirect(idx3[:]), style_sb[j][:], SUBTRACT)

        def release(j):
            nc.vector.tensor_tensor(released[j % 2][:].indirect(idx4[:]), pulled[j][:], wgo_sb[:], MULT)
            nc.sync.dma_start(out[P * j:P * (j + 1), :], released[j % 2][:])

        later_banks = sum_banks

        def output_tile(j):
            for a in range(PASSES):
                for g in range(CHUNKS):
                    second_pass(j, g, a, later_banks[g], a == 0, a == PASSES - 1)
                    if a == PASSES - 1:
                        empty_bank(j, g, later_banks[g])

        pull(0)
        quantize_w2(len(w2_parts) - 1)
        release(0)
        for j in range(1, OUT_TILES):
            output_tile(j)
        for j in range(1, OUT_TILES):
            pull(j)
        for j in range(1, OUT_TILES):
            release(j)
